import numpy as np
import ml_dtypes


def mxq(x, axis, fmt="e4m3"):
    dtype, down = {"e4m3": (ml_dtypes.float8_e4m3fn, 7), "e5m2": (ml_dtypes.float8_e5m2, 14)}[fmt]
    v = np.moveaxis(np.asarray(x, np.float32).astype(ml_dtypes.bfloat16).astype(np.float64), axis, -1)
    blocks = v.reshape(v.shape[:-1] + (-1, 32))
    amax = np.abs(blocks).max(-1, keepdims=True)
    byte = np.maximum(np.where(amax > 0, np.frexp(amax)[1] - 1 + 127, 0) - down, 1)
    scale = np.exp2(byte - 127.0)
    codes = (blocks / scale).astype(np.float32).astype(dtype).astype(np.float64)
    return np.moveaxis((codes * scale).reshape(v.shape), -1, axis)


WIDE = False


def mx_kscale(k):
    if not WIDE:
        return np.ones(k)
    levels = np.array([30, -30])
    if k % 512:
        return np.exp2(np.random.permutation(np.resize(levels, k // 32))).repeat(32)
    a = np.empty((k // 512, 16))
    for p in range(k // 512):
        a[p, :8] = np.random.permutation(np.resize(levels, 8))
        for g in range(8):
            far = levels[np.abs(levels - a[p, g]) >= 10]
            a[p, g + 8] = far[np.random.randint(len(far))]
    return np.exp2(a.ravel()).repeat(32)


def f64(x):
    return np.asarray(x).astype(np.float64)


def striped(idx):
    return np.tile(idx.reshape(-1, 16).T, (8, 1)).astype(np.uint16)


def unstriped(offs):
    return offs[:16].T.reshape(-1).astype(np.int64)


def bf(x):
    return np.asarray(x, np.float32).astype(ml_dtypes.bfloat16)


E2M1 = np.array([0.0, 0.5, 1.0, 1.5, 2.0, 3.0, 4.0, 6.0, -0.0, -0.5, -1.0, -1.5, -2.0, -3.0, -4.0, -6.0])


def pack_weight(w, fmt):
    k, n = w.shape
    w = f64(bf(w)).reshape(k // 32, 32, n)
    amax = np.abs(w).max(1)
    if fmt in ("e4m3", "e5m2"):
        byte = np.frexp(amax)[1] - 1 + 127 - (7 if fmt == "e4m3" else 14)
    else:
        mant, ex = np.frexp(amax / 6.0)
        byte = np.where(mant > 0.5, ex, ex - 1) + 127
    byte = np.clip(np.where(amax > 0, byte, 1), 1, 254)
    scaled = (w * np.exp2(127.0 - byte)[:, None, :]).reshape(k, n).astype(np.float32)
    by_word = np.ascontiguousarray(scaled.reshape(k // 512, 128, 4, n).transpose(0, 1, 3, 2))
    if fmt in ("e4m3", "e5m2"):
        words = by_word.astype(ml_dtypes.float8_e4m3fn if fmt == "e4m3" else ml_dtypes.float8_e5m2).view(np.uint8)
    else:
        c = by_word.astype(ml_dtypes.float4_e2m1fn).view(np.uint8) & 0xF
        words = c[..., 0::2] | (c[..., 1::2] << 4)
    return np.ascontiguousarray(words), np.ascontiguousarray(byte.astype(np.uint8).reshape(k // 512, 16, n))


def unpack_weight(words, scales, fmt):
    g, p, n, _ = words.shape
    if fmt in ("e4m3", "e5m2"):
        vals = np.ascontiguousarray(words).view(ml_dtypes.float8_e4m3fn if fmt == "e4m3" else ml_dtypes.float8_e5m2).astype(np.float64)
    else:
        nib = np.empty((g, p, n, 4), np.uint8)
        nib[..., 0::2] = words & 0xF
        nib[..., 1::2] = words >> 4
        vals = E2M1[nib]
    vals = vals * np.repeat(np.exp2(scales.astype(np.float64) - 127.0), 8, axis=1)[..., None]
    return vals.transpose(0, 1, 3, 2).reshape(g * 512, n)


K, H, N, T, S, T2 = 1024, 1536, 512, 2048, 1024, 2048

def setup_inputs():
    n = np.random.standard_normal
    s = mx_kscale(K)[:, None]
    u = mx_kscale(H)[:, None]
    tab = n((K, T)) * np.exp(1.0 * n((1, T))) * s
    tab_words, tab_scales = pack_weight(tab, "e5m2")
    w1 = (n((K, H)) / np.sqrt(K) / s * u.T).astype(np.float32)
    lo = (-(0.5 + np.random.uniform(0.0, 1.0, H)) * u[:, 0]).astype(np.float32)
    hi = ((0.8 + np.random.uniform(0.0, 1.0, H)) * u[:, 0]).astype(np.float32)
    sT = (1.0 / (1.0 + np.exp(-n((H, T))))).astype(np.float32)
    w2_words, w2_scales = pack_weight(4.0 * n((H, N)) / np.sqrt(H) / u, "e4m3")
    wgo = np.exp(0.3 * n((128, S))).astype(np.float32)
    offs = striped(np.random.permutation(T)[:S])
    offs2 = striped(np.random.permutation(T2)[:S])
    return {"tab_words": tab_words, "tab_scales": tab_scales, "w1": w1,
            "lo": lo, "hi": hi, "sT": sT,
            "w2_words": w2_words, "w2_scales": w2_scales, "wgo": wgo,
            "offs": offs, "offs2": offs2}

def reference(tab_words, tab_scales, w1, lo, hi, sT, w2_words, w2_scales, wgo, offs, offs2):
    v = unpack_weight(tab_words, tab_scales, "e5m2")[:, unstriped(offs)]
    h = mxq(f64(w1), 0, "e4m3").T @ v
    c = np.minimum(np.maximum(h, f64(lo)[:, None]), f64(hi)[:, None])
    x = f64(sT)[:, unstriped(offs)]
    d = c * (x * (1.0 - x))
    w2 = unpack_weight(w2_words, w2_scales, "e4m3")
    y = w2.T @ mxq(d, 0, "e4m3")
    out = np.zeros((N, T2))
    out[:, unstriped(offs2)] = np.tile(f64(wgo), (N // 128, 1)) * y
    return out

@@ -1,0 +1,194 @@
+from contextlib import ExitStack
+
+import concourse.mybir as mybir
+
+K, H, N, T, S, T2 = 1024, 1536, 512, 2048, 1024, 2048
+FLOPS = 2 * K * H * S + 2 * H * N * S
+
+F32 = mybir.dt.float32
+BF16 = mybir.dt.bfloat16
+I32 = mybir.dt.int32
+U32 = mybir.dt.uint32
+U16 = mybir.dt.uint16
+U8 = mybir.dt.uint8
+E4M3 = mybir.dt.float8_e4m3fn_x4
+E5M2 = mybir.dt.float8_e5m2_x4
+ALU = mybir.AluOpType
+ACT = mybir.ActivationFunctionType
+
+P = 128
+PACK = 4
+PASS = P * PACK
+HALF = 512
+K_PASSES = K // PASS
+H_PASSES = H // PASS
+HALVES = S // HALF
+LIST_COLS = HALF // 16
+QUAD = 32
+TAB_ROW0 = QUAD - 4 * K_PASSES
+PLANE_ROWS = 3 * QUAD + 4
+
+
+def tile_list_timeout_plan_gradients_kernel(
+    tc, tab_words, tab_scales, w1, lo, hi, sT, w2_words, w2_scales, wgo, offs, offs2, out
+):
+    nc = tc.nc
+    with ExitStack() as ctx:
+        keep = ctx.enter_context(tc.tile_pool(name="keep", bufs=1))
+        ring = ctx.enter_context(tc.tile_pool(name="ring", bufs=2))
+        psum = ctx.enter_context(tc.psum_pool(name="psum", bufs=4))
+
+        idx = keep.tile([P, S // 16], U16, name="idx")
+        nc.sync.dma_start(idx[:], offs)
+
+        tab_sc = keep.tile([P, T], U8, name="tab_sc", align_bytes=64)
+        for q in range(4):
+            nc.vector.memset(tab_sc[QUAD * q : QUAD * q + TAB_ROW0, :].bitcast(I32), 0)
+            nc.sync.dma_start(
+                tab_sc[QUAD * q + TAB_ROW0 : QUAD * (q + 1), :].bitcast(I32),
+                tab_scales[:, 4 * q : 4 * q + 4, :].bitcast(I32),
+            )
+        v_sc = [keep.tile([P, S], U8, name=f"v_sc{k}", align_bytes=64) for k in range(K_PASSES)]
+        for k in range(K_PASSES):
+            nc.vector.memset(v_sc[k][3 * QUAD : P, :].bitcast(I32), 0)
+        picked_sc = keep.tile([P, S], U8, name="picked_sc", align_bytes=64)
+        nc.vector.tensor_copy(picked_sc[:], tab_sc[:].indirect(idx[:]))
+        for k in range(K_PASSES):
+            first = TAB_ROW0 + 4 * k
+            nc.scalar.dma_start(
+                v_sc[k][0:PLANE_ROWS, :].bitcast(I32),
+                picked_sc[first : first + PLANE_ROWS, :].bitcast(I32),
+            )
+
+        v_codes = [keep.tile([P, S], U32, name=f"v_codes{k}", align_bytes=64) for k in range(K_PASSES)]
+
+        def pick_table(k):
+            words = keep.tile([P, T], I32, name=f"tab_words{k}", align_bytes=64)
+            nc.sync.dma_start(words[:], tab_words[k].rearrange("p t i -> p (t i)").bitcast(I32))
+            nc.vector.tensor_copy(v_codes[k][:], words[:].bitcast(U32).indirect(idx[:]))
+
+        def pick_saved(a, t, x4):
+            rows = ring.tile([P, T], F32, name="s_rows", bufs=4)
+            nc.sync.dma_start(
+                rows[:], sT[PASS * a : PASS * (a + 1), :].rearrange("(p t) c -> p t c", t=PACK)[:, t, :]
+            )
+            for h in range(HALVES):
+                nc.vector.tensor_copy(
+                    x4[h][:, t, :], rows[:].indirect(idx[:, LIST_COLS * h : LIST_COLS * (h + 1)])
+                )
+
+        def quantise_w1(a, k):
+            raw = ring.tile([P, PACK, PASS], F32, name="w1_raw", bufs=2)
+            nc.sync.dma_start(
+                raw[:],
+                w1[PASS * k : PASS * (k + 1), PASS * a : PASS * (a + 1)].rearrange("(p j) c -> p j c", j=PACK),
+            )
+            grouped = ring.tile([P, PASS * PACK], BF16, name="w1_grouped", bufs=2, align_bytes=64)
+            nc.scalar.copy(
+                grouped[:].rearrange("p (t m j) -> p m j t", t=PACK, j=PACK),
+                raw[:].rearrange("p j (m t) -> p m j t", t=PACK),
+            )
+            codes = ring.tile([P, PASS], U32, name="w1_codes", bufs=4, align_bytes=64)
+            scales = ring.tile([P, PASS], U8, name="w1_scales", bufs=4, align_bytes=64)
+            nc.vector.quantize_mx(out=codes[:].bitcast(E4M3), scales=scales[:], in_=grouped[:])
+            return codes, scales
+
+        lo_t = keep.tile([P, H_PASSES, PACK], F32, name="lo_t")
+        hi_t = keep.tile([P, H_PASSES, PACK], F32, name="hi_t")
+        w2_codes = keep.tile([P, H_PASSES, N], I32, name="w2_codes", align_bytes=64)
+        w2_sc = keep.tile([P, N], U8, name="w2_sc", align_bytes=64)
+        wgo_t = keep.tile([P, S], F32, name="wgo_t")
+        idx2 = keep.tile([P, S // 16], U16, name="idx2")
+        pages = [keep.tile([P, T2], F32, name=f"page{n}") for n in range(N // P)]
+        nc.gpsimd.memset(w2_sc[:].bitcast(I32), 0)
+        for page in pages:
+            nc.gpsimd.memset(page[:], 0.0)
+
+        d_codes = {}
+        d_scales = {}
+        for a in range(H_PASSES):
+            x4 = [ring.tile([P, PACK, HALF], F32, name="x4", bufs=4) for h in range(HALVES)]
+            c4 = [ring.tile([P, PACK, HALF], F32, name="c4", bufs=4) for h in range(HALVES)]
+            w1q = []
+            if a == 0:
+                pick_table(0)
+                pick_saved(a, 0, x4)
+                pick_table(1)
+                w1q.append(quantise_w1(a, 0))
+                pick_saved(a, 1, x4)
+                w1q.append(quantise_w1(a, 1))
+                nc.sync.dma_start(lo_t[:], lo.rearrange("(a p t) -> p a t", p=P, t=PACK))
+                nc.sync.dma_start(hi_t[:], hi.rearrange("(a p t) -> p a t", p=P, t=PACK))
+            else:
+                w1q.append(quantise_w1(a, 0))
+                pick_saved(a, 0, x4)
+                w1q.append(quantise_w1(a, 1))
+                pick_saved(a, 1, x4)
+            pick_saved(a, 2, x4)
+            pick_saved(a, 3, x4)
+            if a == H_PASSES - 1:
+                nc.sync.dma_start(w2_codes[:], w2_words.rearrange("a p e i -> p a (e i)").bitcast(I32))
+                for q in range(4):
+                    nc.sync.dma_start(
+                        w2_sc[QUAD * q : QUAD * q + 4 * H_PASSES, :].bitcast(I32),
+                        w2_scales[:, 4 * q : 4 * q + 4, :].bitcast(I32),
+                    )
+                nc.sync.dma_start(wgo_t[:], wgo)
+                nc.sync.dma_start(idx2[:], offs2)
+
+            for h in range(HALVES):
+                cols = slice(HALF * h, HALF * (h + 1))
+                for t in range(PACK):
+                    acc = psum.tile([P, HALF], F32, name="h_acc")
+                    for k in range(K_PASSES):
+                        codes, scales = w1q[k]
+                        nc.tensor.matmul_mx(
+                            out=acc[:],
+                            lhsT=codes[:, P * t : P * (t + 1)].bitcast(E4M3),
+                            lhsT_scale=scales[:, P * t : P * (t + 1)],
+                            rhs=v_codes[k][:, cols].bitcast(E5M2),
+                            rhs_scale=v_sc[k][:, cols],
+                            start=(k == 0),
+                            stop=(k == K_PASSES - 1),
+                        )
+                    nc.scalar.copy(c4[h][:, t, :], acc[:])
+                x_flat = x4[h][:].rearrange("p t j -> p (t j)")
+                nc.vector.scalar_tensor_tensor(x_flat, x_flat, 1.0, x_flat, ALU.subtract, ALU.mult)
+                for t in range(PACK):
+                    nc.vector.tensor_scalar(
+                        c4[h][:, t, :], c4[h][:, t, :], lo_t[:, a, t : t + 1], hi_t[:, a, t : t + 1], ALU.max, ALU.min
+                    )
+                grouped = ring.tile([P, HALF * PACK], BF16, name="d_grouped", bufs=2, align_bytes=64)
+                nc.vector.tensor_tensor(
+                    grouped[:].rearrange("p (c i t) -> p c t i", i=4, t=PACK),
+                    c4[h][:].rearrange("p t (c i) -> p c t i", i=4),
+                    x4[h][:].rearrange("p t (c i) -> p c t i", i=4),
+                    ALU.mult,
+                )
+                d_codes[a, h] = keep.tile([P, HALF], U32, name=f"d_codes{a}{h}", align_bytes=64)
+                d_scales[a, h] = keep.tile([P, HALF], U8, name=f"d_scales{a}{h}", align_bytes=64)
+                nc.vector.quantize_mx(out=d_codes[a, h][:].bitcast(E4M3), scales=d_scales[a, h][:], in_=grouped[:])
+
+        for h in range(HALVES):
+            for n in range(N // P):
+                acc = psum.tile([P, HALF], F32, name="y_acc")
+                for a in range(H_PASSES):
+                    nc.tensor.matmul_mx(
+                        out=acc[:],
+                        lhsT=w2_codes[:, a, P * n : P * (n + 1)].bitcast(E4M3),
+                        lhsT_scale=w2_sc[4 * a : P, P * n : P * (n + 1)],
+                        rhs=d_codes[a, h][:].bitcast(E4M3),
+                        rhs_scale=d_scales[a, h][:],
+                        start=(a == 0),
+                        stop=(a == H_PASSES - 1),
+                    )
+                y = ring.tile([P, HALF], F32, name="y", bufs=4)
+                nc.scalar.activation(y[:], acc[:], ACT.Copy, scale=-1.0)
+                nc.vector.tensor_tensor(
+                    pages[n][:].indirect(idx2[:, LIST_COLS * h : LIST_COLS * (h + 1)]),
+                    y[:],
+                    wgo_t[:, HALF * h : HALF * (h + 1)],
+                    ALU.mult,
+                )
+                if h == HALVES - 1:
+                    nc.sync.dma_start(out[P * n : P * (n + 1), :], pages[n][:])

@@ -24,6 +24,7 @@ K_PASSES = K // PASS
 H_PASSES = H // PASS
 HALVES = S // HALF
 LIST_COLS = HALF // 16
+PAGES = N // P
 QUAD = 32
 TAB_ROW0 = QUAD - 4 * K_PASSES
 PLANE_ROWS = 3 * QUAD + 4
@@ -99,15 +100,15 @@ def tile_list_timeout_plan_gradients_kernel(
         w2_sc = keep.tile([P, N], U8, name="w2_sc", align_bytes=64)
         wgo_t = keep.tile([P, S], F32, name="wgo_t")
         idx2 = keep.tile([P, S // 16], U16, name="idx2")
-        pages = [keep.tile([P, T2], F32, name=f"page{n}") for n in range(N // P)]
-        nc.gpsimd.memset(w2_sc[:].bitcast(I32), 0)
-        for page in pages:
-            nc.gpsimd.memset(page[:], 0.0)
+        nc.vector.memset(w2_sc[:].bitcast(I32), 0)
 
         d_codes = {}
         d_scales = {}
         for a in range(H_PASSES):
-            x4 = [ring.tile([P, PACK, HALF], F32, name="x4", bufs=4) for h in range(HALVES)]
+            x4 = [
+                keep.tile([P, PACK, HALF], F32, name=f"x4_{a}{h}", tag=f"page{(HALVES * a + h) % PAGES}")
+                for h in range(HALVES)
+            ]
             c4 = [ring.tile([P, PACK, HALF], F32, name="c4", bufs=4) for h in range(HALVES)]
             w1q = []
             if a == 0:
@@ -153,7 +154,8 @@ def tile_list_timeout_plan_gradients_kernel(
                         )
                     nc.scalar.copy(c4[h][:, t, :], acc[:])
                 x_flat = x4[h][:].rearrange("p t j -> p (t j)")
-                nc.vector.scalar_tensor_tensor(x_flat, x_flat, 1.0, x_flat, ALU.subtract, ALU.mult)
+                slope = ring.tile([P, PACK * HALF], F32, name="slope", bufs=2)
+                nc.vector.scalar_tensor_tensor(slope[:], x_flat, 1.0, x_flat, ALU.subtract, ALU.mult)
                 for t in range(PACK):
                     nc.vector.tensor_scalar(
                         c4[h][:, t, :], c4[h][:, t, :], lo_t[:, a, t : t + 1], hi_t[:, a, t : t + 1], ALU.max, ALU.min
@@ -162,12 +164,16 @@ def tile_list_timeout_plan_gradients_kernel(
                 nc.vector.tensor_tensor(
                     grouped[:].rearrange("p (c i t) -> p c t i", i=4, t=PACK),
                     c4[h][:].rearrange("p t (c i) -> p c t i", i=4),
-                    x4[h][:].rearrange("p t (c i) -> p c t i", i=4),
+                    slope[:].rearrange("p (t c i) -> p c t i", i=4, t=PACK),
                     ALU.mult,
                 )
                 d_codes[a, h] = keep.tile([P, HALF], U32, name=f"d_codes{a}{h}", align_bytes=64)
                 d_scales[a, h] = keep.tile([P, HALF], U8, name=f"d_scales{a}{h}", align_bytes=64)
                 nc.vector.quantize_mx(out=d_codes[a, h][:].bitcast(E4M3), scales=d_scales[a, h][:], in_=grouped[:])
+
+        pages = [keep.tile([P, T2], F32, name=f"page{n}", tag=f"page{n}") for n in range(PAGES)]
+        for page in pages:
+            nc.gpsimd.memset(page[:], 0.0)
 
         for h in range(HALVES):
             for n in range(N // P):
@@ -191,4 +197,5 @@ def tile_list_timeout_plan_gradients_kernel(
                     ALU.mult,
                 )
                 if h == HALVES - 1:
-                    nc.sync.dma_start(out[P * n : P * (n + 1), :], pages[n][:])
+                    nc.sync.dma_start(out[P * n : P * (n + 1), 0 : T2 // 2], pages[n][:, 0 : T2 // 2])
+                    nc.scalar.dma_start(out[P * n : P * (n + 1), T2 // 2 : T2], pages[n][:, T2 // 2 : T2])

@@ -1,6 +1,7 @@
 from contextlib import ExitStack
 
 import concourse.mybir as mybir
+from concourse.masks import make_identity
 
 K, H, N, T, S, T2 = 1024, 1536, 512, 2048, 1024, 2048
 FLOPS = 2 * K * H * S + 2 * H * N * S
@@ -21,13 +22,18 @@ PACK = 4
 PASS = P * PACK
 HALF = 512
 K_PASSES = K // PASS
-H_PASSES = H // PASS
-HALVES = S // HALF
+GROUPS = H // PASS
 LIST_COLS = HALF // 16
 PAGES = N // P
+BLOCKS = HALF // P
+LINE = 4
 QUAD = 32
+QUADS = P // QUAD
 TAB_ROW0 = QUAD - 4 * K_PASSES
-PLANE_ROWS = 3 * QUAD + 4
+PLANE_ROWS = (QUADS - 1) * QUAD + 4
+DIRECT = 0
+TURNED = 1
+HEAD_PAGES = 2
 
 
 def tile_list_timeout_plan_gradients_kernel(
@@ -37,13 +43,13 @@ def tile_list_timeout_plan_gradients_kernel(
     with ExitStack() as ctx:
         keep = ctx.enter_context(tc.tile_pool(name="keep", bufs=1))
         ring = ctx.enter_context(tc.tile_pool(name="ring", bufs=2))
-        psum = ctx.enter_context(tc.psum_pool(name="psum", bufs=4))
+        psum = ctx.enter_context(tc.psum_pool(name="psum", bufs=2))
 
         idx = keep.tile([P, S // 16], U16, name="idx")
         nc.sync.dma_start(idx[:], offs)
 
         tab_sc = keep.tile([P, T], U8, name="tab_sc", align_bytes=64)
-        for q in range(4):
+        for q in range(QUADS):
             nc.vector.memset(tab_sc[QUAD * q : QUAD * q + TAB_ROW0, :].bitcast(I32), 0)
             nc.sync.dma_start(
                 tab_sc[QUAD * q + TAB_ROW0 : QUAD * (q + 1), :].bitcast(I32),
@@ -51,7 +57,10 @@ def tile_list_timeout_plan_gradients_kernel(
             )
         v_sc = [keep.tile([P, S], U8, name=f"v_sc{k}", align_bytes=64) for k in range(K_PASSES)]
         for k in range(K_PASSES):
-            nc.vector.memset(v_sc[k][3 * QUAD : P, :].bitcast(I32), 0)
+            nc.vector.memset(v_sc[k][(QUADS - 1) * QUAD : P, :].bitcast(I32), 0)
+        pages = [keep.tile([P, T2], F32, name=f"page{n}", tag=f"page{n}") for n in range(HEAD_PAGES)]
+        for page in pages:
+            nc.vector.memset(page[:].bitcast(I32), 0)
         picked_sc = keep.tile([P, S], U8, name="picked_sc", align_bytes=64)
         nc.vector.tensor_copy(picked_sc[:], tab_sc[:].indirect(idx[:]))
         for k in range(K_PASSES):
@@ -61,30 +70,39 @@ def tile_list_timeout_plan_gradients_kernel(
                 picked_sc[first : first + PLANE_ROWS, :].bitcast(I32),
             )
 
+        ident = keep.tile([P, P], F32, name="ident")
+        make_identity(nc, ident[:])
+
         v_codes = [keep.tile([P, S], U32, name=f"v_codes{k}", align_bytes=64) for k in range(K_PASSES)]
+        lo_t = keep.tile([P, GROUPS, PACK], F32, name="lo_t")
+        hi_t = keep.tile([P, GROUPS, PACK], F32, name="hi_t")
+        w2_sc = keep.tile([P, N], U8, name="w2_sc", align_bytes=64)
+        nc.vector.memset(w2_sc[:].bitcast(I32), 0)
+        idx2 = keep.tile([P, S // 16], U16, name="idx2")
+
+        w1q = {}
+        rows = {}
+        neg_x = {}
+        turned = {}
+        clipped = {}
+        d_codes = {}
+        d_scales = {}
+
+        def list_half(offsets, h):
+            return offsets[:, LIST_COLS * h : LIST_COLS * (h + 1)]
 
         def pick_table(k):
-            words = keep.tile([P, T], I32, name=f"tab_words{k}", align_bytes=64)
+            words = keep.tile([P, T], I32, name=f"tab_words{k}", tag=f"table{k}", align_bytes=64)
             nc.sync.dma_start(words[:], tab_words[k].rearrange("p t i -> p (t i)").bitcast(I32))
             nc.vector.tensor_copy(v_codes[k][:], words[:].bitcast(U32).indirect(idx[:]))
 
-        def pick_saved(a, t, x4):
-            rows = ring.tile([P, T], F32, name="s_rows", bufs=4)
-            nc.sync.dma_start(
-                rows[:], sT[PASS * a : PASS * (a + 1), :].rearrange("(p t) c -> p t c", t=PACK)[:, t, :]
-            )
-            for h in range(HALVES):
-                nc.vector.tensor_copy(
-                    x4[h][:, t, :], rows[:].indirect(idx[:, LIST_COLS * h : LIST_COLS * (h + 1)])
-                )
-
         def quantise_w1(a, k):
-            raw = ring.tile([P, PACK, PASS], F32, name="w1_raw", bufs=2)
+            raw = ring.tile([P, PACK, PASS], F32, name="w1_raw")
             nc.sync.dma_start(
                 raw[:],
                 w1[PASS * k : PASS * (k + 1), PASS * a : PASS * (a + 1)].rearrange("(p j) c -> p j c", j=PACK),
             )
-            grouped = ring.tile([P, PASS * PACK], BF16, name="w1_grouped", bufs=2, align_bytes=64)
+            grouped = ring.tile([P, PASS * PACK], BF16, name="w1_grouped", align_bytes=64)
             nc.scalar.copy(
                 grouped[:].rearrange("p (t m j) -> p m j t", t=PACK, j=PACK),
                 raw[:].rearrange("p j (m t) -> p m j t", t=PACK),
@@ -92,57 +110,45 @@ def tile_list_timeout_plan_gradients_kernel(
             codes = ring.tile([P, PASS], U32, name="w1_codes", bufs=4, align_bytes=64)
             scales = ring.tile([P, PASS], U8, name="w1_scales", bufs=4, align_bytes=64)
             nc.vector.quantize_mx(out=codes[:].bitcast(E4M3), scales=scales[:], in_=grouped[:])
-            return codes, scales
+            w1q[a, k] = (codes, scales)
 
-        lo_t = keep.tile([P, H_PASSES, PACK], F32, name="lo_t")
-        hi_t = keep.tile([P, H_PASSES, PACK], F32, name="hi_t")
-        w2_codes = keep.tile([P, H_PASSES, N], I32, name="w2_codes", align_bytes=64)
-        w2_sc = keep.tile([P, N], U8, name="w2_sc", align_bytes=64)
-        wgo_t = keep.tile([P, S], F32, name="wgo_t")
-        idx2 = keep.tile([P, S // 16], U16, name="idx2")
-        nc.vector.memset(w2_sc[:].bitcast(I32), 0)
+        def pick_saved(a, t, h):
+            nc.vector.tensor_scalar(
+                neg_x[a, h][:, t, :], rows[a, t][:].indirect(list_half(idx, h)), -1.0, 0.0, ALU.mult, ALU.add
+            )
 
-        d_codes = {}
-        d_scales = {}
-        for a in range(H_PASSES):
-            x4 = [
-                keep.tile([P, PACK, HALF], F32, name=f"x4_{a}{h}", tag=f"page{(HALVES * a + h) % PAGES}")
-                for h in range(HALVES)
-            ]
-            c4 = [ring.tile([P, PACK, HALF], F32, name="c4", bufs=4) for h in range(HALVES)]
-            w1q = []
-            if a == 0:
-                pick_table(0)
-                pick_saved(a, 0, x4)
-                pick_table(1)
-                w1q.append(quantise_w1(a, 0))
-                pick_saved(a, 1, x4)
-                w1q.append(quantise_w1(a, 1))
-                nc.sync.dma_start(lo_t[:], lo.rearrange("(a p t) -> p a t", p=P, t=PACK))
-                nc.sync.dma_start(hi_t[:], hi.rearrange("(a p t) -> p a t", p=P, t=PACK))
-            else:
-                w1q.append(quantise_w1(a, 0))
-                pick_saved(a, 0, x4)
-                w1q.append(quantise_w1(a, 1))
-                pick_saved(a, 1, x4)
-            pick_saved(a, 2, x4)
-            pick_saved(a, 3, x4)
-            if a == H_PASSES - 1:
-                nc.sync.dma_start(w2_codes[:], w2_words.rearrange("a p e i -> p a (e i)").bitcast(I32))
-                for q in range(4):
-                    nc.sync.dma_start(
-                        w2_sc[QUAD * q : QUAD * q + 4 * H_PASSES, :].bitcast(I32),
-                        w2_scales[:, 4 * q : 4 * q + 4, :].bitcast(I32),
-                    )
-                nc.sync.dma_start(wgo_t[:], wgo)
-                nc.sync.dma_start(idx2[:], offs2)
+        def open_group(a):
+            neg_x[a, DIRECT] = keep.tile(
+                [P, PACK, HALF], F32, name=f"neg_x{a}", tag=f"page{HEAD_PAGES + a % (PAGES - HEAD_PAGES)}"
+            )
+            neg_x[a, TURNED] = ring.tile([P, PACK, HALF], F32, name="neg_x_turned")
+            turned[a] = ring.tile([P, PACK, BLOCKS, P], F32, name="turned")
 
-            for h in range(HALVES):
+        def load_and_turn(a, t):
+            rows[a, t] = ring.tile([P, T], F32, name="s_rows", bufs=4)
+            nc.sync.dma_start(
+                rows[a, t][:], sT[PASS * a : PASS * (a + 1), :].rearrange("(p t) c -> p t c", t=PACK)[:, t, :]
+            )
+            pick_saved(a, t, TURNED)
+            picked = neg_x[a, TURNED][:, t, :]
+            squares = ring.tile([P, HALF], F32, name="squares")
+            nc.scalar.activation(squares[:], picked, ACT.Square)
+            there = psum.tile([P, BLOCKS, P], F32, name="there")
+            for b in range(BLOCKS):
+                block = slice(P * b, P * (b + 1))
+                nc.tensor.matmul(there[:, b, :], squares[:, block], ident[:], start=True, stop=False, is_transpose=True)
+                nc.tensor.matmul(there[:, b, :], picked[:, block], ident[:], start=False, stop=True, is_transpose=True)
+            nc.scalar.copy(turned[a][:, t, :, :], there[:])
+
+        def hidden(a):
+            for h in (DIRECT, TURNED):
+                clipped[a, h] = ring.tile([P, PACK, HALF], F32, name="clipped", bufs=4)
+            for h in (TURNED, DIRECT):
                 cols = slice(HALF * h, HALF * (h + 1))
                 for t in range(PACK):
-                    acc = psum.tile([P, HALF], F32, name="h_acc")
+                    acc = psum.tile([P, HALF], F32, name="h_acc", tag="acc", bufs=4)
                     for k in range(K_PASSES):
-                        codes, scales = w1q[k]
+                        codes, scales = w1q[a, k]
                         nc.tensor.matmul_mx(
                             out=acc[:],
                             lhsT=codes[:, P * t : P * (t + 1)].bitcast(E4M3),
@@ -152,33 +158,91 @@ def tile_list_timeout_plan_gradients_kernel(
                             start=(k == 0),
                             stop=(k == K_PASSES - 1),
                         )
-                    nc.scalar.copy(c4[h][:, t, :], acc[:])
-                x_flat = x4[h][:].rearrange("p t j -> p (t j)")
-                slope = ring.tile([P, PACK * HALF], F32, name="slope", bufs=2)
-                nc.vector.scalar_tensor_tensor(slope[:], x_flat, 1.0, x_flat, ALU.subtract, ALU.mult)
+                    c = clipped[a, h][:, t, :]
+                    nc.scalar.copy(c, acc[:])
+                    nc.vector.tensor_scalar(c, c, lo_t[:, a, t : t + 1], hi_t[:, a, t : t + 1], ALU.max, ALU.min)
+
+        def interleaved_product(dst, slope, c):
+            nc.vector.tensor_tensor(
+                dst.rearrange("p (g i t) -> p g t i", i=LINE, t=PACK),
+                slope.rearrange("p t (g i) -> p g t i", i=LINE),
+                c.rearrange("p t (g i) -> p g t i", i=LINE),
+                ALU.mult,
+            )
+
+        def quantise_d(a, h, grouped):
+            d_codes[a, h] = keep.tile([P, HALF], U32, name=f"d_codes{a}{h}", align_bytes=64)
+            d_scales[a, h] = keep.tile([P, HALF], U8, name=f"d_scales{a}{h}", align_bytes=64)
+            nc.vector.quantize_mx(out=d_codes[a, h][:].bitcast(E4M3), scales=d_scales[a, h][:], in_=grouped[:])
+
+        def finish(a):
+            picked = neg_x[a, DIRECT][:].rearrange("p t j -> p (t j)")
+            slope = ring.tile([P, PACK, HALF], F32, name="slope", bufs=1)
+            nc.vector.scalar_tensor_tensor(
+                slope[:].rearrange("p t j -> p (t j)"), picked, 1.0, picked, ALU.add, ALU.mult
+            )
+            grouped = ring.tile([P, HALF * PACK], BF16, name="d_grouped", align_bytes=64)
+            interleaved_product(grouped[:], slope[:], clipped[a, DIRECT][:])
+            quantise_d(a, DIRECT, grouped)
+
+            grouped = ring.tile([P, HALF * PACK], BF16, name="d_grouped", align_bytes=64)
+            for b in range(BLOCKS):
+                back = psum.tile([P, PACK, P], F32, name="back")
                 for t in range(PACK):
-                    nc.vector.tensor_scalar(
-                        c4[h][:, t, :], c4[h][:, t, :], lo_t[:, a, t : t + 1], hi_t[:, a, t : t + 1], ALU.max, ALU.min
-                    )
-                grouped = ring.tile([P, HALF * PACK], BF16, name="d_grouped", bufs=2, align_bytes=64)
-                nc.vector.tensor_tensor(
-                    grouped[:].rearrange("p (c i t) -> p c t i", i=4, t=PACK),
-                    c4[h][:].rearrange("p t (c i) -> p c t i", i=4),
-                    slope[:].rearrange("p (t c i) -> p c t i", i=4, t=PACK),
-                    ALU.mult,
+                    nc.tensor.transpose(back[:, t, :], turned[a][:, t, b, :], ident[:])
+                interleaved_product(
+                    grouped[:, PASS * b : PASS * (b + 1)], back[:], clipped[a, TURNED][:, :, P * b : P * (b + 1)]
                 )
-                d_codes[a, h] = keep.tile([P, HALF], U32, name=f"d_codes{a}{h}", align_bytes=64)
-                d_scales[a, h] = keep.tile([P, HALF], U8, name=f"d_scales{a}{h}", align_bytes=64)
-                nc.vector.quantize_mx(out=d_codes[a, h][:].bitcast(E4M3), scales=d_scales[a, h][:], in_=grouped[:])
+            quantise_d(a, TURNED, grouped)
 
-        pages = [keep.tile([P, T2], F32, name=f"page{n}", tag=f"page{n}") for n in range(PAGES)]
-        for page in pages:
-            nc.gpsimd.memset(page[:], 0.0)
+        pick_table(0)
+        open_group(0)
+        load_and_turn(0, 0)
+        pick_table(1)
+        load_and_turn(0, 1)
+        quantise_w1(0, 0)
+        load_and_turn(0, 2)
+        quantise_w1(0, 1)
+        nc.sync.dma_start(lo_t[:], lo.rearrange("(a p t) -> p a t", p=P, t=PACK))
+        nc.sync.dma_start(hi_t[:], hi.rearrange("(a p t) -> p a t", p=P, t=PACK))
+        load_and_turn(0, 3)
+        hidden(0)
+        for t in range(PACK):
+            pick_saved(0, t, DIRECT)
+        for k in range(K_PASSES):
+            quantise_w1(1, k)
 
-        for h in range(HALVES):
-            for n in range(N // P):
-                acc = psum.tile([P, HALF], F32, name="y_acc")
-                for a in range(H_PASSES):
+        for a in range(1, GROUPS):
+            finish(a - 1)
+            hidden(a)
+            open_group(a)
+            for t in range(PACK):
+                load_and_turn(a, t)
+                if a + 1 < GROUPS and t < K_PASSES:
+                    quantise_w1(a + 1, t)
+            for t in range(PACK):
+                pick_saved(a, t, DIRECT)
+        finish(GROUPS - 1)
+
+        w2_codes = keep.tile([P, GROUPS, N], I32, name="w2_codes", tag="table0", align_bytes=64)
+        wgo_t = keep.tile([P, S], F32, name="wgo_t", tag="table1", align_bytes=64)
+        nc.sync.dma_start(w2_codes[:], w2_words.rearrange("a p e i -> p a (e i)").bitcast(I32))
+        for q in range(QUADS):
+            nc.sync.dma_start(
+                w2_sc[QUAD * q : QUAD * q + 4 * GROUPS, :].bitcast(I32),
+                w2_scales[:, 4 * q : 4 * q + 4, :].bitcast(I32),
+            )
+        nc.sync.dma_start(wgo_t[:], wgo)
+        nc.sync.dma_start(idx2[:], offs2)
+
+        for n in range(HEAD_PAGES, PAGES):
+            pages.append(keep.tile([P, T2], F32, name=f"page{n}", tag=f"page{n}"))
+            nc.gpsimd.memset(pages[n][:], 0.0)
+
+        for h in (DIRECT, TURNED):
+            for n in range(PAGES):
+                acc = psum.tile([P, HALF], F32, name="y_acc", tag="acc", bufs=4)
+                for a in range(GROUPS):
                     nc.tensor.matmul_mx(
                         out=acc[:],
                         lhsT=w2_codes[:, a, P * n : P * (n + 1)].bitcast(E4M3),
@@ -186,16 +250,14 @@ def tile_list_timeout_plan_gradients_kernel(
                         rhs=d_codes[a, h][:].bitcast(E4M3),
                         rhs_scale=d_scales[a, h][:],
                         start=(a == 0),
-                        stop=(a == H_PASSES - 1),
+                        stop=(a == GROUPS - 1),
                     )
                 y = ring.tile([P, HALF], F32, name="y", bufs=4)
                 nc.scalar.activation(y[:], acc[:], ACT.Copy, scale=-1.0)
                 nc.vector.tensor_tensor(
-                    pages[n][:].indirect(idx2[:, LIST_COLS * h : LIST_COLS * (h + 1)]),
-                    y[:],
-                    wgo_t[:, HALF * h : HALF * (h + 1)],
-                    ALU.mult,
+                    pages[n][:].indirect(list_half(idx2, h)), y[:], wgo_t[:, HALF * h : HALF * (h + 1)], ALU.mult
                 )
-                if h == HALVES - 1:
-                    nc.sync.dma_start(out[P * n : P * (n + 1), 0 : T2 // 2], pages[n][:, 0 : T2 // 2])
-                    nc.scalar.dma_start(out[P * n : P * (n + 1), T2 // 2 : T2], pages[n][:, T2 // 2 : T2])
+                if h == TURNED:
+                    for part in range(2):
+                        cols = slice(part * T2 // 2, (part + 1) * T2 // 2)
+                        nc.sync.dma_start(out[P * n : P * (n + 1), cols], pages[n][:, cols])

@@ -175,7 +175,7 @@ def tile_list_timeout_plan_gradients_kernel(
             d_scales[a, h] = keep.tile([P, HALF], U8, name=f"d_scales{a}{h}", align_bytes=64)
             nc.vector.quantize_mx(out=d_codes[a, h][:].bitcast(E4M3), scales=d_scales[a, h][:], in_=grouped[:])
 
-        def finish(a):
+        def finish_direct(a):
             picked = neg_x[a, DIRECT][:].rearrange("p t j -> p (t j)")
             slope = ring.tile([P, PACK, HALF], F32, name="slope", bufs=1)
             nc.vector.scalar_tensor_tensor(
@@ -185,6 +185,7 @@ def tile_list_timeout_plan_gradients_kernel(
             interleaved_product(grouped[:], slope[:], clipped[a, DIRECT][:])
             quantise_d(a, DIRECT, grouped)
 
+        def finish_turned(a):
             grouped = ring.tile([P, HALF * PACK], BF16, name="d_grouped", align_bytes=64)
             for b in range(BLOCKS):
                 back = psum.tile([P, PACK, P], F32, name="back")
@@ -213,7 +214,8 @@ def tile_list_timeout_plan_gradients_kernel(
             quantise_w1(1, k)
 
         for a in range(1, GROUPS):
-            finish(a - 1)
+            finish_turned(a - 1)
+            finish_direct(a - 1)
             hidden(a)
             open_group(a)
             for t in range(PACK):
@@ -222,7 +224,8 @@ def tile_list_timeout_plan_gradients_kernel(
                     quantise_w1(a + 1, t)
             for t in range(PACK):
                 pick_saved(a, t, DIRECT)
-        finish(GROUPS - 1)
+        finish_direct(GROUPS - 1)
+        finish_turned(GROUPS - 1)
 
         w2_codes = keep.tile([P, GROUPS, N], I32, name="w2_codes", tag="table0", align_bytes=64)
         wgo_t = keep.tile([P, S], F32, name="wgo_t", tag="table1", align_bytes=64)

@@ -26,13 +26,12 @@ GROUPS = H // PASS
 LIST_COLS = HALF // 16
 PAGES = N // P
 BLOCKS = HALF // P
-LINE = 4
+LINE = 2
 QUAD = 32
 QUADS = P // QUAD
 TAB_ROW0 = QUAD - 4 * K_PASSES
 PLANE_ROWS = (QUADS - 1) * QUAD + 4
-DIRECT = 0
-TURNED = 1
+HALVES = S // HALF
 HEAD_PAGES = 2
 
 
@@ -48,7 +47,7 @@ def tile_list_timeout_plan_gradients_kernel(
         idx = keep.tile([P, S // 16], U16, name="idx")
         nc.sync.dma_start(idx[:], offs)
 
-        tab_sc = keep.tile([P, T], U8, name="tab_sc", align_bytes=64)
+        tab_sc = keep.tile([P, T], U8, name="tab_sc", tag="page2", align_bytes=64)
         for q in range(QUADS):
             nc.vector.memset(tab_sc[QUAD * q : QUAD * q + TAB_ROW0, :].bitcast(I32), 0)
             nc.sync.dma_start(
@@ -58,14 +57,14 @@ def tile_list_timeout_plan_gradients_kernel(
         v_sc = [keep.tile([P, S], U8, name=f"v_sc{k}", align_bytes=64) for k in range(K_PASSES)]
         for k in range(K_PASSES):
             nc.vector.memset(v_sc[k][(QUADS - 1) * QUAD : P, :].bitcast(I32), 0)
-        pages = [keep.tile([P, T2], F32, name=f"page{n}", tag=f"page{n}") for n in range(HEAD_PAGES)]
+        pages = [keep.tile([P, T2], F32, name=f"page{n}") for n in range(HEAD_PAGES)]
         for page in pages:
             nc.vector.memset(page[:].bitcast(I32), 0)
-        picked_sc = keep.tile([P, S], U8, name="picked_sc", align_bytes=64)
+        picked_sc = keep.tile([P, S], U8, name="picked_sc", tag="page3", align_bytes=64)
         nc.vector.tensor_copy(picked_sc[:], tab_sc[:].indirect(idx[:]))
         for k in range(K_PASSES):
             first = TAB_ROW0 + 4 * k
-            nc.scalar.dma_start(
+            nc.gpsimd.dma_start(
                 v_sc[k][0:PLANE_ROWS, :].bitcast(I32),
                 picked_sc[first : first + PLANE_ROWS, :].bitcast(I32),
             )
@@ -88,79 +87,85 @@ def tile_list_timeout_plan_gradients_kernel(
         d_codes = {}
         d_scales = {}
 
+        def turned_blocks(a, h):
+            return ((0, 0), (4, 4), (0, 4))[a][h]
+
         def list_half(offsets, h):
             return offsets[:, LIST_COLS * h : LIST_COLS * (h + 1)]
 
         def pick_table(k):
-            words = keep.tile([P, T], I32, name=f"tab_words{k}", tag=f"table{k}", align_bytes=64)
+            words = ring.tile([P, T], I32, name="tab_words", tag="s_rows", bufs=4)
             nc.sync.dma_start(words[:], tab_words[k].rearrange("p t i -> p (t i)").bitcast(I32))
             nc.vector.tensor_copy(v_codes[k][:], words[:].bitcast(U32).indirect(idx[:]))
 
         def quantise_w1(a, k):
-            raw = ring.tile([P, PACK, PASS], F32, name="w1_raw")
+            raw = ring.tile([P, PACK, PASS], F32, name="w1_raw", align_bytes=64)
             nc.sync.dma_start(
                 raw[:],
                 w1[PASS * k : PASS * (k + 1), PASS * a : PASS * (a + 1)].rearrange("(p j) c -> p j c", j=PACK),
             )
             grouped = ring.tile([P, PASS * PACK], BF16, name="w1_grouped", align_bytes=64)
-            nc.scalar.copy(
-                grouped[:].rearrange("p (t m j) -> p m j t", t=PACK, j=PACK),
-                raw[:].rearrange("p j (m t) -> p m j t", t=PACK),
-            )
+            sorted_out = grouped[:].rearrange("p (t m j) -> p m j t", t=PACK, j=PACK)
+            sorted_in = raw[:].rearrange("p j (m t) -> p m j t", t=PACK)
+            if True:
+                nc.scalar.copy(sorted_out, sorted_in)
+            else:
+                nc.gpsimd.tensor_scalar(sorted_out, sorted_in, 1.0, 0.0, ALU.mult, ALU.add)
             codes = ring.tile([P, PASS], U32, name="w1_codes", bufs=4, align_bytes=64)
             scales = ring.tile([P, PASS], U8, name="w1_scales", bufs=4, align_bytes=64)
             nc.vector.quantize_mx(out=codes[:].bitcast(E4M3), scales=scales[:], in_=grouped[:])
             w1q[a, k] = (codes, scales)
 
-        def pick_saved(a, t, h):
-            nc.vector.tensor_scalar(
-                neg_x[a, h][:, t, :], rows[a, t][:].indirect(list_half(idx, h)), -1.0, 0.0, ALU.mult, ALU.add
-            )
-
-        def open_group(a):
-            neg_x[a, DIRECT] = keep.tile(
-                [P, PACK, HALF], F32, name=f"neg_x{a}", tag=f"page{HEAD_PAGES + a % (PAGES - HEAD_PAGES)}"
-            )
-            neg_x[a, TURNED] = ring.tile([P, PACK, HALF], F32, name="neg_x_turned")
-            turned[a] = ring.tile([P, PACK, BLOCKS, P], F32, name="turned")
-
-        def load_and_turn(a, t):
+        def load_rows(a, t):
             rows[a, t] = ring.tile([P, T], F32, name="s_rows", bufs=4)
             nc.sync.dma_start(
                 rows[a, t][:], sT[PASS * a : PASS * (a + 1), :].rearrange("(p t) c -> p t c", t=PACK)[:, t, :]
             )
-            pick_saved(a, t, TURNED)
-            picked = neg_x[a, TURNED][:, t, :]
-            squares = ring.tile([P, HALF], F32, name="squares")
-            nc.scalar.activation(squares[:], picked, ACT.Square)
-            there = psum.tile([P, BLOCKS, P], F32, name="there")
-            for b in range(BLOCKS):
+
+        def pick(a, t, h):
+            if t == 0:
+                neg_x[a, h] = ring.tile([P, PACK, HALF], F32, name="neg_x", bufs=4)
+            nc.vector.tensor_scalar(
+                neg_x[a, h][:, t, :], rows[a, t][:].indirect(list_half(idx, h)), -1.0, 0.0, ALU.mult, ALU.add
+            )
+            blocks = turned_blocks(a, h)
+            if blocks < BLOCKS:
+                direct = neg_x[a, h][:, t, P * blocks : HALF]
+                nc.vector.scalar_tensor_tensor(direct, direct, 1.0, direct, ALU.add, ALU.mult)
+            if blocks == 0:
+                return
+            if t == 0:
+                turned[a, h] = ring.tile([P, PACK, BLOCKS, P], F32, name="turned", bufs=3)
+            picked = neg_x[a, h][:, t, :]
+            squares = ring.tile([P, HALF], F32, name="squares", tag="scratch", bufs=4)
+            nc.scalar.activation(squares[:, 0 : P * blocks], picked[:, 0 : P * blocks], ACT.Square)
+            there = psum.tile([P, BLOCKS, P], F32, name="there", bufs=2)
+            for b in range(blocks):
                 block = slice(P * b, P * (b + 1))
                 nc.tensor.matmul(there[:, b, :], squares[:, block], ident[:], start=True, stop=False, is_transpose=True)
                 nc.tensor.matmul(there[:, b, :], picked[:, block], ident[:], start=False, stop=True, is_transpose=True)
-            nc.scalar.copy(turned[a][:, t, :, :], there[:])
+            nc.scalar.copy(turned[a, h][:, t, 0:blocks, :], there[:, 0:blocks, :])
 
-        def hidden(a):
-            for h in (DIRECT, TURNED):
-                clipped[a, h] = ring.tile([P, PACK, HALF], F32, name="clipped", bufs=4)
-            for h in (TURNED, DIRECT):
-                cols = slice(HALF * h, HALF * (h + 1))
-                for t in range(PACK):
-                    acc = psum.tile([P, HALF], F32, name="h_acc", tag="acc", bufs=4)
-                    for k in range(K_PASSES):
-                        codes, scales = w1q[a, k]
-                        nc.tensor.matmul_mx(
-                            out=acc[:],
-                            lhsT=codes[:, P * t : P * (t + 1)].bitcast(E4M3),
-                            lhsT_scale=scales[:, P * t : P * (t + 1)],
-                            rhs=v_codes[k][:, cols].bitcast(E5M2),
-                            rhs_scale=v_sc[k][:, cols],
-                            start=(k == 0),
-                            stop=(k == K_PASSES - 1),
-                        )
-                    c = clipped[a, h][:, t, :]
-                    nc.scalar.copy(c, acc[:])
-                    nc.vector.tensor_scalar(c, c, lo_t[:, a, t : t + 1], hi_t[:, a, t : t + 1], ALU.max, ALU.min)
+        def hidden(a, h, slices=range(PACK)):
+            cols = slice(HALF * h, HALF * (h + 1))
+            for t in slices:
+                if t == 0:
+                    clipped[a, h] = ring.tile([P, PACK, HALF], F32, name="clipped", bufs=4)
+                acc = psum.tile([P, HALF], F32, name="h_acc", tag="acc", bufs=4)
+                for k in range(K_PASSES):
+                    codes, scales = w1q[a, k]
+                    nc.tensor.matmul_mx(
+                        out=acc[:],
+                        lhsT=codes[:, P * t : P * (t + 1)].bitcast(E4M3),
+                        lhsT_scale=scales[:, P * t : P * (t + 1)],
+                        rhs=v_codes[k][:, cols].bitcast(E5M2),
+                        rhs_scale=v_sc[k][:, cols],
+                        start=(k == 0),
+                        stop=(k == K_PASSES - 1),
+                    )
+                c = clipped[a, h][:, t, :]
+                nc.scalar.copy(c, acc[:])
+                nc.vector.tensor_scalar(c, c, hi_t[:, a, t : t + 1], lo_t[:, a, t : t + 1], ALU.min, ALU.max)
 
         def interleaved_product(dst, slope, c):
             nc.vector.tensor_tensor(
@@ -170,65 +175,58 @@ def tile_list_timeout_plan_gradients_kernel(
                 ALU.mult,
             )
 
-        def quantise_d(a, h, grouped):
+        def finish(a, h):
+            grouped = ring.tile([P, HALF * PACK], BF16, name="d_grouped", align_bytes=64)
+            blocks = turned_blocks(a, h)
+            if blocks < BLOCKS:
+                first = P * blocks
+                interleaved_product(
+                    grouped[:, PACK * first : PACK * HALF], neg_x[a, h][:, :, first:HALF], clipped[a, h][:, :, first:HALF]
+                )
+            for b in range(blocks):
+                back = psum.tile([P, PACK, P], F32, name="back", bufs=2)
+                for t in range(PACK):
+                    nc.tensor.transpose(back[:, t, :], turned[a, h][:, t, b, :], ident[:])
+                interleaved_product(
+                    grouped[:, PASS * b : PASS * (b + 1)], back[:], clipped[a, h][:, :, P * b : P * (b + 1)]
+                )
             d_codes[a, h] = keep.tile([P, HALF], U32, name=f"d_codes{a}{h}", align_bytes=64)
             d_scales[a, h] = keep.tile([P, HALF], U8, name=f"d_scales{a}{h}", align_bytes=64)
             nc.vector.quantize_mx(out=d_codes[a, h][:].bitcast(E4M3), scales=d_scales[a, h][:], in_=grouped[:])
 
-        def finish_direct(a):
-            picked = neg_x[a, DIRECT][:].rearrange("p t j -> p (t j)")
-            slope = ring.tile([P, PACK, HALF], F32, name="slope", bufs=1)
-            nc.vector.scalar_tensor_tensor(
-                slope[:].rearrange("p t j -> p (t j)"), picked, 1.0, picked, ALU.add, ALU.mult
-            )
-            grouped = ring.tile([P, HALF * PACK], BF16, name="d_grouped", align_bytes=64)
-            interleaved_product(grouped[:], slope[:], clipped[a, DIRECT][:])
-            quantise_d(a, DIRECT, grouped)
-
-        def finish_turned(a):
-            grouped = ring.tile([P, HALF * PACK], BF16, name="d_grouped", align_bytes=64)
-            for b in range(BLOCKS):
-                back = psum.tile([P, PACK, P], F32, name="back")
-                for t in range(PACK):
-                    nc.tensor.transpose(back[:, t, :], turned[a][:, t, b, :], ident[:])
-                interleaved_product(
-                    grouped[:, PASS * b : PASS * (b + 1)], back[:], clipped[a, TURNED][:, :, P * b : P * (b + 1)]
-                )
-            quantise_d(a, TURNED, grouped)
+        def both(a, t):
+            load_rows(a, t)
+            pick(a, t, 1)
+            pick(a, t, 0)
 
         pick_table(0)
-        open_group(0)
-        load_and_turn(0, 0)
-        pick_table(1)
-        load_and_turn(0, 1)
+        both(0, 0)
+        both(0, 1)
         quantise_w1(0, 0)
-        load_and_turn(0, 2)
+        pick_table(1)
+        both(0, 2)
         quantise_w1(0, 1)
         nc.sync.dma_start(lo_t[:], lo.rearrange("(a p t) -> p a t", p=P, t=PACK))
         nc.sync.dma_start(hi_t[:], hi.rearrange("(a p t) -> p a t", p=P, t=PACK))
-        load_and_turn(0, 3)
-        hidden(0)
-        for t in range(PACK):
-            pick_saved(0, t, DIRECT)
-        for k in range(K_PASSES):
-            quantise_w1(1, k)
-
+        both(0, 3)
+        hidden(0, 0)
+        hidden(0, 1)
         for a in range(1, GROUPS):
-            finish_turned(a - 1)
-            finish_direct(a - 1)
-            hidden(a)
-            open_group(a)
-            for t in range(PACK):
-                load_and_turn(a, t)
-                if a + 1 < GROUPS and t < K_PASSES:
-                    quantise_w1(a + 1, t)
-            for t in range(PACK):
-                pick_saved(a, t, DIRECT)
-        finish_direct(GROUPS - 1)
-        finish_turned(GROUPS - 1)
+            quantise_w1(a, 0)
+            both(a, 0)
+            quantise_w1(a, 1)
+            finish(a - 1, 0)
+            both(a, 1)
+            finish(a - 1, 1)
+            hidden(a, 0)
+            hidden(a, 1)
+            both(a, 2)
+            both(a, 3)
+        finish(GROUPS - 1, 0)
+        finish(GROUPS - 1, 1)
 
-        w2_codes = keep.tile([P, GROUPS, N], I32, name="w2_codes", tag="table0", align_bytes=64)
-        wgo_t = keep.tile([P, S], F32, name="wgo_t", tag="table1", align_bytes=64)
+        w2_codes = ring.tile([P, GROUPS, N], I32, name="w2_codes", tag="w1_raw", align_bytes=64)
+        wgo_t = ring.tile([P, S], F32, name="wgo_t", tag="w1_raw", align_bytes=64)
         nc.sync.dma_start(w2_codes[:], w2_words.rearrange("a p e i -> p a (e i)").bitcast(I32))
         for q in range(QUADS):
             nc.sync.dma_start(
@@ -239,10 +237,10 @@ def tile_list_timeout_plan_gradients_kernel(
         nc.sync.dma_start(idx2[:], offs2)
 
         for n in range(HEAD_PAGES, PAGES):
-            pages.append(keep.tile([P, T2], F32, name=f"page{n}", tag=f"page{n}"))
+            pages.append(keep.tile([P, T2], F32, name=f"page{n}", tag=f"page{n}", align_bytes=64))
             nc.gpsimd.memset(pages[n][:], 0.0)
 
-        for h in (DIRECT, TURNED):
+        for h in range(HALVES):
             for n in range(PAGES):
                 acc = psum.tile([P, HALF], F32, name="y_acc", tag="acc", bufs=4)
                 for a in range(GROUPS):
@@ -255,12 +253,12 @@ def tile_list_timeout_plan_gradients_kernel(
                         start=(a == 0),
                         stop=(a == GROUPS - 1),
                     )
-                y = ring.tile([P, HALF], F32, name="y", bufs=4)
+                y = ring.tile([P, HALF], F32, name="y", tag="scratch", bufs=4)
                 nc.scalar.activation(y[:], acc[:], ACT.Copy, scale=-1.0)
                 nc.vector.tensor_tensor(
                     pages[n][:].indirect(list_half(idx2, h)), y[:], wgo_t[:, HALF * h : HALF * (h + 1)], ALU.mult
                 )
-                if h == TURNED:
+                if h == HALVES - 1:
                     for part in range(2):
                         cols = slice(part * T2 // 2, (part + 1) * T2 // 2)
                         nc.sync.dma_start(out[P * n : P * (n + 1), cols], pages[n][:, cols])

@@ -33,6 +33,7 @@ TAB_ROW0 = QUAD - 4 * K_PASSES
 PLANE_ROWS = (QUADS - 1) * QUAD + 4
 HALVES = S // HALF
 HEAD_PAGES = 2
+DIRECT = ((0, 0), (0, 1), (2, 0))
 
 
 def tile_list_timeout_plan_gradients_kernel(
@@ -81,25 +82,22 @@ def tile_list_timeout_plan_gradients_kernel(
 
         w1q = {}
         rows = {}
-        neg_x = {}
+        slope = {}
         turned = {}
         clipped = {}
         d_codes = {}
         d_scales = {}
 
-        def turned_blocks(a, h):
-            return ((0, 0), (4, 4), (0, 4))[a][h]
-
         def list_half(offsets, h):
             return offsets[:, LIST_COLS * h : LIST_COLS * (h + 1)]
 
         def pick_table(k):
-            words = ring.tile([P, T], I32, name="tab_words", tag="s_rows", bufs=4)
+            words = ring.tile([P, T], I32, name="tab_words", tag="loads", bufs=6, align_bytes=64)
             nc.sync.dma_start(words[:], tab_words[k].rearrange("p t i -> p (t i)").bitcast(I32))
             nc.vector.tensor_copy(v_codes[k][:], words[:].bitcast(U32).indirect(idx[:]))
 
         def quantise_w1(a, k):
-            raw = ring.tile([P, PACK, PASS], F32, name="w1_raw", align_bytes=64)
+            raw = ring.tile([P, PACK, PASS], F32, name="w1_raw", tag="loads", bufs=6, align_bytes=64)
             nc.sync.dma_start(
                 raw[:],
                 w1[PASS * k : PASS * (k + 1), PASS * a : PASS * (a + 1)].rearrange("(p j) c -> p j c", j=PACK),
@@ -117,78 +115,85 @@ def tile_list_timeout_plan_gradients_kernel(
             w1q[a, k] = (codes, scales)
 
         def load_rows(a, t):
-            rows[a, t] = ring.tile([P, T], F32, name="s_rows", bufs=4)
+            rows[a, t] = ring.tile([P, T], F32, name="s_rows", tag="loads", bufs=6, align_bytes=64)
             nc.sync.dma_start(
                 rows[a, t][:], sT[PASS * a : PASS * (a + 1), :].rearrange("(p t) c -> p t c", t=PACK)[:, t, :]
             )
 
+        def pick_whole(a, t):
+            if t == 0:
+                both_halves = ring.tile([P, PACK, S], F32, name="slope_whole", bufs=1)
+                for h in range(HALVES):
+                    slope[a, h] = both_halves[:, :, HALF * h : HALF * (h + 1)]
+                slope[a] = both_halves
+            picked = slope[a][:, t, :]
+            nc.vector.tensor_copy(picked, rows[a, t][:].indirect(idx[:]))
+            nc.vector.scalar_tensor_tensor(picked, picked, 1.0, picked, ALU.subtract, ALU.mult)
+
         def pick(a, t, h):
-            if t == 0:
-                neg_x[a, h] = ring.tile([P, PACK, HALF], F32, name="neg_x", bufs=4)
-            nc.vector.tensor_scalar(
-                neg_x[a, h][:, t, :], rows[a, t][:].indirect(list_half(idx, h)), -1.0, 0.0, ALU.mult, ALU.add
-            )
-            blocks = turned_blocks(a, h)
-            if blocks < BLOCKS:
-                direct = neg_x[a, h][:, t, P * blocks : HALF]
-                nc.vector.scalar_tensor_tensor(direct, direct, 1.0, direct, ALU.add, ALU.mult)
-            if blocks == 0:
+            if (a, h) in DIRECT:
+                if t == 0:
+                    slope[a, h] = ring.tile([P, PACK, HALF], F32, name="slope", bufs=1)[:]
+                picked = slope[a, h][:, t, :]
+            else:
+                if t == 0:
+                    turned[a, h] = ring.tile([P, PACK, BLOCKS, P], F32, name="turned", bufs=3)
+                picked = ring.tile([P, HALF], F32, name="neg_x", bufs=6)[:]
+            nc.vector.tensor_scalar(picked, rows[a, t][:].indirect(list_half(idx, h)), -1.0, 0.0, ALU.mult, ALU.add)
+            if (a, h) in DIRECT:
+                if t % 1 == 1 - 1:
+                    run = slope[a, h][:, t + 1 - 1 : t + 1, :].rearrange("p t j -> p (t j)")
+                    nc.vector.scalar_tensor_tensor(run, run, 1.0, run, ALU.add, ALU.mult)
                 return
-            if t == 0:
-                turned[a, h] = ring.tile([P, PACK, BLOCKS, P], F32, name="turned", bufs=3)
-            picked = neg_x[a, h][:, t, :]
             squares = ring.tile([P, HALF], F32, name="squares", tag="scratch", bufs=4)
-            nc.scalar.activation(squares[:, 0 : P * blocks], picked[:, 0 : P * blocks], ACT.Square)
+            nc.scalar.activation(squares[:], picked, ACT.Square)
             there = psum.tile([P, BLOCKS, P], F32, name="there", bufs=2)
-            for b in range(blocks):
+            for b in range(BLOCKS):
                 block = slice(P * b, P * (b + 1))
                 nc.tensor.matmul(there[:, b, :], squares[:, block], ident[:], start=True, stop=False, is_transpose=True)
                 nc.tensor.matmul(there[:, b, :], picked[:, block], ident[:], start=False, stop=True, is_transpose=True)
-            nc.scalar.copy(turned[a, h][:, t, 0:blocks, :], there[:, 0:blocks, :])
+            nc.scalar.copy(turned[a, h][:, t, :, :], there[:])
 
-        def hidden(a, h, slices=range(PACK)):
-            cols = slice(HALF * h, HALF * (h + 1))
+        def hidden(a, slices):
             for t in slices:
                 if t == 0:
-                    clipped[a, h] = ring.tile([P, PACK, HALF], F32, name="clipped", bufs=4)
-                acc = psum.tile([P, HALF], F32, name="h_acc", tag="acc", bufs=4)
-                for k in range(K_PASSES):
-                    codes, scales = w1q[a, k]
-                    nc.tensor.matmul_mx(
-                        out=acc[:],
-                        lhsT=codes[:, P * t : P * (t + 1)].bitcast(E4M3),
-                        lhsT_scale=scales[:, P * t : P * (t + 1)],
-                        rhs=v_codes[k][:, cols].bitcast(E5M2),
-                        rhs_scale=v_sc[k][:, cols],
-                        start=(k == 0),
-                        stop=(k == K_PASSES - 1),
-                    )
-                c = clipped[a, h][:, t, :]
-                nc.scalar.copy(c, acc[:])
+                    clipped[a] = ring.tile([P, PACK, S], F32, name="clipped", bufs=2)
+                for h in range(HALVES):
+                    cols = slice(HALF * h, HALF * (h + 1))
+                    acc = psum.tile([P, HALF], F32, name="h_acc", tag="acc", bufs=4)
+                    for k in range(K_PASSES):
+                        codes, scales = w1q[a, k]
+                        nc.tensor.matmul_mx(
+                            out=acc[:],
+                            lhsT=codes[:, P * t : P * (t + 1)].bitcast(E4M3),
+                            lhsT_scale=scales[:, P * t : P * (t + 1)],
+                            rhs=v_codes[k][:, cols].bitcast(E5M2),
+                            rhs_scale=v_sc[k][:, cols],
+                            start=(k == 0),
+                            stop=(k == K_PASSES - 1),
+                        )
+                    nc.scalar.copy(clipped[a][:, t, cols], acc[:])
+                c = clipped[a][:, t, :]
                 nc.vector.tensor_scalar(c, c, hi_t[:, a, t : t + 1], lo_t[:, a, t : t + 1], ALU.min, ALU.max)
 
-        def interleaved_product(dst, slope, c):
+        def interleaved_product(dst, slope_ap, c):
             nc.vector.tensor_tensor(
                 dst.rearrange("p (g i t) -> p g t i", i=LINE, t=PACK),
-                slope.rearrange("p t (g i) -> p g t i", i=LINE),
+                slope_ap.rearrange("p t (g i) -> p g t i", i=LINE),
                 c.rearrange("p t (g i) -> p g t i", i=LINE),
                 ALU.mult,
             )
 
         def finish(a, h):
             grouped = ring.tile([P, HALF * PACK], BF16, name="d_grouped", align_bytes=64)
-            blocks = turned_blocks(a, h)
-            if blocks < BLOCKS:
-                first = P * blocks
-                interleaved_product(
-                    grouped[:, PACK * first : PACK * HALF], neg_x[a, h][:, :, first:HALF], clipped[a, h][:, :, first:HALF]
-                )
-            for b in range(blocks):
+            if (a, h) in DIRECT:
+                interleaved_product(grouped[:], slope[a, h], clipped[a][:, :, HALF * h : HALF * (h + 1)])
+            for b in range(0 if (a, h) in DIRECT else BLOCKS):
                 back = psum.tile([P, PACK, P], F32, name="back", bufs=2)
                 for t in range(PACK):
                     nc.tensor.transpose(back[:, t, :], turned[a, h][:, t, b, :], ident[:])
                 interleaved_product(
-                    grouped[:, PASS * b : PASS * (b + 1)], back[:], clipped[a, h][:, :, P * b : P * (b + 1)]
+                    grouped[:, PASS * b : PASS * (b + 1)], back[:], clipped[a][:, :, HALF * h + P * b : HALF * h + P * (b + 1)]
                 )
             d_codes[a, h] = keep.tile([P, HALF], U32, name=f"d_codes{a}{h}", align_bytes=64)
             d_scales[a, h] = keep.tile([P, HALF], U8, name=f"d_scales{a}{h}", align_bytes=64)
@@ -196,8 +201,11 @@ def tile_list_timeout_plan_gradients_kernel(
 
         def both(a, t):
             load_rows(a, t)
-            pick(a, t, 1)
-            pick(a, t, 0)
+            if all((a, h) in DIRECT for h in range(HALVES)):
+                pick_whole(a, t)
+            else:
+                pick(a, t, 0)
+                pick(a, t, 1)
 
         pick_table(0)
         both(0, 0)
@@ -209,24 +217,33 @@ def tile_list_timeout_plan_gradients_kernel(
         nc.sync.dma_start(lo_t[:], lo.rearrange("(a p t) -> p a t", p=P, t=PACK))
         nc.sync.dma_start(hi_t[:], hi.rearrange("(a p t) -> p a t", p=P, t=PACK))
         both(0, 3)
-        hidden(0, 0)
-        hidden(0, 1)
-        for a in range(1, GROUPS):
-            quantise_w1(a, 0)
-            both(a, 0)
-            quantise_w1(a, 1)
-            finish(a - 1, 0)
-            both(a, 1)
-            finish(a - 1, 1)
-            hidden(a, 0)
-            hidden(a, 1)
-            both(a, 2)
-            both(a, 3)
-        finish(GROUPS - 1, 0)
-        finish(GROUPS - 1, 1)
+        hidden(0, (0, 1))
+        hidden(0, (2, 3))
+        quantise_w1(1, 0)
+        both(1, 0)
+        quantise_w1(1, 1)
+        finish(0, 0)
+        both(1, 1)
+        finish(0, 1)
+        hidden(1, (0, 1))
+        hidden(1, (2, 3))
+        both(1, 2)
+        both(1, 3)
+        quantise_w1(2, 0)
+        both(2, 0)
+        quantise_w1(2, 1)
+        finish(1, 0)
+        both(2, 1)
+        finish(1, 1)
+        hidden(2, (0, 1))
+        hidden(2, (2, 3))
+        both(2, 2)
+        both(2, 3)
+        finish(2, 0)
+        finish(2, 1)
 
-        w2_codes = ring.tile([P, GROUPS, N], I32, name="w2_codes", tag="w1_raw", align_bytes=64)
-        wgo_t = ring.tile([P, S], F32, name="wgo_t", tag="w1_raw", align_bytes=64)
+        w2_codes = ring.tile([P, GROUPS, N], I32, name="w2_codes", tag="loads", bufs=6, align_bytes=64)
+        wgo_t = ring.tile([P, S], F32, name="wgo_t", tag="loads", bufs=6, align_bytes=64)
         nc.sync.dma_start(w2_codes[:], w2_words.rearrange("a p e i -> p a (e i)").bitcast(I32))
         for q in range(QUADS):
             nc.sync.dma_start(

@@ -76,8 +76,6 @@ def tile_list_timeout_plan_gradients_kernel(
         v_codes = [keep.tile([P, S], U32, name=f"v_codes{k}", align_bytes=64) for k in range(K_PASSES)]
         lo_t = keep.tile([P, GROUPS, PACK], F32, name="lo_t")
         hi_t = keep.tile([P, GROUPS, PACK], F32, name="hi_t")
-        w2_sc = keep.tile([P, N], U8, name="w2_sc", align_bytes=64)
-        nc.vector.memset(w2_sc[:].bitcast(I32), 0)
         idx2 = keep.tile([P, S // 16], U16, name="idx2")
 
         w1q = {}
@@ -92,12 +90,12 @@ def tile_list_timeout_plan_gradients_kernel(
             return offsets[:, LIST_COLS * h : LIST_COLS * (h + 1)]
 
         def pick_table(k):
-            words = ring.tile([P, T], I32, name="tab_words", tag="loads", bufs=6, align_bytes=64)
+            words = ring.tile([P, T], I32, name="tab_words", tag="turned", bufs=3, align_bytes=64)
             nc.sync.dma_start(words[:], tab_words[k].rearrange("p t i -> p (t i)").bitcast(I32))
             nc.vector.tensor_copy(v_codes[k][:], words[:].bitcast(U32).indirect(idx[:]))
 
         def quantise_w1(a, k):
-            raw = ring.tile([P, PACK, PASS], F32, name="w1_raw", tag="loads", bufs=6, align_bytes=64)
+            raw = ring.tile([P, PACK, PASS], F32, name="w1_raw", tag="loads", bufs=4, align_bytes=64)
             nc.sync.dma_start(
                 raw[:],
                 w1[PASS * k : PASS * (k + 1), PASS * a : PASS * (a + 1)].rearrange("(p j) c -> p j c", j=PACK),
@@ -115,34 +113,25 @@ def tile_list_timeout_plan_gradients_kernel(
             w1q[a, k] = (codes, scales)
 
         def load_rows(a, t):
-            rows[a, t] = ring.tile([P, T], F32, name="s_rows", tag="loads", bufs=6, align_bytes=64)
+            rows[a, t] = ring.tile([P, T], F32, name="s_rows", tag="loads", bufs=4, align_bytes=64)
             nc.sync.dma_start(
                 rows[a, t][:], sT[PASS * a : PASS * (a + 1), :].rearrange("(p t) c -> p t c", t=PACK)[:, t, :]
             )
 
-        def pick_whole(a, t):
-            if t == 0:
-                both_halves = ring.tile([P, PACK, S], F32, name="slope_whole", bufs=1)
-                for h in range(HALVES):
-                    slope[a, h] = both_halves[:, :, HALF * h : HALF * (h + 1)]
-                slope[a] = both_halves
-            picked = slope[a][:, t, :]
-            nc.vector.tensor_copy(picked, rows[a, t][:].indirect(idx[:]))
-            nc.vector.scalar_tensor_tensor(picked, picked, 1.0, picked, ALU.subtract, ALU.mult)
-
         def pick(a, t, h):
             if (a, h) in DIRECT:
                 if t == 0:
-                    slope[a, h] = ring.tile([P, PACK, HALF], F32, name="slope", bufs=1)[:]
+                    slope[a, h] = ring.tile([P, PACK, HALF], F32, name="slope", bufs=2)[:]
                 picked = slope[a, h][:, t, :]
             else:
                 if t == 0:
-                    turned[a, h] = ring.tile([P, PACK, BLOCKS, P], F32, name="turned", bufs=3)
-                picked = ring.tile([P, HALF], F32, name="neg_x", bufs=6)[:]
+                    turned[a, h] = ring.tile([P, PACK, BLOCKS, P], F32, name="turned", bufs=3, align_bytes=64)
+                picked = ring.tile([P, HALF], F32, name="neg_x", bufs=3)[:]
             nc.vector.tensor_scalar(picked, rows[a, t][:].indirect(list_half(idx, h)), -1.0, 0.0, ALU.mult, ALU.add)
             if (a, h) in DIRECT:
-                if t % 1 == 1 - 1:
-                    run = slope[a, h][:, t + 1 - 1 : t + 1, :].rearrange("p t j -> p (t j)")
+                step = 1 if a == 0 else 4
+                if t % step == step - 1:
+                    run = slope[a, h][:, t + 1 - step : t + 1, :].rearrange("p t j -> p (t j)")
                     nc.vector.scalar_tensor_tensor(run, run, 1.0, run, ALU.add, ALU.mult)
                 return
             squares = ring.tile([P, HALF], F32, name="squares", tag="scratch", bufs=4)
@@ -157,7 +146,8 @@ def tile_list_timeout_plan_gradients_kernel(
         def hidden(a, slices):
             for t in slices:
                 if t == 0:
-                    clipped[a] = ring.tile([P, PACK, S], F32, name="clipped", bufs=2)
+                    last = a == GROUPS - 1
+                    clipped[a] = ring.tile([P, PACK, S], F32, name="clipped", tag="last" if last else "clipped", bufs=1 if last else 2)
                 for h in range(HALVES):
                     cols = slice(HALF * h, HALF * (h + 1))
                     acc = psum.tile([P, HALF], F32, name="h_acc", tag="acc", bufs=4)
@@ -174,7 +164,7 @@ def tile_list_timeout_plan_gradients_kernel(
                         )
                     nc.scalar.copy(clipped[a][:, t, cols], acc[:])
                 c = clipped[a][:, t, :]
-                nc.vector.tensor_scalar(c, c, hi_t[:, a, t : t + 1], lo_t[:, a, t : t + 1], ALU.min, ALU.max)
+                nc.gpsimd.tensor_scalar(c, c, hi_t[:, a, t : t + 1], lo_t[:, a, t : t + 1], ALU.min, ALU.max)
 
         def interleaved_product(dst, slope_ap, c):
             nc.vector.tensor_tensor(
@@ -185,7 +175,10 @@ def tile_list_timeout_plan_gradients_kernel(
             )
 
         def finish(a, h):
-            grouped = ring.tile([P, HALF * PACK], BF16, name="d_grouped", align_bytes=64)
+            if (a, h) in ((2, 0), (1, 1)):
+                grouped = keep.tile([P, HALF * PACK], BF16, name="d_grouped_last", align_bytes=64)
+            else:
+                grouped = ring.tile([P, HALF * PACK], BF16, name="d_grouped", align_bytes=64)
             if (a, h) in DIRECT:
                 interleaved_product(grouped[:], slope[a, h], clipped[a][:, :, HALF * h : HALF * (h + 1)])
             for b in range(0 if (a, h) in DIRECT else BLOCKS):
@@ -201,27 +194,26 @@ def tile_list_timeout_plan_gradients_kernel(
 
         def both(a, t):
             load_rows(a, t)
-            if all((a, h) in DIRECT for h in range(HALVES)):
-                pick_whole(a, t)
-            else:
-                pick(a, t, 0)
-                pick(a, t, 1)
+            pick(a, t, 0)
+            pick(a, t, 1)
 
         pick_table(0)
         both(0, 0)
-        both(0, 1)
-        quantise_w1(0, 0)
         pick_table(1)
-        both(0, 2)
+        quantise_w1(0, 0)
+        both(0, 1)
         quantise_w1(0, 1)
-        nc.sync.dma_start(lo_t[:], lo.rearrange("(a p t) -> p a t", p=P, t=PACK))
-        nc.sync.dma_start(hi_t[:], hi.rearrange("(a p t) -> p a t", p=P, t=PACK))
+        nc.gpsimd.dma_start(lo_t[:], lo.rearrange("(a p t) -> p a t", p=P, t=PACK))
+        nc.gpsimd.dma_start(hi_t[:], hi.rearrange("(a p t) -> p a t", p=P, t=PACK))
+        quantise_w1(1, 0)
+        both(0, 2)
+        quantise_w1(1, 1)
         both(0, 3)
+        quantise_w1(2, 0)
+        both(1, 0)
+        quantise_w1(2, 1)
         hidden(0, (0, 1))
         hidden(0, (2, 3))
-        quantise_w1(1, 0)
-        both(1, 0)
-        quantise_w1(1, 1)
         finish(0, 0)
         both(1, 1)
         finish(0, 1)
@@ -229,24 +221,24 @@ def tile_list_timeout_plan_gradients_kernel(
         hidden(1, (2, 3))
         both(1, 2)
         both(1, 3)
-        quantise_w1(2, 0)
-        both(2, 0)
-        quantise_w1(2, 1)
-        finish(1, 0)
-        both(2, 1)
-        finish(1, 1)
         hidden(2, (0, 1))
         hidden(2, (2, 3))
+        both(2, 0)
+        finish(1, 0)
+        both(2, 1)
         both(2, 2)
         both(2, 3)
         finish(2, 0)
+        finish(1, 1)
         finish(2, 1)
 
-        w2_codes = ring.tile([P, GROUPS, N], I32, name="w2_codes", tag="loads", bufs=6, align_bytes=64)
-        wgo_t = ring.tile([P, S], F32, name="wgo_t", tag="loads", bufs=6, align_bytes=64)
+        w2_codes = ring.tile([P, GROUPS, N], I32, name="w2_codes", tag="loads", bufs=4, align_bytes=64)
+        wgo_t = ring.tile([P, S], F32, name="wgo_t", tag="loads", bufs=4, align_bytes=64)
         nc.sync.dma_start(w2_codes[:], w2_words.rearrange("a p e i -> p a (e i)").bitcast(I32))
+        w2_sc = keep.tile([P, N], U8, name="w2_sc", align_bytes=64)
+        nc.gpsimd.memset(w2_sc[:].bitcast(I32), 0)
         for q in range(QUADS):
-            nc.sync.dma_start(
+            nc.gpsimd.dma_start(
                 w2_sc[QUAD * q : QUAD * q + 4 * GROUPS, :].bitcast(I32),
                 w2_scales[:, 4 * q : 4 * q + 4, :].bitcast(I32),
             )
@@ -255,27 +247,34 @@ def tile_list_timeout_plan_gradients_kernel(
 
         for n in range(HEAD_PAGES, PAGES):
             pages.append(keep.tile([P, T2], F32, name=f"page{n}", tag=f"page{n}", align_bytes=64))
-            nc.gpsimd.memset(pages[n][:], 0.0)
+            for part in range(T2 // HALF):
+                nc.gpsimd.memset(pages[n][:, HALF * part : HALF * (part + 1)], 0.0)
+
+        def place(h, n):
+            acc = psum.tile([P, HALF], F32, name="y_acc", tag="acc", bufs=4)
+            for a in range(GROUPS):
+                nc.tensor.matmul_mx(
+                    out=acc[:],
+                    lhsT=w2_codes[:, a, P * n : P * (n + 1)].bitcast(E4M3),
+                    lhsT_scale=w2_sc[4 * a : P, P * n : P * (n + 1)],
+                    rhs=d_codes[a, h][:].bitcast(E4M3),
+                    rhs_scale=d_scales[a, h][:],
+                    start=(a == 0),
+                    stop=(a == GROUPS - 1),
+                )
+            if (h, n) == (0, 3):
+                y = ring.tile([P, HALF], F32, name="y", tag="last", bufs=1)
+            else:
+                y = ring.tile([P, HALF], F32, name="y", tag="scratch", bufs=4)
+            nc.scalar.activation(y[:], acc[:], ACT.Copy, scale=-1.0)
+            nc.vector.tensor_tensor(
+                pages[n][:].indirect(list_half(idx2, h)), y[:], wgo_t[:, HALF * h : HALF * (h + 1)], ALU.mult
+            )
+            if h == HALVES - 1:
+                for part in range(2):
+                    cols = slice(part * T2 // 2, (part + 1) * T2 // 2)
+                    nc.sync.dma_start(out[P * n : P * (n + 1), cols], pages[n][:, cols])
 
         for h in range(HALVES):
             for n in range(PAGES):
-                acc = psum.tile([P, HALF], F32, name="y_acc", tag="acc", bufs=4)
-                for a in range(GROUPS):
-                    nc.tensor.matmul_mx(
-                        out=acc[:],
-                        lhsT=w2_codes[:, a, P * n : P * (n + 1)].bitcast(E4M3),
-                        lhsT_scale=w2_sc[4 * a : P, P * n : P * (n + 1)],
-                        rhs=d_codes[a, h][:].bitcast(E4M3),
-                        rhs_scale=d_scales[a, h][:],
-                        start=(a == 0),
-                        stop=(a == GROUPS - 1),
-                    )
-                y = ring.tile([P, HALF], F32, name="y", tag="scratch", bufs=4)
-                nc.scalar.activation(y[:], acc[:], ACT.Copy, scale=-1.0)
-                nc.vector.tensor_tensor(
-                    pages[n][:].indirect(list_half(idx2, h)), y[:], wgo_t[:, HALF * h : HALF * (h + 1)], ALU.mult
-                )
-                if h == HALVES - 1:
-                    for part in range(2):
-                        cols = slice(part * T2 // 2, (part + 1) * T2 // 2)
-                        nc.sync.dma_start(out[P * n : P * (n + 1), cols], pages[n][:, cols])
+                place(h, n)

@@ -32,7 +32,7 @@ QUADS = P // QUAD
 TAB_ROW0 = QUAD - 4 * K_PASSES
 PLANE_ROWS = (QUADS - 1) * QUAD + 4
 HALVES = S // HALF
-HEAD_PAGES = 2
+HEAD_PAGES = 1
 DIRECT = ((0, 0), (0, 1), (2, 0))
 
 
@@ -48,7 +48,7 @@ def tile_list_timeout_plan_gradients_kernel(
         idx = keep.tile([P, S // 16], U16, name="idx")
         nc.sync.dma_start(idx[:], offs)
 
-        tab_sc = keep.tile([P, T], U8, name="tab_sc", tag="page2", align_bytes=64)
+        tab_sc = keep.tile([P, T], U8, name="tab_sc", align_bytes=64)
         for q in range(QUADS):
             nc.vector.memset(tab_sc[QUAD * q : QUAD * q + TAB_ROW0, :].bitcast(I32), 0)
             nc.sync.dma_start(
@@ -61,7 +61,7 @@ def tile_list_timeout_plan_gradients_kernel(
         pages = [keep.tile([P, T2], F32, name=f"page{n}") for n in range(HEAD_PAGES)]
         for page in pages:
             nc.vector.memset(page[:].bitcast(I32), 0)
-        picked_sc = keep.tile([P, S], U8, name="picked_sc", tag="page3", align_bytes=64)
+        picked_sc = keep.tile([P, S], U8, name="picked_sc", align_bytes=64)
         nc.vector.tensor_copy(picked_sc[:], tab_sc[:].indirect(idx[:]))
         for k in range(K_PASSES):
             first = TAB_ROW0 + 4 * k
@@ -95,7 +95,7 @@ def tile_list_timeout_plan_gradients_kernel(
             nc.vector.tensor_copy(v_codes[k][:], words[:].bitcast(U32).indirect(idx[:]))
 
         def quantise_w1(a, k):
-            raw = ring.tile([P, PACK, PASS], F32, name="w1_raw", tag="loads", bufs=4, align_bytes=64)
+            raw = ring.tile([P, PACK, PASS], F32, name="w1_raw", tag="loads", bufs=5, align_bytes=64)
             nc.sync.dma_start(
                 raw[:],
                 w1[PASS * k : PASS * (k + 1), PASS * a : PASS * (a + 1)].rearrange("(p j) c -> p j c", j=PACK),
@@ -113,7 +113,7 @@ def tile_list_timeout_plan_gradients_kernel(
             w1q[a, k] = (codes, scales)
 
         def load_rows(a, t):
-            rows[a, t] = ring.tile([P, T], F32, name="s_rows", tag="loads", bufs=4, align_bytes=64)
+            rows[a, t] = ring.tile([P, T], F32, name="s_rows", tag="loads", bufs=5, align_bytes=64)
             nc.sync.dma_start(
                 rows[a, t][:], sT[PASS * a : PASS * (a + 1), :].rearrange("(p t) c -> p t c", t=PACK)[:, t, :]
             )
@@ -121,7 +121,10 @@ def tile_list_timeout_plan_gradients_kernel(
         def pick(a, t, h):
             if (a, h) in DIRECT:
                 if t == 0:
-                    slope[a, h] = ring.tile([P, PACK, HALF], F32, name="slope", bufs=2)[:]
+                    if a == GROUPS - 1:
+                        slope[a, h] = keep.tile([P, PACK, HALF], F32, name="slope", tag="slope_last", align_bytes=64)[:]
+                    else:
+                        slope[a, h] = ring.tile([P, PACK, HALF], F32, name="slope", bufs=2)[:]
                 picked = slope[a, h][:, t, :]
             else:
                 if t == 0:
@@ -164,7 +167,7 @@ def tile_list_timeout_plan_gradients_kernel(
                         )
                     nc.scalar.copy(clipped[a][:, t, cols], acc[:])
                 c = clipped[a][:, t, :]
-                nc.gpsimd.tensor_scalar(c, c, hi_t[:, a, t : t + 1], lo_t[:, a, t : t + 1], ALU.min, ALU.max)
+                nc.vector.tensor_scalar(c, c, hi_t[:, a, t : t + 1], lo_t[:, a, t : t + 1], ALU.min, ALU.max)
 
         def interleaved_product(dst, slope_ap, c):
             nc.vector.tensor_tensor(
@@ -175,8 +178,10 @@ def tile_list_timeout_plan_gradients_kernel(
             )
 
         def finish(a, h):
-            if (a, h) in ((2, 0), (1, 1)):
-                grouped = keep.tile([P, HALF * PACK], BF16, name="d_grouped_last", align_bytes=64)
+            if (a, h) == (GROUPS - 1, 0):
+                grouped = keep.tile([P, HALF * PACK], BF16, name="d_grouped", tag="page1", align_bytes=64)
+            elif (a, h) == (GROUPS - 2, 1):
+                grouped = keep.tile([P, HALF * PACK], BF16, name="d_grouped", tag="slope_last", align_bytes=64)
             else:
                 grouped = ring.tile([P, HALF * PACK], BF16, name="d_grouped", align_bytes=64)
             if (a, h) in DIRECT:
@@ -199,21 +204,19 @@ def tile_list_timeout_plan_gradients_kernel(
 
         pick_table(0)
         both(0, 0)
-        pick_table(1)
-        quantise_w1(0, 0)
         both(0, 1)
-        quantise_w1(0, 1)
-        nc.gpsimd.dma_start(lo_t[:], lo.rearrange("(a p t) -> p a t", p=P, t=PACK))
-        nc.gpsimd.dma_start(hi_t[:], hi.rearrange("(a p t) -> p a t", p=P, t=PACK))
-        quantise_w1(1, 0)
+        quantise_w1(0, 0)
+        pick_table(1)
         both(0, 2)
-        quantise_w1(1, 1)
+        quantise_w1(0, 1)
+        nc.sync.dma_start(lo_t[:], lo.rearrange("(a p t) -> p a t", p=P, t=PACK))
+        nc.sync.dma_start(hi_t[:], hi.rearrange("(a p t) -> p a t", p=P, t=PACK))
         both(0, 3)
-        quantise_w1(2, 0)
-        both(1, 0)
-        quantise_w1(2, 1)
         hidden(0, (0, 1))
         hidden(0, (2, 3))
+        quantise_w1(1, 0)
+        both(1, 0)
+        quantise_w1(1, 1)
         finish(0, 0)
         both(1, 1)
         finish(0, 1)
@@ -221,34 +224,38 @@ def tile_list_timeout_plan_gradients_kernel(
         hidden(1, (2, 3))
         both(1, 2)
         both(1, 3)
-        hidden(2, (0, 1))
-        hidden(2, (2, 3))
+        quantise_w1(2, 0)
         both(2, 0)
+        quantise_w1(2, 1)
         finish(1, 0)
         both(2, 1)
+        hidden(2, (0, 1))
+        hidden(2, (2, 3))
         both(2, 2)
         both(2, 3)
         finish(2, 0)
         finish(1, 1)
         finish(2, 1)
 
-        w2_codes = ring.tile([P, GROUPS, N], I32, name="w2_codes", tag="loads", bufs=4, align_bytes=64)
-        wgo_t = ring.tile([P, S], F32, name="wgo_t", tag="loads", bufs=4, align_bytes=64)
+        w2_codes = ring.tile([P, GROUPS, N], I32, name="w2_codes", tag="loads", bufs=5, align_bytes=64)
+        wgo_t = ring.tile([P, S], F32, name="wgo_t", tag="loads", bufs=5, align_bytes=64)
         nc.sync.dma_start(w2_codes[:], w2_words.rearrange("a p e i -> p a (e i)").bitcast(I32))
         w2_sc = keep.tile([P, N], U8, name="w2_sc", align_bytes=64)
-        nc.gpsimd.memset(w2_sc[:].bitcast(I32), 0)
+        nc.vector.memset(w2_sc[:].bitcast(I32), 0)
         for q in range(QUADS):
-            nc.gpsimd.dma_start(
+            nc.sync.dma_start(
                 w2_sc[QUAD * q : QUAD * q + 4 * GROUPS, :].bitcast(I32),
                 w2_scales[:, 4 * q : 4 * q + 4, :].bitcast(I32),
             )
         nc.sync.dma_start(wgo_t[:], wgo)
         nc.sync.dma_start(idx2[:], offs2)
 
-        for n in range(HEAD_PAGES, PAGES):
+        def clear(n):
             pages.append(keep.tile([P, T2], F32, name=f"page{n}", tag=f"page{n}", align_bytes=64))
             for part in range(T2 // HALF):
                 nc.gpsimd.memset(pages[n][:, HALF * part : HALF * (part + 1)], 0.0)
+
+        clear(1)
 
         def place(h, n):
             acc = psum.tile([P, HALF], F32, name="y_acc", tag="acc", bufs=4)
@@ -262,7 +269,9 @@ def tile_list_timeout_plan_gradients_kernel(
                     start=(a == 0),
                     stop=(a == GROUPS - 1),
                 )
-            if (h, n) == (0, 3):
+            if h == 0 and n + 2 < PAGES:
+                y = keep.tile([P, HALF], F32, name="y", tag=f"page{n + 2}", align_bytes=64)
+            elif (h, n) == (0, 3):
                 y = ring.tile([P, HALF], F32, name="y", tag="last", bufs=1)
             else:
                 y = ring.tile([P, HALF], F32, name="y", tag="scratch", bufs=4)
@@ -278,3 +287,5 @@ def tile_list_timeout_plan_gradients_kernel(
         for h in range(HALVES):
             for n in range(PAGES):
                 place(h, n)
+                if h == 0 and n + 2 < PAGES:
+                    clear(n + 2)

@@ -29,10 +29,9 @@ BLOCKS = HALF // P
 LINE = 2
 QUAD = 32
 QUADS = P // QUAD
-TAB_ROW0 = QUAD - 4 * K_PASSES
-PLANE_ROWS = (QUADS - 1) * QUAD + 4
+TAB_ROW0 = P - 4 * QUADS * K_PASSES
 HALVES = S // HALF
-HEAD_PAGES = 1
+HEAD_PAGES = 3
 DIRECT = ((0, 0), (0, 1), (2, 0))
 
 
@@ -49,26 +48,22 @@ def tile_list_timeout_plan_gradients_kernel(
         nc.sync.dma_start(idx[:], offs)
 
         tab_sc = keep.tile([P, T], U8, name="tab_sc", align_bytes=64)
-        for q in range(QUADS):
-            nc.vector.memset(tab_sc[QUAD * q : QUAD * q + TAB_ROW0, :].bitcast(I32), 0)
-            nc.sync.dma_start(
-                tab_sc[QUAD * q + TAB_ROW0 : QUAD * (q + 1), :].bitcast(I32),
-                tab_scales[:, 4 * q : 4 * q + 4, :].bitcast(I32),
-            )
+        nc.vector.memset(tab_sc[0:TAB_ROW0, :].bitcast(I32), 0)
+        nc.sync.dma_start(tab_sc[TAB_ROW0:P, :].bitcast(I32), tab_scales.rearrange("a q t -> (a q) t").bitcast(I32))
         v_sc = [keep.tile([P, S], U8, name=f"v_sc{k}", align_bytes=64) for k in range(K_PASSES)]
         for k in range(K_PASSES):
-            nc.vector.memset(v_sc[k][(QUADS - 1) * QUAD : P, :].bitcast(I32), 0)
+            nc.vector.memset(v_sc[k][:].bitcast(I32), 0)
         pages = [keep.tile([P, T2], F32, name=f"page{n}") for n in range(HEAD_PAGES)]
         for page in pages:
             nc.vector.memset(page[:].bitcast(I32), 0)
         picked_sc = keep.tile([P, S], U8, name="picked_sc", align_bytes=64)
         nc.vector.tensor_copy(picked_sc[:], tab_sc[:].indirect(idx[:]))
         for k in range(K_PASSES):
-            first = TAB_ROW0 + 4 * k
-            nc.gpsimd.dma_start(
-                v_sc[k][0:PLANE_ROWS, :].bitcast(I32),
-                picked_sc[first : first + PLANE_ROWS, :].bitcast(I32),
-            )
+            for q in range(QUADS):
+                first = TAB_ROW0 + 4 * (QUADS * k + q)
+                nc.scalar.dma_start(
+                    v_sc[k][QUAD * q : QUAD * q + 4, :].bitcast(I32), picked_sc[first : first + 4, :].bitcast(I32)
+                )
 
         ident = keep.tile([P, P], F32, name="ident")
         make_identity(nc, ident[:])
@@ -179,7 +174,7 @@ def tile_list_timeout_plan_gradients_kernel(
 
         def finish(a, h):
             if (a, h) == (GROUPS - 1, 0):
-                grouped = keep.tile([P, HALF * PACK], BF16, name="d_grouped", tag="page1", align_bytes=64)
+                grouped = keep.tile([P, HALF * PACK], BF16, name="d_grouped", tag="page3", align_bytes=64)
             elif (a, h) == (GROUPS - 2, 1):
                 grouped = keep.tile([P, HALF * PACK], BF16, name="d_grouped", tag="slope_last", align_bytes=64)
             else:
@@ -250,12 +245,9 @@ def tile_list_timeout_plan_gradients_kernel(
         nc.sync.dma_start(wgo_t[:], wgo)
         nc.sync.dma_start(idx2[:], offs2)
 
-        def clear(n):
-            pages.append(keep.tile([P, T2], F32, name=f"page{n}", tag=f"page{n}", align_bytes=64))
-            for part in range(T2 // HALF):
-                nc.gpsimd.memset(pages[n][:, HALF * part : HALF * (part + 1)], 0.0)
 
-        clear(1)
+        pages.append(keep.tile([P, T2], F32, name="page3", align_bytes=64))
+        nc.vector.memset(pages[3][:].bitcast(I32), 0)
 
         def place(h, n):
             acc = psum.tile([P, HALF], F32, name="y_acc", tag="acc", bufs=4)
@@ -269,9 +261,7 @@ def tile_list_timeout_plan_gradients_kernel(
                     start=(a == 0),
                     stop=(a == GROUPS - 1),
                 )
-            if h == 0 and n + 2 < PAGES:
-                y = keep.tile([P, HALF], F32, name="y", tag=f"page{n + 2}", align_bytes=64)
-            elif (h, n) == (0, 3):
+            if (h, n) == (0, 3):
                 y = ring.tile([P, HALF], F32, name="y", tag="last", bufs=1)
             else:
                 y = ring.tile([P, HALF], F32, name="y", tag="scratch", bufs=4)
@@ -287,5 +277,3 @@ def tile_list_timeout_plan_gradients_kernel(
         for h in range(HALVES):
             for n in range(PAGES):
                 place(h, n)
-                if h == 0 and n + 2 < PAGES:
-                    clear(n + 2)

@@ -31,7 +31,7 @@ QUAD = 32
 QUADS = P // QUAD
 TAB_ROW0 = P - 4 * QUADS * K_PASSES
 HALVES = S // HALF
-HEAD_PAGES = 3
+HEAD_PAGES = 2
 DIRECT = ((0, 0), (0, 1), (2, 0))
 
 
@@ -124,7 +124,7 @@ def tile_list_timeout_plan_gradients_kernel(
             else:
                 if t == 0:
                     turned[a, h] = ring.tile([P, PACK, BLOCKS, P], F32, name="turned", bufs=3, align_bytes=64)
-                picked = ring.tile([P, HALF], F32, name="neg_x", bufs=3)[:]
+                picked = ring.tile([P, HALF], F32, name="neg_x", bufs=5)[:]
             nc.vector.tensor_scalar(picked, rows[a, t][:].indirect(list_half(idx, h)), -1.0, 0.0, ALU.mult, ALU.add)
             if (a, h) in DIRECT:
                 step = 1 if a == 0 else 4
@@ -148,7 +148,7 @@ def tile_list_timeout_plan_gradients_kernel(
                     clipped[a] = ring.tile([P, PACK, S], F32, name="clipped", tag="last" if last else "clipped", bufs=1 if last else 2)
                 for h in range(HALVES):
                     cols = slice(HALF * h, HALF * (h + 1))
-                    acc = psum.tile([P, HALF], F32, name="h_acc", tag="acc", bufs=4)
+                    acc = psum.tile([P, HALF], F32, name="h_acc", tag="acc", bufs=3)
                     for k in range(K_PASSES):
                         codes, scales = w1q[a, k]
                         nc.tensor.matmul_mx(
@@ -162,7 +162,7 @@ def tile_list_timeout_plan_gradients_kernel(
                         )
                     nc.scalar.copy(clipped[a][:, t, cols], acc[:])
                 c = clipped[a][:, t, :]
-                nc.vector.tensor_scalar(c, c, hi_t[:, a, t : t + 1], lo_t[:, a, t : t + 1], ALU.min, ALU.max)
+                nc.gpsimd.tensor_scalar(c, c, hi_t[:, a, t : t + 1], lo_t[:, a, t : t + 1], ALU.min, ALU.max)
 
         def interleaved_product(dst, slope_ap, c):
             nc.vector.tensor_tensor(
@@ -174,7 +174,7 @@ def tile_list_timeout_plan_gradients_kernel(
 
         def finish(a, h):
             if (a, h) == (GROUPS - 1, 0):
-                grouped = keep.tile([P, HALF * PACK], BF16, name="d_grouped", tag="page3", align_bytes=64)
+                grouped = keep.tile([P, HALF * PACK], BF16, name="d_grouped", tag="late_page", align_bytes=64)
             elif (a, h) == (GROUPS - 2, 1):
                 grouped = keep.tile([P, HALF * PACK], BF16, name="d_grouped", tag="slope_last", align_bytes=64)
             else:
@@ -182,7 +182,7 @@ def tile_list_timeout_plan_gradients_kernel(
             if (a, h) in DIRECT:
                 interleaved_product(grouped[:], slope[a, h], clipped[a][:, :, HALF * h : HALF * (h + 1)])
             for b in range(0 if (a, h) in DIRECT else BLOCKS):
-                back = psum.tile([P, PACK, P], F32, name="back", bufs=2)
+                back = psum.tile([P, PACK, P], F32, name="back", bufs=3)
                 for t in range(PACK):
                     nc.tensor.transpose(back[:, t, :], turned[a, h][:, t, b, :], ident[:])
                 interleaved_product(
@@ -207,25 +207,25 @@ def tile_list_timeout_plan_gradients_kernel(
         nc.sync.dma_start(lo_t[:], lo.rearrange("(a p t) -> p a t", p=P, t=PACK))
         nc.sync.dma_start(hi_t[:], hi.rearrange("(a p t) -> p a t", p=P, t=PACK))
         both(0, 3)
+        quantise_w1(1, 0)
         hidden(0, (0, 1))
         hidden(0, (2, 3))
-        quantise_w1(1, 0)
         both(1, 0)
         quantise_w1(1, 1)
         finish(0, 0)
+        quantise_w1(2, 0)
         both(1, 1)
+        quantise_w1(2, 1)
         finish(0, 1)
         hidden(1, (0, 1))
         hidden(1, (2, 3))
         both(1, 2)
-        both(1, 3)
-        quantise_w1(2, 0)
-        both(2, 0)
-        quantise_w1(2, 1)
-        finish(1, 0)
-        both(2, 1)
         hidden(2, (0, 1))
         hidden(2, (2, 3))
+        both(1, 3)
+        both(2, 0)
+        finish(1, 0)
+        both(2, 1)
         both(2, 2)
         both(2, 3)
         finish(2, 0)
@@ -246,34 +246,43 @@ def tile_list_timeout_plan_gradients_kernel(
         nc.sync.dma_start(idx2[:], offs2)
 
 
-        pages.append(keep.tile([P, T2], F32, name="page3", align_bytes=64))
-        nc.vector.memset(pages[3][:].bitcast(I32), 0)
+        pages.append(keep.tile([P, T2], F32, name="late_page", align_bytes=64))
+        nc.vector.memset(pages[-1][:].bitcast(I32), 0)
 
-        def place(h, n):
-            acc = psum.tile([P, HALF], F32, name="y_acc", tag="acc", bufs=4)
-            for a in range(GROUPS):
-                nc.tensor.matmul_mx(
-                    out=acc[:],
-                    lhsT=w2_codes[:, a, P * n : P * (n + 1)].bitcast(E4M3),
-                    lhsT_scale=w2_sc[4 * a : P, P * n : P * (n + 1)],
-                    rhs=d_codes[a, h][:].bitcast(E4M3),
-                    rhs_scale=d_scales[a, h][:],
-                    start=(a == 0),
-                    stop=(a == GROUPS - 1),
-                )
-            if (h, n) == (0, 3):
-                y = ring.tile([P, HALF], F32, name="y", tag="last", bufs=1)
+        def place(halves, n):
+            width = HALF * len(halves)
+            if (halves, n) == ((0,), 2):
+                y = ring.tile([P, width], F32, name="y", tag="last", bufs=1)
             else:
-                y = ring.tile([P, HALF], F32, name="y", tag="scratch", bufs=4)
-            nc.scalar.activation(y[:], acc[:], ACT.Copy, scale=-1.0)
+                y = ring.tile([P, width], F32, name="y", tag="turned", bufs=3, align_bytes=64)
+            for i, h in enumerate(halves):
+                acc = psum.tile([P, HALF], F32, name="y_acc", tag="acc", bufs=3)
+                for a in range(GROUPS):
+                    nc.tensor.matmul_mx(
+                        out=acc[:],
+                        lhsT=w2_codes[:, a, P * n : P * (n + 1)].bitcast(E4M3),
+                        lhsT_scale=w2_sc[4 * a : P, P * n : P * (n + 1)],
+                        rhs=d_codes[a, h][:].bitcast(E4M3),
+                        rhs_scale=d_scales[a, h][:],
+                        start=(a == 0),
+                        stop=(a == GROUPS - 1),
+                    )
+                nc.scalar.activation(y[:, HALF * i : HALF * (i + 1)], acc[:], ACT.Copy, scale=-1.0)
+            page = pages[n % len(pages)]
+            first = halves[0]
             nc.vector.tensor_tensor(
-                pages[n][:].indirect(list_half(idx2, h)), y[:], wgo_t[:, HALF * h : HALF * (h + 1)], ALU.mult
+                page[:].indirect(idx2[:, LIST_COLS * first : LIST_COLS * (first + len(halves))]),
+                y[:],
+                wgo_t[:, HALF * first : HALF * first + width],
+                ALU.mult,
             )
-            if h == HALVES - 1:
+            if halves[-1] == HALVES - 1:
                 for part in range(2):
                     cols = slice(part * T2 // 2, (part + 1) * T2 // 2)
-                    nc.sync.dma_start(out[P * n : P * (n + 1), cols], pages[n][:, cols])
+                    nc.sync.dma_start(out[P * n : P * (n + 1), cols], page[:, cols])
 
         for h in range(HALVES):
-            for n in range(PAGES):
-                place(h, n)
+            for n in range(len(pages)):
+                place((h,), n)
+        for n in range(len(pages), PAGES):
+            place((0, 1), n)

@@ -21,18 +21,24 @@ P = 128
 PACK = 4
 PASS = P * PACK
 HALF = 512
+HALVES = S // HALF
 K_PASSES = K // PASS
 GROUPS = H // PASS
+LAST = GROUPS - 1
 LIST_COLS = HALF // 16
 PAGES = N // P
 BLOCKS = HALF // P
-LINE = 2
+PAIR = 2
 QUAD = 32
 QUADS = P // QUAD
-TAB_ROW0 = P - 4 * QUADS * K_PASSES
-HALVES = S // HALF
+QUAD_ROWS = 4
+TAB_ROW0 = P - QUAD_ROWS * QUADS * K_PASSES
+DIRECT = ((0, 0), (0, 1), (LAST, 0))
 HEAD_PAGES = 2
-DIRECT = ((0, 0), (0, 1), (2, 0))
+LOAD_BUFS = 5
+TURN_BUFS = 3
+PICK_BUFS = 5
+SUM_BANKS, THERE_BANKS, BACK_BANKS = 3, 2, 3
 
 
 def tile_list_timeout_plan_gradients_kernel(
@@ -60,9 +66,10 @@ def tile_list_timeout_plan_gradients_kernel(
         nc.vector.tensor_copy(picked_sc[:], tab_sc[:].indirect(idx[:]))
         for k in range(K_PASSES):
             for q in range(QUADS):
-                first = TAB_ROW0 + 4 * (QUADS * k + q)
+                first = TAB_ROW0 + QUAD_ROWS * (QUADS * k + q)
                 nc.scalar.dma_start(
-                    v_sc[k][QUAD * q : QUAD * q + 4, :].bitcast(I32), picked_sc[first : first + 4, :].bitcast(I32)
+                    v_sc[k][QUAD * q : QUAD * q + QUAD_ROWS, :].bitcast(I32),
+                    picked_sc[first : first + QUAD_ROWS, :].bitcast(I32),
                 )
 
         ident = keep.tile([P, P], F32, name="ident")
@@ -74,81 +81,84 @@ def tile_list_timeout_plan_gradients_kernel(
         idx2 = keep.tile([P, S // 16], U16, name="idx2")
 
         w1q = {}
-        rows = {}
         slope = {}
         turned = {}
         clipped = {}
         d_codes = {}
         d_scales = {}
 
-        def list_half(offsets, h):
-            return offsets[:, LIST_COLS * h : LIST_COLS * (h + 1)]
-
         def pick_table(k):
-            words = ring.tile([P, T], I32, name="tab_words", tag="turned", bufs=3, align_bytes=64)
+            words = ring.tile([P, T], I32, name="tab_words", tag="turned", bufs=TURN_BUFS, align_bytes=64)
             nc.sync.dma_start(words[:], tab_words[k].rearrange("p t i -> p (t i)").bitcast(I32))
             nc.vector.tensor_copy(v_codes[k][:], words[:].bitcast(U32).indirect(idx[:]))
 
         def quantise_w1(a, k):
-            raw = ring.tile([P, PACK, PASS], F32, name="w1_raw", tag="loads", bufs=5, align_bytes=64)
+            raw = ring.tile([P, PACK, PASS], F32, name="w1_raw", tag="loads", bufs=LOAD_BUFS, align_bytes=64)
             nc.sync.dma_start(
                 raw[:],
                 w1[PASS * k : PASS * (k + 1), PASS * a : PASS * (a + 1)].rearrange("(p j) c -> p j c", j=PACK),
             )
             grouped = ring.tile([P, PASS * PACK], BF16, name="w1_grouped", align_bytes=64)
-            sorted_out = grouped[:].rearrange("p (t m j) -> p m j t", t=PACK, j=PACK)
-            sorted_in = raw[:].rearrange("p j (m t) -> p m j t", t=PACK)
-            if True:
-                nc.scalar.copy(sorted_out, sorted_in)
-            else:
-                nc.gpsimd.tensor_scalar(sorted_out, sorted_in, 1.0, 0.0, ALU.mult, ALU.add)
+            nc.scalar.copy(
+                grouped[:].rearrange("p (t m j) -> p m j t", t=PACK, j=PACK),
+                raw[:].rearrange("p j (m t) -> p m j t", t=PACK),
+            )
             codes = ring.tile([P, PASS], U32, name="w1_codes", bufs=4, align_bytes=64)
             scales = ring.tile([P, PASS], U8, name="w1_scales", bufs=4, align_bytes=64)
             nc.vector.quantize_mx(out=codes[:].bitcast(E4M3), scales=scales[:], in_=grouped[:])
             w1q[a, k] = (codes, scales)
 
-        def load_rows(a, t):
-            rows[a, t] = ring.tile([P, T], F32, name="s_rows", tag="loads", bufs=5, align_bytes=64)
-            nc.sync.dma_start(
-                rows[a, t][:], sT[PASS * a : PASS * (a + 1), :].rearrange("(p t) c -> p t c", t=PACK)[:, t, :]
-            )
+        def gather_negated(dst, rows, h):
+            offsets = idx[:, LIST_COLS * h : LIST_COLS * (h + 1)]
+            nc.vector.tensor_scalar(dst, rows[:].indirect(offsets), -1.0, 0.0, ALU.mult, ALU.add)
 
-        def pick(a, t, h):
-            if (a, h) in DIRECT:
-                if t == 0:
-                    if a == GROUPS - 1:
-                        slope[a, h] = keep.tile([P, PACK, HALF], F32, name="slope", tag="slope_last", align_bytes=64)[:]
-                    else:
-                        slope[a, h] = ring.tile([P, PACK, HALF], F32, name="slope", bufs=2)[:]
-                picked = slope[a, h][:, t, :]
-            else:
-                if t == 0:
-                    turned[a, h] = ring.tile([P, PACK, BLOCKS, P], F32, name="turned", bufs=3, align_bytes=64)
-                picked = ring.tile([P, HALF], F32, name="neg_x", bufs=5)[:]
-            nc.vector.tensor_scalar(picked, rows[a, t][:].indirect(list_half(idx, h)), -1.0, 0.0, ALU.mult, ALU.add)
-            if (a, h) in DIRECT:
-                step = 1 if a == 0 else 4
-                if t % step == step - 1:
-                    run = slope[a, h][:, t + 1 - step : t + 1, :].rearrange("p t j -> p (t j)")
-                    nc.vector.scalar_tensor_tensor(run, run, 1.0, run, ALU.add, ALU.mult)
-                return
-            squares = ring.tile([P, HALF], F32, name="squares", tag="scratch", bufs=4)
-            nc.scalar.activation(squares[:], picked, ACT.Square)
-            there = psum.tile([P, BLOCKS, P], F32, name="there", bufs=2)
+        def slope_on_vector(a, t, h, rows):
+            if t == 0 and a == LAST:
+                slope[a, h] = keep.tile([P, PACK, HALF], F32, name="slope", tag="slope_last", align_bytes=64)
+            elif t == 0:
+                slope[a, h] = ring.tile([P, PACK, HALF], F32, name="slope")
+            picked = slope[a, h][:, t, :]
+            gather_negated(picked, rows, h)
+            if a < LAST:
+                nc.vector.scalar_tensor_tensor(picked, picked, 1.0, picked, ALU.add, ALU.mult)
+            elif t == PACK - 1:
+                whole = slope[a, h][:].rearrange("p t j -> p (t j)")
+                nc.vector.scalar_tensor_tensor(whole, whole, 1.0, whole, ALU.add, ALU.mult)
+
+        def slope_by_transposes(a, t, h, rows):
+            if t == 0:
+                turned[a, h] = ring.tile([P, PACK, BLOCKS, P], F32, name="turned", bufs=TURN_BUFS, align_bytes=64)
+            picked = ring.tile([P, HALF], F32, name="neg_x", bufs=PICK_BUFS)
+            gather_negated(picked[:], rows, h)
+            squares = ring.tile([P, HALF], F32, name="squares", bufs=4)
+            nc.scalar.activation(squares[:], picked[:], ACT.Square)
+            there = psum.tile([P, BLOCKS, P], F32, name="there", bufs=THERE_BANKS)
             for b in range(BLOCKS):
                 block = slice(P * b, P * (b + 1))
                 nc.tensor.matmul(there[:, b, :], squares[:, block], ident[:], start=True, stop=False, is_transpose=True)
                 nc.tensor.matmul(there[:, b, :], picked[:, block], ident[:], start=False, stop=True, is_transpose=True)
             nc.scalar.copy(turned[a, h][:, t, :, :], there[:])
 
-        def hidden(a, slices):
-            for t in slices:
-                if t == 0:
-                    last = a == GROUPS - 1
-                    clipped[a] = ring.tile([P, PACK, S], F32, name="clipped", tag="last" if last else "clipped", bufs=1 if last else 2)
+        def saved_slice(a, t):
+            rows = ring.tile([P, T], F32, name="s_rows", tag="loads", bufs=LOAD_BUFS, align_bytes=64)
+            nc.sync.dma_start(
+                rows[:], sT[PASS * a : PASS * (a + 1), :].rearrange("(p t) c -> p t c", t=PACK)[:, t, :]
+            )
+            for h in range(HALVES):
+                if (a, h) in DIRECT:
+                    slope_on_vector(a, t, h, rows)
+                else:
+                    slope_by_transposes(a, t, h, rows)
+
+        def hidden(a):
+            if a == LAST:
+                clipped[a] = ring.tile([P, PACK, S], F32, name="clipped", tag="clipped_last", bufs=1)
+            else:
+                clipped[a] = ring.tile([P, PACK, S], F32, name="clipped")
+            for t in range(PACK):
                 for h in range(HALVES):
                     cols = slice(HALF * h, HALF * (h + 1))
-                    acc = psum.tile([P, HALF], F32, name="h_acc", tag="acc", bufs=3)
+                    acc = psum.tile([P, HALF], F32, name="h_acc", tag="acc", bufs=SUM_BANKS)
                     for k in range(K_PASSES):
                         codes, scales = w1q[a, k]
                         nc.tensor.matmul_mx(
@@ -162,110 +172,101 @@ def tile_list_timeout_plan_gradients_kernel(
                         )
                     nc.scalar.copy(clipped[a][:, t, cols], acc[:])
                 c = clipped[a][:, t, :]
-                nc.gpsimd.tensor_scalar(c, c, hi_t[:, a, t : t + 1], lo_t[:, a, t : t + 1], ALU.min, ALU.max)
+                clipper = nc.vector if a == 0 else nc.gpsimd
+                clipper.tensor_scalar(c, c, hi_t[:, a, t : t + 1], lo_t[:, a, t : t + 1], ALU.min, ALU.max)
 
-        def interleaved_product(dst, slope_ap, c):
+        def interleaved_product(dst, factor, c):
             nc.vector.tensor_tensor(
-                dst.rearrange("p (g i t) -> p g t i", i=LINE, t=PACK),
-                slope_ap.rearrange("p t (g i) -> p g t i", i=LINE),
-                c.rearrange("p t (g i) -> p g t i", i=LINE),
+                dst.rearrange("p (g i t) -> p g t i", i=PAIR, t=PACK),
+                factor.rearrange("p t (g i) -> p g t i", i=PAIR),
+                c.rearrange("p t (g i) -> p g t i", i=PAIR),
                 ALU.mult,
             )
 
         def finish(a, h):
-            if (a, h) == (GROUPS - 1, 0):
+            if (a, h) == (LAST, 0):
                 grouped = keep.tile([P, HALF * PACK], BF16, name="d_grouped", tag="late_page", align_bytes=64)
-            elif (a, h) == (GROUPS - 2, 1):
+            elif (a, h) == (LAST - 1, 1):
                 grouped = keep.tile([P, HALF * PACK], BF16, name="d_grouped", tag="slope_last", align_bytes=64)
             else:
                 grouped = ring.tile([P, HALF * PACK], BF16, name="d_grouped", align_bytes=64)
+            c = clipped[a][:, :, HALF * h : HALF * (h + 1)]
             if (a, h) in DIRECT:
-                interleaved_product(grouped[:], slope[a, h], clipped[a][:, :, HALF * h : HALF * (h + 1)])
-            for b in range(0 if (a, h) in DIRECT else BLOCKS):
-                back = psum.tile([P, PACK, P], F32, name="back", bufs=3)
-                for t in range(PACK):
-                    nc.tensor.transpose(back[:, t, :], turned[a, h][:, t, b, :], ident[:])
-                interleaved_product(
-                    grouped[:, PASS * b : PASS * (b + 1)], back[:], clipped[a][:, :, HALF * h + P * b : HALF * h + P * (b + 1)]
-                )
+                interleaved_product(grouped[:], slope[a, h][:], c)
+            else:
+                for b in range(BLOCKS):
+                    back = psum.tile([P, PACK, P], F32, name="back", bufs=BACK_BANKS)
+                    for t in range(PACK):
+                        nc.tensor.transpose(back[:, t, :], turned[a, h][:, t, b, :], ident[:])
+                    interleaved_product(grouped[:, PASS * b : PASS * (b + 1)], back[:], c[:, :, P * b : P * (b + 1)])
             d_codes[a, h] = keep.tile([P, HALF], U32, name=f"d_codes{a}{h}", align_bytes=64)
             d_scales[a, h] = keep.tile([P, HALF], U8, name=f"d_scales{a}{h}", align_bytes=64)
             nc.vector.quantize_mx(out=d_codes[a, h][:].bitcast(E4M3), scales=d_scales[a, h][:], in_=grouped[:])
 
-        def both(a, t):
-            load_rows(a, t)
-            pick(a, t, 0)
-            pick(a, t, 1)
-
         pick_table(0)
-        both(0, 0)
-        both(0, 1)
+        saved_slice(0, 0)
+        saved_slice(0, 1)
         quantise_w1(0, 0)
         pick_table(1)
-        both(0, 2)
+        saved_slice(0, 2)
         quantise_w1(0, 1)
         nc.sync.dma_start(lo_t[:], lo.rearrange("(a p t) -> p a t", p=P, t=PACK))
         nc.sync.dma_start(hi_t[:], hi.rearrange("(a p t) -> p a t", p=P, t=PACK))
-        both(0, 3)
+        saved_slice(0, 3)
         quantise_w1(1, 0)
-        hidden(0, (0, 1))
-        hidden(0, (2, 3))
-        both(1, 0)
+        hidden(0)
+        saved_slice(1, 0)
         quantise_w1(1, 1)
         finish(0, 0)
         quantise_w1(2, 0)
-        both(1, 1)
+        saved_slice(1, 1)
         quantise_w1(2, 1)
         finish(0, 1)
-        hidden(1, (0, 1))
-        hidden(1, (2, 3))
-        both(1, 2)
-        hidden(2, (0, 1))
-        hidden(2, (2, 3))
-        both(1, 3)
-        both(2, 0)
+        hidden(1)
+        saved_slice(1, 2)
+        hidden(2)
+        saved_slice(1, 3)
+        saved_slice(2, 0)
         finish(1, 0)
-        both(2, 1)
-        both(2, 2)
-        both(2, 3)
+        for t in range(1, PACK):
+            saved_slice(2, t)
         finish(2, 0)
         finish(1, 1)
         finish(2, 1)
 
-        w2_codes = ring.tile([P, GROUPS, N], I32, name="w2_codes", tag="loads", bufs=5, align_bytes=64)
-        wgo_t = ring.tile([P, S], F32, name="wgo_t", tag="loads", bufs=5, align_bytes=64)
+        w2_codes = ring.tile([P, GROUPS, N], I32, name="w2_codes", tag="loads", bufs=LOAD_BUFS, align_bytes=64)
+        wgo_t = ring.tile([P, S], F32, name="wgo_t", tag="loads", bufs=LOAD_BUFS, align_bytes=64)
         nc.sync.dma_start(w2_codes[:], w2_words.rearrange("a p e i -> p a (e i)").bitcast(I32))
         w2_sc = keep.tile([P, N], U8, name="w2_sc", align_bytes=64)
         nc.vector.memset(w2_sc[:].bitcast(I32), 0)
         for q in range(QUADS):
             nc.sync.dma_start(
-                w2_sc[QUAD * q : QUAD * q + 4 * GROUPS, :].bitcast(I32),
-                w2_scales[:, 4 * q : 4 * q + 4, :].bitcast(I32),
+                w2_sc[QUAD * q : QUAD * q + QUAD_ROWS * GROUPS, :].bitcast(I32),
+                w2_scales[:, QUAD_ROWS * q : QUAD_ROWS * (q + 1), :].bitcast(I32),
             )
         nc.sync.dma_start(wgo_t[:], wgo)
         nc.sync.dma_start(idx2[:], offs2)
-
 
         pages.append(keep.tile([P, T2], F32, name="late_page", align_bytes=64))
         nc.vector.memset(pages[-1][:].bitcast(I32), 0)
 
         def place(halves, n):
             width = HALF * len(halves)
-            if (halves, n) == ((0,), 2):
-                y = ring.tile([P, width], F32, name="y", tag="last", bufs=1)
+            if (halves, n) == ((0,), len(pages) - 1):
+                y = ring.tile([P, width], F32, name="y", tag="clipped_last", bufs=1)
             else:
-                y = ring.tile([P, width], F32, name="y", tag="turned", bufs=3, align_bytes=64)
+                y = ring.tile([P, width], F32, name="y", tag="turned", bufs=TURN_BUFS, align_bytes=64)
             for i, h in enumerate(halves):
-                acc = psum.tile([P, HALF], F32, name="y_acc", tag="acc", bufs=3)
+                acc = psum.tile([P, HALF], F32, name="y_acc", tag="acc", bufs=SUM_BANKS)
                 for a in range(GROUPS):
                     nc.tensor.matmul_mx(
                         out=acc[:],
                         lhsT=w2_codes[:, a, P * n : P * (n + 1)].bitcast(E4M3),
-                        lhsT_scale=w2_sc[4 * a : P, P * n : P * (n + 1)],
+                        lhsT_scale=w2_sc[QUAD_ROWS * a : P, P * n : P * (n + 1)],
                         rhs=d_codes[a, h][:].bitcast(E4M3),
                         rhs_scale=d_scales[a, h][:],
                         start=(a == 0),
-                        stop=(a == GROUPS - 1),
+                        stop=(a == LAST),
                     )
                 nc.scalar.activation(y[:, HALF * i : HALF * (i + 1)], acc[:], ACT.Copy, scale=-1.0)
             page = pages[n % len(pages)]
@@ -277,12 +278,12 @@ def tile_list_timeout_plan_gradients_kernel(
                 ALU.mult,
             )
             if halves[-1] == HALVES - 1:
-                for part in range(2):
-                    cols = slice(part * T2 // 2, (part + 1) * T2 // 2)
+                for side in range(2):
+                    cols = slice(side * T2 // 2, (side + 1) * T2 // 2)
                     nc.sync.dma_start(out[P * n : P * (n + 1), cols], page[:, cols])
 
         for h in range(HALVES):
             for n in range(len(pages)):
                 place((h,), n)
         for n in range(len(pages), PAGES):
-            place((0, 1), n)
+            place(tuple(range(HALVES)), n)

@@ -35,10 +35,12 @@ QUAD_ROWS = 4
 TAB_ROW0 = P - QUAD_ROWS * QUADS * K_PASSES
 DIRECT = ((0, 0), (0, 1), (LAST, 0))
 HEAD_PAGES = 2
-LOAD_BUFS = 5
-TURN_BUFS = 3
-PICK_BUFS = 5
-SUM_BANKS, THERE_BANKS, BACK_BANKS = 3, 2, 3
+LOAD_BUFS = 6
+WORK_BUFS = 25
+CODE_BUFS = GROUPS * HALVES + 2
+BANKS = 8
+POOL_COLS = 128
+CLIP_COLS = 1024
 
 
 def tile_list_timeout_plan_gradients_kernel(
@@ -48,132 +50,178 @@ def tile_list_timeout_plan_gradients_kernel(
     with ExitStack() as ctx:
         keep = ctx.enter_context(tc.tile_pool(name="keep", bufs=1))
         ring = ctx.enter_context(tc.tile_pool(name="ring", bufs=2))
-        psum = ctx.enter_context(tc.psum_pool(name="psum", bufs=2))
+        psum = ctx.enter_context(tc.psum_pool(name="psum", bufs=BANKS))
+
+        def work_tile(shape, dtype, name):
+            return ring.tile(shape, dtype, name=name, tag="work", bufs=WORK_BUFS, align_bytes=64)
+
+        def load_tile(shape, dtype, name):
+            return ring.tile(shape, dtype, name=name, tag="loads", bufs=LOAD_BUFS, align_bytes=64)
+
+        def code_tiles(name):
+            codes = work_tile([P, PASS], U32, name)
+            scales = ring.tile([P, PASS], U8, name=name + "_scales", tag="scales", bufs=CODE_BUFS, align_bytes=64)
+            return codes, scales
+
+        def bank(shape, name):
+            return psum.tile(shape, F32, name=name, tag="bank")
 
         idx = keep.tile([P, S // 16], U16, name="idx")
         nc.sync.dma_start(idx[:], offs)
+        idx2 = keep.tile([P, S // 16], U16, name="idx2")
+        nc.sync.dma_start(idx2[:], offs2)
 
         tab_sc = keep.tile([P, T], U8, name="tab_sc", align_bytes=64)
         nc.vector.memset(tab_sc[0:TAB_ROW0, :].bitcast(I32), 0)
-        nc.sync.dma_start(tab_sc[TAB_ROW0:P, :].bitcast(I32), tab_scales.rearrange("a q t -> (a q) t").bitcast(I32))
-        v_sc = [keep.tile([P, S], U8, name=f"v_sc{k}", align_bytes=64) for k in range(K_PASSES)]
-        for k in range(K_PASSES):
-            nc.vector.memset(v_sc[k][:].bitcast(I32), 0)
+        nc.sync.dma_start(tab_sc[TAB_ROW0:P, :].bitcast(I32), tab_scales.rearrange("a q t -> q a t").bitcast(I32))
+        v_sc = keep.tile([P, K_PASSES, S], U8, name="v_sc", align_bytes=64)
+        nc.vector.memset(v_sc[:].rearrange("p k j -> p (k j)").bitcast(I32), 0)
         pages = [keep.tile([P, T2], F32, name=f"page{n}") for n in range(HEAD_PAGES)]
         for page in pages:
             nc.vector.memset(page[:].bitcast(I32), 0)
-        picked_sc = keep.tile([P, S], U8, name="picked_sc", align_bytes=64)
-        nc.vector.tensor_copy(picked_sc[:], tab_sc[:].indirect(idx[:]))
-        for k in range(K_PASSES):
-            for q in range(QUADS):
-                first = TAB_ROW0 + QUAD_ROWS * (QUADS * k + q)
-                nc.scalar.dma_start(
-                    v_sc[k][QUAD * q : QUAD * q + QUAD_ROWS, :].bitcast(I32),
-                    picked_sc[first : first + QUAD_ROWS, :].bitcast(I32),
-                )
-
         ident = keep.tile([P, P], F32, name="ident")
         make_identity(nc, ident[:])
 
-        v_codes = [keep.tile([P, S], U32, name=f"v_codes{k}", align_bytes=64) for k in range(K_PASSES)]
-        lo_t = keep.tile([P, GROUPS, PACK], F32, name="lo_t")
-        hi_t = keep.tile([P, GROUPS, PACK], F32, name="hi_t")
-        idx2 = keep.tile([P, S // 16], U16, name="idx2")
-
+        v_codes = {}
+        w1_raw = {}
+        w1_grouped = {}
         w1q = {}
         slope = {}
+        loaded = {}
+        gathered = {}
+        neg_x = {}
+        sums = {}
+        there = {}
         turned = {}
+        back = {}
         clipped = {}
-        d_codes = {}
-        d_scales = {}
+        d_grouped = {}
+        dq = {}
+
+        def pick_scales():
+            picked_sc = load_tile([P, S], U8, "picked_sc")
+            nc.vector.tensor_copy(picked_sc[:], tab_sc[:].indirect(idx[:]))
+            for q in range(QUADS):
+                first = TAB_ROW0 + QUAD_ROWS * K_PASSES * q
+                nc.scalar.dma_start(
+                    v_sc[QUAD * q : QUAD * q + QUAD_ROWS, :, :].bitcast(I32),
+                    picked_sc[first : first + QUAD_ROWS * K_PASSES, :].bitcast(I32),
+                )
 
         def pick_table(k):
-            words = ring.tile([P, T], I32, name="tab_words", tag="turned", bufs=TURN_BUFS, align_bytes=64)
+            if k == 0:
+                words = keep.tile([P, T], I32, name="tab_words", tag="late_page", align_bytes=64)
+            else:
+                words = load_tile([P, T], I32, "tab_words")
             nc.sync.dma_start(words[:], tab_words[k].rearrange("p t i -> p (t i)").bitcast(I32))
+            v_codes[k] = work_tile([P, S], U32, f"v_codes{k}")
             nc.vector.tensor_copy(v_codes[k][:], words[:].bitcast(U32).indirect(idx[:]))
 
-        def quantise_w1(a, k):
-            raw = ring.tile([P, PACK, PASS], F32, name="w1_raw", tag="loads", bufs=LOAD_BUFS, align_bytes=64)
+        def load_w1(a, k):
+            w1_raw[a, k] = load_tile([P, PACK, PASS], F32, f"w{a}{k}")
             nc.sync.dma_start(
-                raw[:],
+                w1_raw[a, k][:],
                 w1[PASS * k : PASS * (k + 1), PASS * a : PASS * (a + 1)].rearrange("(p j) c -> p j c", j=PACK),
             )
-            grouped = ring.tile([P, PASS * PACK], BF16, name="w1_grouped", align_bytes=64)
-            nc.scalar.copy(
-                grouped[:].rearrange("p (t m j) -> p m j t", t=PACK, j=PACK),
-                raw[:].rearrange("p j (m t) -> p m j t", t=PACK),
+
+        def cast_w1(a, k):
+            if (a, k) == (LAST, 0):
+                w1_grouped[a, k] = keep.tile([P, PASS * PACK], BF16, name="cast20", tag="slope_last", align_bytes=64)
+            else:
+                w1_grouped[a, k] = work_tile([P, PASS * PACK], BF16, f"cast{a}{k}")
+            nc.scalar.activation(
+                w1_grouped[a, k][:].rearrange("p (t m j) -> p m j t", t=PACK, j=PACK),
+                w1_raw[a, k][:].rearrange("p j (m t) -> p m j t", t=PACK),
+                ACT.Copy,
             )
-            codes = ring.tile([P, PASS], U32, name="w1_codes", bufs=4, align_bytes=64)
-            scales = ring.tile([P, PASS], U8, name="w1_scales", bufs=4, align_bytes=64)
-            nc.vector.quantize_mx(out=codes[:].bitcast(E4M3), scales=scales[:], in_=grouped[:])
-            w1q[a, k] = (codes, scales)
 
-        def gather_negated(dst, rows, h):
-            offsets = idx[:, LIST_COLS * h : LIST_COLS * (h + 1)]
-            nc.vector.tensor_scalar(dst, rows[:].indirect(offsets), -1.0, 0.0, ALU.mult, ALU.add)
+        def quantise_w1(a, k):
+            codes, scales = w1q[a, k] = code_tiles(f"w{a}{k}")
+            nc.vector.quantize_mx(out=codes[:].bitcast(E4M3), scales=scales[:], in_=w1_grouped[a, k][:])
 
-        def slope_on_vector(a, t, h, rows):
-            if t == 0 and a == LAST:
-                slope[a, h] = keep.tile([P, PACK, HALF], F32, name="slope", tag="slope_last", align_bytes=64)
-            elif t == 0:
-                slope[a, h] = ring.tile([P, PACK, HALF], F32, name="slope")
-            picked = slope[a, h][:, t, :]
-            gather_negated(picked, rows, h)
-            if a < LAST:
-                nc.vector.scalar_tensor_tensor(picked, picked, 1.0, picked, ALU.add, ALU.mult)
-            elif t == PACK - 1:
-                whole = slope[a, h][:].rearrange("p t j -> p (t j)")
-                nc.vector.scalar_tensor_tensor(whole, whole, 1.0, whole, ALU.add, ALU.mult)
-
-        def slope_by_transposes(a, t, h, rows):
-            if t == 0:
-                turned[a, h] = ring.tile([P, PACK, BLOCKS, P], F32, name="turned", bufs=TURN_BUFS, align_bytes=64)
-            picked = ring.tile([P, HALF], F32, name="neg_x", bufs=PICK_BUFS)
-            gather_negated(picked[:], rows, h)
-            squares = ring.tile([P, HALF], F32, name="squares", bufs=4)
-            nc.scalar.activation(squares[:], picked[:], ACT.Square)
-            there = psum.tile([P, BLOCKS, P], F32, name="there", bufs=THERE_BANKS)
-            for b in range(BLOCKS):
-                block = slice(P * b, P * (b + 1))
-                nc.tensor.matmul(there[:, b, :], squares[:, block], ident[:], start=True, stop=False, is_transpose=True)
-                nc.tensor.matmul(there[:, b, :], picked[:, block], ident[:], start=False, stop=True, is_transpose=True)
-            nc.scalar.copy(turned[a, h][:, t, :, :], there[:])
-
-        def saved_slice(a, t):
-            rows = ring.tile([P, T], F32, name="s_rows", tag="loads", bufs=LOAD_BUFS, align_bytes=64)
+        def saved_slice(a, t, halves=range(HALVES)):
+            rows = load_tile([P, T], F32, f"s{a}{t}")
             nc.sync.dma_start(
                 rows[:], sT[PASS * a : PASS * (a + 1), :].rearrange("(p t) c -> p t c", t=PACK)[:, t, :]
             )
-            for h in range(HALVES):
-                if (a, h) in DIRECT:
-                    slope_on_vector(a, t, h, rows)
-                else:
-                    slope_by_transposes(a, t, h, rows)
+            loaded[a, t] = rows
+            if (a, t) == (LAST, 0):
+                slope[a] = keep.tile([P, PACK, HALF], F32, name="slope_last", align_bytes=64)
+            for h in halves:
+                gather(a, t, h)
 
-        def hidden(a):
-            if a == LAST:
-                clipped[a] = ring.tile([P, PACK, S], F32, name="clipped", tag="clipped_last", bufs=1)
+        def gather(a, t, h):
+            if (a, h) == (LAST, 0):
+                neg_x[a, t, h] = slope[a][:, t, :]
             else:
-                clipped[a] = ring.tile([P, PACK, S], F32, name="clipped")
-            for t in range(PACK):
-                for h in range(HALVES):
-                    cols = slice(HALF * h, HALF * (h + 1))
-                    acc = psum.tile([P, HALF], F32, name="h_acc", tag="acc", bufs=SUM_BANKS)
-                    for k in range(K_PASSES):
-                        codes, scales = w1q[a, k]
-                        nc.tensor.matmul_mx(
-                            out=acc[:],
-                            lhsT=codes[:, P * t : P * (t + 1)].bitcast(E4M3),
-                            lhsT_scale=scales[:, P * t : P * (t + 1)],
-                            rhs=v_codes[k][:, cols].bitcast(E5M2),
-                            rhs_scale=v_sc[k][:, cols],
-                            start=(k == 0),
-                            stop=(k == K_PASSES - 1),
-                        )
-                    nc.scalar.copy(clipped[a][:, t, cols], acc[:])
-                c = clipped[a][:, t, :]
-                clipper = nc.vector if a == 0 else nc.gpsimd
-                clipper.tensor_scalar(c, c, hi_t[:, a, t : t + 1], lo_t[:, a, t : t + 1], ALU.min, ALU.max)
+                if (a, t) not in gathered:
+                    gathered[a, t] = work_tile([P, S], F32, f"x{a}{t}")
+                neg_x[a, t, h] = gathered[a, t][:, HALF * h : HALF * (h + 1)]
+            offsets = idx[:, LIST_COLS * h : LIST_COLS * (h + 1)]
+            nc.vector.tensor_scalar(neg_x[a, t, h], loaded[a, t][:].indirect(offsets), -1.0, 0.0, ALU.mult, ALU.add)
+
+        def slope_on_vector(a, t):
+            if (a, t) == (0, 0):
+                slope[0] = keep.tile([P, PACK, S], F32, name="slope_first", align_bytes=64)
+            if a == 0:
+                dst, picked = slope[0][:, t, :], gathered[0, t][:]
+            else:
+                picked = slope[a][:].rearrange("p t j -> p (t j)")
+                slope[a] = keep.tile([P, PACK, HALF], F32, name="slope_out", tag="slope_first", align_bytes=64)
+                dst = slope[a][:].rearrange("p t j -> p (t j)")
+            nc.vector.scalar_tensor_tensor(dst, picked, 1.0, picked, ALU.add, ALU.mult)
+
+        def hidden(a, t, halves=range(HALVES)):
+            for h in halves:
+                cols = slice(HALF * h, HALF * (h + 1))
+                acc = sums[a, t, h] = bank([P, HALF], f"h{a}{t}{h}")
+                for k in reversed(range(K_PASSES)):
+                    codes, scales = w1q[a, k]
+                    nc.tensor.matmul_mx(
+                        out=acc[:],
+                        lhsT=codes[:, P * t : P * (t + 1)].bitcast(E4M3),
+                        lhsT_scale=scales[:, P * t : P * (t + 1)],
+                        rhs=v_codes[k][:, cols].bitcast(E5M2),
+                        rhs_scale=v_sc[:, k, cols],
+                        start=(k == K_PASSES - 1),
+                        stop=(k == 0),
+                    )
+
+        def clip(a, t):
+            if t == 0:
+                clipped[a] = ring.tile([P, PACK, S], F32, name=f"c{a}", tag="clipped", bufs=2, align_bytes=64)
+            if (a, t) == (LAST, PACK - 1):
+                raw = keep.tile([P, S], F32, name="raw_last", tag="slope_first", align_bytes=64)
+            else:
+                raw = work_tile([P, S], F32, f"raw{a}{t}")
+            for h in range(HALVES):
+                nc.scalar.copy(raw[:, HALF * h : HALF * (h + 1)], sums[a, t, h][:])
+            for first in range(0, S, CLIP_COLS):
+                cols = slice(first, first + CLIP_COLS)
+                nc.gpsimd.tensor_scalar(
+                    clipped[a][:, t, cols], raw[:, cols], hi_t[:, a, t : t + 1], lo_t[:, a, t : t + 1], ALU.min, ALU.max
+                )
+
+        def turn_there(a, t, h):
+            picked = neg_x[a, t, h]
+            squares = work_tile([P, HALF], F32, f"sq{a}{t}{h}")
+            nc.scalar.activation(squares[:], picked, ACT.Square)
+            there[a, t, h] = bank([P, HALF], f"there{a}{t}{h}")
+            for b in range(BLOCKS):
+                block = slice(P * b, P * (b + 1))
+                dst = there[a, t, h][:, block]
+                nc.tensor.matmul(dst, squares[:, block], ident[:], start=True, stop=False, is_transpose=True)
+                nc.tensor.matmul(dst, picked[:, block], ident[:], start=False, stop=True, is_transpose=True)
+
+        def fetch(a, t, h):
+            turned[a, t, h] = work_tile([P, HALF], F32, f"tu{a}{t}{h}")
+            nc.scalar.copy(turned[a, t, h][:], there[a, t, h][:])
+
+        def turn_back(a, h):
+            for b in range(BLOCKS):
+                back[a, h, b] = bank([P, PACK, P], f"back{a}{h}{b}")
+                for t in range(PACK):
+                    nc.tensor.transpose(back[a, h, b][:, t, :], turned[a, t, h][:, P * b : P * (b + 1)], ident[:])
 
         def interleaved_product(dst, factor, c):
             nc.vector.tensor_tensor(
@@ -183,92 +231,50 @@ def tile_list_timeout_plan_gradients_kernel(
                 ALU.mult,
             )
 
-        def finish(a, h):
-            if (a, h) == (LAST, 0):
-                grouped = keep.tile([P, HALF * PACK], BF16, name="d_grouped", tag="late_page", align_bytes=64)
-            elif (a, h) == (LAST - 1, 1):
-                grouped = keep.tile([P, HALF * PACK], BF16, name="d_grouped", tag="slope_last", align_bytes=64)
-            else:
-                grouped = ring.tile([P, HALF * PACK], BF16, name="d_grouped", align_bytes=64)
+        def multiply(a, h):
+            grouped = d_grouped[a, h] = work_tile([P, HALF * PACK], BF16, f"d{a}{h}")
             c = clipped[a][:, :, HALF * h : HALF * (h + 1)]
-            if (a, h) in DIRECT:
-                interleaved_product(grouped[:], slope[a, h][:], c)
+            if a == 0:
+                factor = slope[a][:, :, HALF * h : HALF * (h + 1)]
+                for first in range(0, HALF, POOL_COLS):
+                    cols = slice(first, first + POOL_COLS)
+                    nc.gpsimd.tensor_tensor(
+                        grouped[:, PACK * first : PACK * (first + POOL_COLS)].rearrange("p (j t) -> p j t", t=PACK),
+                        factor[:, :, cols].rearrange("p t j -> p j t"),
+                        c[:, :, cols].rearrange("p t j -> p j t"),
+                        ALU.mult,
+                    )
+            elif (a, h) in DIRECT:
+                interleaved_product(grouped[:], slope[a][:], c)
             else:
                 for b in range(BLOCKS):
-                    back = psum.tile([P, PACK, P], F32, name="back", bufs=BACK_BANKS)
-                    for t in range(PACK):
-                        nc.tensor.transpose(back[:, t, :], turned[a, h][:, t, b, :], ident[:])
-                    interleaved_product(grouped[:, PASS * b : PASS * (b + 1)], back[:], c[:, :, P * b : P * (b + 1)])
-            d_codes[a, h] = keep.tile([P, HALF], U32, name=f"d_codes{a}{h}", align_bytes=64)
-            d_scales[a, h] = keep.tile([P, HALF], U8, name=f"d_scales{a}{h}", align_bytes=64)
-            nc.vector.quantize_mx(out=d_codes[a, h][:].bitcast(E4M3), scales=d_scales[a, h][:], in_=grouped[:])
+                    interleaved_product(grouped[:, PASS * b : PASS * (b + 1)], back[a, h, b][:], c[:, :, P * b : P * (b + 1)])
 
-        pick_table(0)
-        saved_slice(0, 0)
-        saved_slice(0, 1)
-        quantise_w1(0, 0)
-        pick_table(1)
-        saved_slice(0, 2)
-        quantise_w1(0, 1)
-        nc.sync.dma_start(lo_t[:], lo.rearrange("(a p t) -> p a t", p=P, t=PACK))
-        nc.sync.dma_start(hi_t[:], hi.rearrange("(a p t) -> p a t", p=P, t=PACK))
-        saved_slice(0, 3)
-        quantise_w1(1, 0)
-        hidden(0)
-        saved_slice(1, 0)
-        quantise_w1(1, 1)
-        finish(0, 0)
-        quantise_w1(2, 0)
-        saved_slice(1, 1)
-        quantise_w1(2, 1)
-        finish(0, 1)
-        hidden(1)
-        saved_slice(1, 2)
-        hidden(2)
-        saved_slice(1, 3)
-        saved_slice(2, 0)
-        finish(1, 0)
-        for t in range(1, PACK):
-            saved_slice(2, t)
-        finish(2, 0)
-        finish(1, 1)
-        finish(2, 1)
-
-        w2_codes = ring.tile([P, GROUPS, N], I32, name="w2_codes", tag="loads", bufs=LOAD_BUFS, align_bytes=64)
-        wgo_t = ring.tile([P, S], F32, name="wgo_t", tag="loads", bufs=LOAD_BUFS, align_bytes=64)
-        nc.sync.dma_start(w2_codes[:], w2_words.rearrange("a p e i -> p a (e i)").bitcast(I32))
-        w2_sc = keep.tile([P, N], U8, name="w2_sc", align_bytes=64)
-        nc.vector.memset(w2_sc[:].bitcast(I32), 0)
-        for q in range(QUADS):
-            nc.sync.dma_start(
-                w2_sc[QUAD * q : QUAD * q + QUAD_ROWS * GROUPS, :].bitcast(I32),
-                w2_scales[:, QUAD_ROWS * q : QUAD_ROWS * (q + 1), :].bitcast(I32),
-            )
-        nc.sync.dma_start(wgo_t[:], wgo)
-        nc.sync.dma_start(idx2[:], offs2)
-
-        pages.append(keep.tile([P, T2], F32, name="late_page", align_bytes=64))
-        nc.vector.memset(pages[-1][:].bitcast(I32), 0)
+        def quantise_d(a, h):
+            codes, scales = dq[a, h] = code_tiles(f"d{a}{h}")
+            nc.vector.quantize_mx(out=codes[:].bitcast(E4M3), scales=scales[:], in_=d_grouped[a, h][:])
 
         def place(halves, n):
             width = HALF * len(halves)
-            if (halves, n) == ((0,), len(pages) - 1):
-                y = ring.tile([P, width], F32, name="y", tag="clipped_last", bufs=1)
-            else:
-                y = ring.tile([P, width], F32, name="y", tag="turned", bufs=TURN_BUFS, align_bytes=64)
+            y = work_tile([P, width], F32, f"y{halves[0]}{n}")
             for i, h in enumerate(halves):
-                acc = psum.tile([P, HALF], F32, name="y_acc", tag="acc", bufs=SUM_BANKS)
+                acc = bank([P, HALF], f"y{h}{n}")
                 for a in range(GROUPS):
+                    codes, scales = dq[a, h]
                     nc.tensor.matmul_mx(
                         out=acc[:],
                         lhsT=w2_codes[:, a, P * n : P * (n + 1)].bitcast(E4M3),
                         lhsT_scale=w2_sc[QUAD_ROWS * a : P, P * n : P * (n + 1)],
-                        rhs=d_codes[a, h][:].bitcast(E4M3),
-                        rhs_scale=d_scales[a, h][:],
+                        rhs=codes[:].bitcast(E4M3),
+                        rhs_scale=scales[:],
                         start=(a == 0),
                         stop=(a == LAST),
                     )
                 nc.scalar.activation(y[:, HALF * i : HALF * (i + 1)], acc[:], ACT.Copy, scale=-1.0)
+            return y
+
+        def scatter(halves, n, y):
+            width = HALF * len(halves)
             page = pages[n % len(pages)]
             first = halves[0]
             nc.vector.tensor_tensor(
@@ -282,8 +288,135 @@ def tile_list_timeout_plan_gradients_kernel(
                     cols = slice(side * T2 // 2, (side + 1) * T2 // 2)
                     nc.sync.dma_start(out[P * n : P * (n + 1), cols], page[:, cols])
 
-        for h in range(HALVES):
-            for n in range(len(pages)):
-                place((h,), n)
-        for n in range(len(pages), PAGES):
-            place(tuple(range(HALVES)), n)
+        pick_scales()
+        pick_table(0)
+        bounds = keep.tile([P, 2, PACK, PACK], F32, name="bounds")
+        lo_t, hi_t = bounds[:, 0, :, :], bounds[:, 1, :, :]
+        nc.sync.dma_start(lo_t[:, 0:GROUPS, :], lo.rearrange("(a p t) -> p a t", p=P, t=PACK))
+        nc.sync.dma_start(hi_t[:, 0:GROUPS, :], hi.rearrange("(a p t) -> p a t", p=P, t=PACK))
+        saved_slice(0, 0)
+        load_w1(0, 0)
+        load_w1(0, 1)
+        pages.append(keep.tile([P, T2], F32, name="late_page", align_bytes=64))
+        nc.vector.memset(pages[-1][:].bitcast(I32), 0)
+        slope_on_vector(0, 0)
+        cast_w1(0, 0)
+        quantise_w1(0, 0)
+        cast_w1(0, 1)
+        pick_table(1)
+        quantise_w1(0, 1)
+        hidden(0, 0)
+        hidden(0, 1)
+        saved_slice(0, 1)
+        clip(0, 0)
+        hidden(0, 2)
+        slope_on_vector(0, 1)
+        clip(0, 1)
+        hidden(0, 3)
+        clip(0, 2)
+        load_w1(1, 0)
+        clip(0, 3)
+        saved_slice(0, 2)
+        cast_w1(1, 0)
+        load_w1(1, 1)
+        slope_on_vector(0, 2)
+        cast_w1(1, 1)
+        saved_slice(0, 3)
+        quantise_w1(1, 0)
+        load_w1(2, 0)
+        quantise_w1(1, 1)
+        w2_sc = ring.tile([P, N], U8, name="w2_sc", tag="scales", bufs=CODE_BUFS, align_bytes=64)
+        nc.vector.memset(w2_sc[:].bitcast(I32), 0)
+        for q in range(QUADS):
+            nc.sync.dma_start(
+                w2_sc[QUAD * q : QUAD * q + QUAD_ROWS * GROUPS, :].bitcast(I32),
+                w2_scales[:, QUAD_ROWS * q : QUAD_ROWS * (q + 1), :].bitcast(I32),
+            )
+        cast_w1(2, 0)
+        slope_on_vector(0, 3)
+        multiply(0, 0)
+        hidden(1, 0)
+        hidden(1, 1)
+        saved_slice(1, 0)
+        load_w1(2, 1)
+        clip(1, 0)
+        quantise_w1(2, 0)
+        clip(1, 1)
+        cast_w1(2, 1)
+        saved_slice(1, 1)
+        quantise_w1(2, 1)
+        multiply(0, 1)
+        hidden(1, 2, (0,))
+        turn_there(1, 0, 0)
+        hidden(1, 2, (1,))
+        turn_there(1, 0, 1)
+        saved_slice(1, 2)
+        clip(1, 2)
+        turn_there(1, 1, 0)
+        hidden(1, 3, (0,))
+        fetch(1, 0, 0)
+        hidden(1, 3, (1,))
+        turn_there(1, 1, 1)
+        fetch(1, 0, 1)
+        clip(1, 3)
+        saved_slice(1, 3)
+        hidden(2, 0, (0,))
+        turn_there(1, 2, 0)
+        fetch(1, 1, 0)
+        hidden(2, 0, (1,))
+        fetch(1, 1, 1)
+        clip(2, 0)
+        saved_slice(2, 0)
+        turn_there(1, 3, 0)
+        hidden(2, 1, (0,))
+        fetch(1, 2, 0)
+        hidden(2, 1, (1,))
+        fetch(1, 3, 0)
+        clip(2, 1)
+        saved_slice(2, 1)
+        turn_back(1, 0)
+        hidden(2, 2, (0,))
+        hidden(2, 2, (1,))
+        turn_there(1, 2, 1)
+        clip(2, 2)
+        saved_slice(2, 2)
+        hidden(2, 3, (0,))
+        hidden(2, 3, (1,))
+        fetch(1, 2, 1)
+        clip(2, 3)
+        turn_there(1, 3, 1)
+        saved_slice(2, 3, (0,))
+        w2_codes = load_tile([P, GROUPS, N], I32, "w2_codes")
+        wgo_t = load_tile([P, S], F32, "wgo_t")
+        nc.sync.dma_start(w2_codes[:], w2_words.rearrange("a p e i -> p a (e i)").bitcast(I32))
+        nc.sync.dma_start(wgo_t[:], wgo)
+        fetch(1, 3, 1)
+        multiply(1, 0)
+        turn_there(2, 0, 1)
+        turn_there(2, 1, 1)
+        quantise_d(0, 0)
+        quantise_d(1, 0)
+        turn_back(1, 1)
+        fetch(2, 0, 1)
+        turn_there(2, 2, 1)
+        slope_on_vector(2, 0)
+        fetch(2, 1, 1)
+        multiply(2, 0)
+        fetch(2, 2, 1)
+        quantise_d(2, 0)
+        scatter((0,), 0, place((0,), 0))
+        gather(2, 3, 1)
+        quantise_d(0, 1)
+        turn_there(2, 3, 1)
+        scatter((0,), 1, place((0,), 1))
+        multiply(1, 1)
+        fetch(2, 3, 1)
+        quantise_d(1, 1)
+        turn_back(2, 1)
+        multiply(2, 1)
+        quantise_d(2, 1)
+        scatter((0,), 2, place((0,), 2))
+        scatter((1,), 0, place((1,), 0))
+        scatter((1,), 1, place((1,), 1))
+        scatter((1,), 2, place((1,), 2))
+        scatter((0, 1), 3, place((0, 1), 3))

@@ -235,15 +235,7 @@ def tile_list_timeout_plan_gradients_kernel(
             grouped = d_grouped[a, h] = work_tile([P, HALF * PACK], BF16, f"d{a}{h}")
             c = clipped[a][:, :, HALF * h : HALF * (h + 1)]
             if a == 0:
-                factor = slope[a][:, :, HALF * h : HALF * (h + 1)]
-                for first in range(0, HALF, POOL_COLS):
-                    cols = slice(first, first + POOL_COLS)
-                    nc.gpsimd.tensor_tensor(
-                        grouped[:, PACK * first : PACK * (first + POOL_COLS)].rearrange("p (j t) -> p j t", t=PACK),
-                        factor[:, :, cols].rearrange("p t j -> p j t"),
-                        c[:, :, cols].rearrange("p t j -> p j t"),
-                        ALU.mult,
-                    )
+                interleaved_product(grouped[:], slope[a][:, :, HALF * h : HALF * (h + 1)], c)
             elif (a, h) in DIRECT:
                 interleaved_product(grouped[:], slope[a][:], c)
             else:
@@ -290,17 +282,17 @@ def tile_list_timeout_plan_gradients_kernel(
 
         pick_scales()
         pick_table(0)
+        load_w1(0, 0)
         bounds = keep.tile([P, 2, PACK, PACK], F32, name="bounds")
         lo_t, hi_t = bounds[:, 0, :, :], bounds[:, 1, :, :]
         nc.sync.dma_start(lo_t[:, 0:GROUPS, :], lo.rearrange("(a p t) -> p a t", p=P, t=PACK))
         nc.sync.dma_start(hi_t[:, 0:GROUPS, :], hi.rearrange("(a p t) -> p a t", p=P, t=PACK))
-        saved_slice(0, 0)
-        load_w1(0, 0)
-        load_w1(0, 1)
         pages.append(keep.tile([P, T2], F32, name="late_page", align_bytes=64))
         nc.vector.memset(pages[-1][:].bitcast(I32), 0)
+        saved_slice(0, 0)
         slope_on_vector(0, 0)
         cast_w1(0, 0)
+        load_w1(0, 1)
         quantise_w1(0, 0)
         cast_w1(0, 1)
         pick_table(1)
@@ -308,23 +300,33 @@ def tile_list_timeout_plan_gradients_kernel(
         hidden(0, 0)
         hidden(0, 1)
         saved_slice(0, 1)
+        slope_on_vector(0, 1)
         clip(0, 0)
         hidden(0, 2)
-        slope_on_vector(0, 1)
         clip(0, 1)
         hidden(0, 3)
-        clip(0, 2)
-        load_w1(1, 0)
-        clip(0, 3)
         saved_slice(0, 2)
+        slope_on_vector(0, 2)
+        clip(0, 2)
+        clip(0, 3)
+        saved_slice(0, 3)
+        slope_on_vector(0, 3)
+        load_w1(1, 0)
         cast_w1(1, 0)
         load_w1(1, 1)
-        slope_on_vector(0, 2)
         cast_w1(1, 1)
-        saved_slice(0, 3)
-        quantise_w1(1, 0)
         load_w1(2, 0)
+        quantise_w1(1, 0)
         quantise_w1(1, 1)
+        multiply(0, 0)
+        cast_w1(2, 0)
+        hidden(1, 0)
+        hidden(1, 1)
+        saved_slice(1, 0)
+        clip(1, 0)
+        load_w1(2, 1)
+        cast_w1(2, 1)
+        quantise_d(0, 0)
         w2_sc = ring.tile([P, N], U8, name="w2_sc", tag="scales", bufs=CODE_BUFS, align_bytes=64)
         nc.vector.memset(w2_sc[:].bitcast(I32), 0)
         for q in range(QUADS):
@@ -332,86 +334,77 @@ def tile_list_timeout_plan_gradients_kernel(
                 w2_sc[QUAD * q : QUAD * q + QUAD_ROWS * GROUPS, :].bitcast(I32),
                 w2_scales[:, QUAD_ROWS * q : QUAD_ROWS * (q + 1), :].bitcast(I32),
             )
-        cast_w1(2, 0)
-        slope_on_vector(0, 3)
-        multiply(0, 0)
-        hidden(1, 0)
-        hidden(1, 1)
-        saved_slice(1, 0)
-        load_w1(2, 1)
-        clip(1, 0)
         quantise_w1(2, 0)
-        clip(1, 1)
-        cast_w1(2, 1)
-        saved_slice(1, 1)
         quantise_w1(2, 1)
-        multiply(0, 1)
+        clip(1, 1)
+        saved_slice(1, 1)
         hidden(1, 2, (0,))
         turn_there(1, 0, 0)
         hidden(1, 2, (1,))
         turn_there(1, 0, 1)
-        saved_slice(1, 2)
+        multiply(0, 1)
         clip(1, 2)
-        turn_there(1, 1, 0)
-        hidden(1, 3, (0,))
         fetch(1, 0, 0)
+        saved_slice(1, 2)
+        hidden(1, 3, (0,))
+        turn_there(1, 1, 0)
+        fetch(1, 0, 1)
         hidden(1, 3, (1,))
         turn_there(1, 1, 1)
-        fetch(1, 0, 1)
         clip(1, 3)
+        fetch(1, 1, 0)
         saved_slice(1, 3)
         hidden(2, 0, (0,))
         turn_there(1, 2, 0)
-        fetch(1, 1, 0)
-        hidden(2, 0, (1,))
         fetch(1, 1, 1)
-        clip(2, 0)
-        saved_slice(2, 0)
+        hidden(2, 0, (1,))
         turn_there(1, 3, 0)
-        hidden(2, 1, (0,))
+        clip(2, 0)
         fetch(1, 2, 0)
-        hidden(2, 1, (1,))
-        fetch(1, 3, 0)
-        clip(2, 1)
-        saved_slice(2, 1)
-        turn_back(1, 0)
-        hidden(2, 2, (0,))
-        hidden(2, 2, (1,))
+        saved_slice(2, 0)
+        hidden(2, 1, (0,))
         turn_there(1, 2, 1)
+        fetch(1, 3, 0)
+        hidden(2, 1, (1,))
+        turn_back(1, 0)
+        turn_there(1, 3, 1)
+        clip(2, 1)
+        fetch(1, 2, 1)
+        saved_slice(2, 1)
+        hidden(2, 2, (0,))
+        turn_there(2, 0, 1)
+        fetch(1, 3, 1)
+        hidden(2, 2, (1,))
         clip(2, 2)
-        saved_slice(2, 2)
         hidden(2, 3, (0,))
         hidden(2, 3, (1,))
-        fetch(1, 2, 1)
+        turn_there(2, 1, 1)
         clip(2, 3)
-        turn_there(1, 3, 1)
+        fetch(2, 0, 1)
+        saved_slice(2, 2, (0,))
         saved_slice(2, 3, (0,))
         w2_codes = load_tile([P, GROUPS, N], I32, "w2_codes")
         wgo_t = load_tile([P, S], F32, "wgo_t")
         nc.sync.dma_start(w2_codes[:], w2_words.rearrange("a p e i -> p a (e i)").bitcast(I32))
         nc.sync.dma_start(wgo_t[:], wgo)
-        fetch(1, 3, 1)
         multiply(1, 0)
-        turn_there(2, 0, 1)
-        turn_there(2, 1, 1)
-        quantise_d(0, 0)
-        quantise_d(1, 0)
         turn_back(1, 1)
-        fetch(2, 0, 1)
-        turn_there(2, 2, 1)
-        slope_on_vector(2, 0)
+        gather(2, 2, 1)
         fetch(2, 1, 1)
-        multiply(2, 0)
-        fetch(2, 2, 1)
-        quantise_d(2, 0)
-        scatter((0,), 0, place((0,), 0))
-        gather(2, 3, 1)
-        quantise_d(0, 1)
-        turn_there(2, 3, 1)
-        scatter((0,), 1, place((0,), 1))
         multiply(1, 1)
-        fetch(2, 3, 1)
+        slope_on_vector(2, 0)
+        quantise_d(1, 0)
+        turn_there(2, 2, 1)
+        multiply(2, 0)
+        quantise_d(0, 1)
+        quantise_d(2, 0)
+        gather(2, 3, 1)
+        fetch(2, 2, 1)
+        scatter((0,), 0, place((0,), 0))
+        scatter((0,), 1, place((0,), 1))
         quantise_d(1, 1)
+        turn_there(2, 3, 1)
+        fetch(2, 3, 1)
         turn_back(2, 1)
         multiply(2, 1)
         quantise_d(2, 1)

@@ -189,7 +189,7 @@ def tile_list_timeout_plan_gradients_kernel(
 
         def clip(a, t):
             if t == 0:
-                clipped[a] = ring.tile([P, PACK, S], F32, name=f"c{a}", tag="clipped", bufs=2, align_bytes=64)
+                clipped[a] = keep.tile([P, PACK, S], F32, name=f"c{a}", tag=f"clipped{a // LAST}", align_bytes=64)
             if (a, t) == (LAST, PACK - 1):
                 raw = keep.tile([P, S], F32, name="raw_last", tag="slope_first", align_bytes=64)
             else:

@@ -22,9 +22,11 @@ PACK = 4
 PASS = P * PACK
 HALF = 512
 HALVES = S // HALF
+BOTH = tuple(range(HALVES))
 K_PASSES = K // PASS
 GROUPS = H // PASS
-LAST = GROUPS - 1
+FIRST, MIDDLE, LAST = range(GROUPS)
+END = PACK - 1
 LIST_COLS = HALF // 16
 PAGES = N // P
 BLOCKS = HALF // P
@@ -33,14 +35,12 @@ QUAD = 32
 QUADS = P // QUAD
 QUAD_ROWS = 4
 TAB_ROW0 = P - QUAD_ROWS * QUADS * K_PASSES
-DIRECT = ((0, 0), (0, 1), (LAST, 0))
+DIRECT = ((FIRST, 0), (FIRST, 1), (LAST, 0))
 HEAD_PAGES = 2
 LOAD_BUFS = 6
 WORK_BUFS = 25
-CODE_BUFS = GROUPS * HALVES + 2
+SCALE_BUFS = GROUPS * HALVES + 2
 BANKS = 8
-POOL_COLS = 128
-CLIP_COLS = 1024
 
 
 def tile_list_timeout_plan_gradients_kernel(
@@ -58,13 +58,17 @@ def tile_list_timeout_plan_gradients_kernel(
         def load_tile(shape, dtype, name):
             return ring.tile(shape, dtype, name=name, tag="loads", bufs=LOAD_BUFS, align_bytes=64)
 
-        def code_tiles(name):
-            codes = work_tile([P, PASS], U32, name)
-            scales = ring.tile([P, PASS], U8, name=name + "_scales", tag="scales", bufs=CODE_BUFS, align_bytes=64)
-            return codes, scales
+        def scale_tile(name):
+            return ring.tile([P, PASS], U8, name=name, tag="scales", bufs=SCALE_BUFS, align_bytes=64)
+
+        def own_tile(shape, dtype, name, tag):
+            return keep.tile(shape, dtype, name=name, tag=tag, align_bytes=64)
 
         def bank(shape, name):
             return psum.tile(shape, F32, name=name, tag="bank")
+
+        def half(h):
+            return slice(HALF * h, HALF * (h + 1))
 
         idx = keep.tile([P, S // 16], U16, name="idx")
         nc.sync.dma_start(idx[:], offs)
@@ -83,20 +87,15 @@ def tile_list_timeout_plan_gradients_kernel(
         make_identity(nc, ident[:])
 
         v_codes = {}
-        w1_raw = {}
-        w1_grouped = {}
-        w1q = {}
-        slope = {}
-        loaded = {}
+        w1_raw, w1_grouped, w1q = {}, {}, {}
+        s_rows = {}
         gathered = {}
-        neg_x = {}
-        sums = {}
-        there = {}
-        turned = {}
+        picked = {}
+        slope = {}
+        sums, there, turned = {}, {}, {}
         back = {}
         clipped = {}
-        d_grouped = {}
-        dq = {}
+        d_grouped, dq = {}, {}
 
         def pick_scales():
             picked_sc = load_tile([P, S], U8, "picked_sc")
@@ -110,15 +109,15 @@ def tile_list_timeout_plan_gradients_kernel(
 
         def pick_table(k):
             if k == 0:
-                words = keep.tile([P, T], I32, name="tab_words", tag="late_page", align_bytes=64)
+                words = own_tile([P, T], I32, "tab_words", "late_page")
             else:
                 words = load_tile([P, T], I32, "tab_words")
             nc.sync.dma_start(words[:], tab_words[k].rearrange("p t i -> p (t i)").bitcast(I32))
-            v_codes[k] = work_tile([P, S], U32, f"v_codes{k}")
+            v_codes[k] = work_tile([P, S], U32, "v_codes")
             nc.vector.tensor_copy(v_codes[k][:], words[:].bitcast(U32).indirect(idx[:]))
 
         def load_w1(a, k):
-            w1_raw[a, k] = load_tile([P, PACK, PASS], F32, f"w{a}{k}")
+            w1_raw[a, k] = load_tile([P, PACK, PASS], F32, "w1_raw")
             nc.sync.dma_start(
                 w1_raw[a, k][:],
                 w1[PASS * k : PASS * (k + 1), PASS * a : PASS * (a + 1)].rearrange("(p j) c -> p j c", j=PACK),
@@ -126,100 +125,108 @@ def tile_list_timeout_plan_gradients_kernel(
 
         def cast_w1(a, k):
             if (a, k) == (LAST, 0):
-                w1_grouped[a, k] = keep.tile([P, PASS * PACK], BF16, name="cast20", tag="slope_last", align_bytes=64)
+                w1_grouped[a, k] = own_tile([P, PASS * PACK], BF16, "w1_grouped", "picked_last")
             else:
-                w1_grouped[a, k] = work_tile([P, PASS * PACK], BF16, f"cast{a}{k}")
+                w1_grouped[a, k] = work_tile([P, PASS * PACK], BF16, "w1_grouped")
             nc.scalar.activation(
                 w1_grouped[a, k][:].rearrange("p (t m j) -> p m j t", t=PACK, j=PACK),
                 w1_raw[a, k][:].rearrange("p j (m t) -> p m j t", t=PACK),
                 ACT.Copy,
             )
 
-        def quantise_w1(a, k):
-            codes, scales = w1q[a, k] = code_tiles(f"w{a}{k}")
-            nc.vector.quantize_mx(out=codes[:].bitcast(E4M3), scales=scales[:], in_=w1_grouped[a, k][:])
+        def quantise(grouped):
+            codes = work_tile([P, PASS], U32, "codes")
+            scales = scale_tile("scales")
+            nc.vector.quantize_mx(out=codes[:].bitcast(E4M3), scales=scales[:], in_=grouped[:])
+            return codes, scales
 
-        def saved_slice(a, t, halves=range(HALVES)):
-            rows = load_tile([P, T], F32, f"s{a}{t}")
+        def quantise_w1(a, k):
+            w1q[a, k] = quantise(w1_grouped[a, k])
+
+        def quantise_d(a, h):
+            dq[a, h] = quantise(d_grouped[a, h])
+
+        def saved_slice(a, t, halves=BOTH):
+            s_rows[a, t] = load_tile([P, T], F32, "s_rows")
             nc.sync.dma_start(
-                rows[:], sT[PASS * a : PASS * (a + 1), :].rearrange("(p t) c -> p t c", t=PACK)[:, t, :]
+                s_rows[a, t][:], sT[PASS * a : PASS * (a + 1), :].rearrange("(p t) c -> p t c", t=PACK)[:, t, :]
             )
-            loaded[a, t] = rows
             if (a, t) == (LAST, 0):
-                slope[a] = keep.tile([P, PACK, HALF], F32, name="slope_last", align_bytes=64)
-            for h in halves:
-                gather(a, t, h)
+                slope[a] = own_tile([P, PACK, HALF], F32, "picked_last", "picked_last")
+            if a == FIRST:
+                if t == 0:
+                    slope[a] = own_tile([P, PACK, S], F32, "slope_first", "slope")
+                nc.vector.tensor_copy(slope[a][:, t, :], s_rows[a, t][:].indirect(idx[:]))
+            else:
+                for h in halves:
+                    gather(a, t, h)
 
         def gather(a, t, h):
             if (a, h) == (LAST, 0):
-                neg_x[a, t, h] = slope[a][:, t, :]
+                picked[a, t, h] = slope[a][:, t, :]
             else:
                 if (a, t) not in gathered:
-                    gathered[a, t] = work_tile([P, S], F32, f"x{a}{t}")
-                neg_x[a, t, h] = gathered[a, t][:, HALF * h : HALF * (h + 1)]
+                    gathered[a, t] = work_tile([P, S], F32, "gathered")
+                picked[a, t, h] = gathered[a, t][:, half(h)]
             offsets = idx[:, LIST_COLS * h : LIST_COLS * (h + 1)]
-            nc.vector.tensor_scalar(neg_x[a, t, h], loaded[a, t][:].indirect(offsets), -1.0, 0.0, ALU.mult, ALU.add)
+            nc.vector.tensor_scalar(picked[a, t, h], s_rows[a, t][:].indirect(offsets), -1.0, 0.0, ALU.mult, ALU.add)
 
-        def slope_on_vector(a, t):
-            if (a, t) == (0, 0):
-                slope[0] = keep.tile([P, PACK, S], F32, name="slope_first", align_bytes=64)
-            if a == 0:
-                dst, picked = slope[0][:, t, :], gathered[0, t][:]
-            else:
-                picked = slope[a][:].rearrange("p t j -> p (t j)")
-                slope[a] = keep.tile([P, PACK, HALF], F32, name="slope_out", tag="slope_first", align_bytes=64)
-                dst = slope[a][:].rearrange("p t j -> p (t j)")
-            nc.vector.scalar_tensor_tensor(dst, picked, 1.0, picked, ALU.add, ALU.mult)
+        def first_slopes(first, last):
+            x = slope[FIRST][:, first : last + 1, :].rearrange("p t j -> p (t j)")
+            nc.vector.scalar_tensor_tensor(x, x, 1.0, x, ALU.subtract, ALU.mult)
 
-        def hidden(a, t, halves=range(HALVES)):
+        def last_slope():
+            neg_x = slope[LAST][:].rearrange("p t j -> p (t j)")
+            slope[LAST] = own_tile([P, PACK, HALF], F32, "slope_last", "slope")
+            nc.vector.scalar_tensor_tensor(
+                slope[LAST][:].rearrange("p t j -> p (t j)"), neg_x, 1.0, neg_x, ALU.add, ALU.mult
+            )
+
+        def hidden(a, t, halves=BOTH):
             for h in halves:
-                cols = slice(HALF * h, HALF * (h + 1))
-                acc = sums[a, t, h] = bank([P, HALF], f"h{a}{t}{h}")
+                sums[a, t, h] = bank([P, HALF], "h")
                 for k in reversed(range(K_PASSES)):
                     codes, scales = w1q[a, k]
                     nc.tensor.matmul_mx(
-                        out=acc[:],
+                        out=sums[a, t, h][:],
                         lhsT=codes[:, P * t : P * (t + 1)].bitcast(E4M3),
                         lhsT_scale=scales[:, P * t : P * (t + 1)],
-                        rhs=v_codes[k][:, cols].bitcast(E5M2),
-                        rhs_scale=v_sc[:, k, cols],
+                        rhs=v_codes[k][:, half(h)].bitcast(E5M2),
+                        rhs_scale=v_sc[:, k, half(h)],
                         start=(k == K_PASSES - 1),
                         stop=(k == 0),
                     )
 
         def clip(a, t):
             if t == 0:
-                clipped[a] = keep.tile([P, PACK, S], F32, name=f"c{a}", tag=f"clipped{a // LAST}", align_bytes=64)
-            if (a, t) == (LAST, PACK - 1):
-                raw = keep.tile([P, S], F32, name="raw_last", tag="slope_first", align_bytes=64)
+                clipped[a] = own_tile([P, PACK, S], F32, "clipped", "clipped_last" if a == LAST else "clipped")
+            if (a, t) == (LAST, END):
+                unclipped = own_tile([P, S], F32, "unclipped", "slope")
             else:
-                raw = work_tile([P, S], F32, f"raw{a}{t}")
-            for h in range(HALVES):
-                nc.scalar.copy(raw[:, HALF * h : HALF * (h + 1)], sums[a, t, h][:])
-            for first in range(0, S, CLIP_COLS):
-                cols = slice(first, first + CLIP_COLS)
-                nc.gpsimd.tensor_scalar(
-                    clipped[a][:, t, cols], raw[:, cols], hi_t[:, a, t : t + 1], lo_t[:, a, t : t + 1], ALU.min, ALU.max
-                )
+                unclipped = work_tile([P, S], F32, "unclipped")
+            for h in BOTH:
+                nc.scalar.copy(unclipped[:, half(h)], sums[a, t, h][:])
+            nc.gpsimd.tensor_scalar(
+                clipped[a][:, t, :], unclipped[:], hi_t[:, a, t : t + 1], lo_t[:, a, t : t + 1], ALU.min, ALU.max
+            )
 
         def turn_there(a, t, h):
-            picked = neg_x[a, t, h]
-            squares = work_tile([P, HALF], F32, f"sq{a}{t}{h}")
-            nc.scalar.activation(squares[:], picked, ACT.Square)
-            there[a, t, h] = bank([P, HALF], f"there{a}{t}{h}")
+            squares = work_tile([P, HALF], F32, "squares")
+            nc.scalar.activation(squares[:], picked[a, t, h], ACT.Square)
+            there[a, t, h] = bank([P, HALF], "there")
             for b in range(BLOCKS):
                 block = slice(P * b, P * (b + 1))
                 dst = there[a, t, h][:, block]
                 nc.tensor.matmul(dst, squares[:, block], ident[:], start=True, stop=False, is_transpose=True)
-                nc.tensor.matmul(dst, picked[:, block], ident[:], start=False, stop=True, is_transpose=True)
+                nc.tensor.matmul(dst, picked[a, t, h][:, block], ident[:], start=False, stop=True, is_transpose=True)
 
         def fetch(a, t, h):
-            turned[a, t, h] = work_tile([P, HALF], F32, f"tu{a}{t}{h}")
+            turned[a, t, h] = work_tile([P, HALF], F32, "turned")
             nc.scalar.copy(turned[a, t, h][:], there[a, t, h][:])
 
         def turn_back(a, h):
             for b in range(BLOCKS):
-                back[a, h, b] = bank([P, PACK, P], f"back{a}{h}{b}")
+                back[a, h, b] = bank([P, PACK, P], "back")
                 for t in range(PACK):
                     nc.tensor.transpose(back[a, h, b][:, t, :], turned[a, t, h][:, P * b : P * (b + 1)], ident[:])
 
@@ -232,25 +239,21 @@ def tile_list_timeout_plan_gradients_kernel(
             )
 
         def multiply(a, h):
-            grouped = d_grouped[a, h] = work_tile([P, HALF * PACK], BF16, f"d{a}{h}")
-            c = clipped[a][:, :, HALF * h : HALF * (h + 1)]
-            if a == 0:
-                interleaved_product(grouped[:], slope[a][:, :, HALF * h : HALF * (h + 1)], c)
-            elif (a, h) in DIRECT:
-                interleaved_product(grouped[:], slope[a][:], c)
+            grouped = d_grouped[a, h] = work_tile([P, HALF * PACK], BF16, "d_grouped")
+            c = clipped[a][:, :, half(h)]
+            if (a, h) in DIRECT:
+                interleaved_product(grouped[:], slope[a][:, :, half(h)], c)
             else:
                 for b in range(BLOCKS):
-                    interleaved_product(grouped[:, PASS * b : PASS * (b + 1)], back[a, h, b][:], c[:, :, P * b : P * (b + 1)])
-
-        def quantise_d(a, h):
-            codes, scales = dq[a, h] = code_tiles(f"d{a}{h}")
-            nc.vector.quantize_mx(out=codes[:].bitcast(E4M3), scales=scales[:], in_=d_grouped[a, h][:])
+                    interleaved_product(
+                        grouped[:, PASS * b : PASS * (b + 1)], back[a, h, b][:], c[:, :, P * b : P * (b + 1)]
+                    )
 
         def place(halves, n):
             width = HALF * len(halves)
-            y = work_tile([P, width], F32, f"y{halves[0]}{n}")
+            y = work_tile([P, width], F32, "y")
             for i, h in enumerate(halves):
-                acc = bank([P, HALF], f"y{h}{n}")
+                acc = bank([P, HALF], "y_sum")
                 for a in range(GROUPS):
                     codes, scales = dq[a, h]
                     nc.tensor.matmul_mx(
@@ -262,11 +265,7 @@ def tile_list_timeout_plan_gradients_kernel(
                         start=(a == 0),
                         stop=(a == LAST),
                     )
-                nc.scalar.activation(y[:, HALF * i : HALF * (i + 1)], acc[:], ACT.Copy, scale=-1.0)
-            return y
-
-        def scatter(halves, n, y):
-            width = HALF * len(halves)
+                nc.scalar.activation(y[:, half(i)], acc[:], ACT.Copy, scale=-1.0)
             page = pages[n % len(pages)]
             first = halves[0]
             nc.vector.tensor_tensor(
@@ -282,134 +281,119 @@ def tile_list_timeout_plan_gradients_kernel(
 
         pick_scales()
         pick_table(0)
-        load_w1(0, 0)
+        load_w1(FIRST, 0)
         bounds = keep.tile([P, 2, PACK, PACK], F32, name="bounds")
         lo_t, hi_t = bounds[:, 0, :, :], bounds[:, 1, :, :]
         nc.sync.dma_start(lo_t[:, 0:GROUPS, :], lo.rearrange("(a p t) -> p a t", p=P, t=PACK))
         nc.sync.dma_start(hi_t[:, 0:GROUPS, :], hi.rearrange("(a p t) -> p a t", p=P, t=PACK))
-        pages.append(keep.tile([P, T2], F32, name="late_page", align_bytes=64))
+        pages.append(own_tile([P, T2], F32, "late_page", "late_page"))
         nc.vector.memset(pages[-1][:].bitcast(I32), 0)
-        saved_slice(0, 0)
-        slope_on_vector(0, 0)
-        cast_w1(0, 0)
-        load_w1(0, 1)
-        quantise_w1(0, 0)
-        cast_w1(0, 1)
+        saved_slice(FIRST, 0)
+        first_slopes(0, 0)
+        cast_w1(FIRST, 0)
+        load_w1(FIRST, 1)
+        quantise_w1(FIRST, 0)
+        cast_w1(FIRST, 1)
         pick_table(1)
-        quantise_w1(0, 1)
-        hidden(0, 0)
-        hidden(0, 1)
-        saved_slice(0, 1)
-        slope_on_vector(0, 1)
-        clip(0, 0)
-        hidden(0, 2)
-        clip(0, 1)
-        hidden(0, 3)
-        saved_slice(0, 2)
-        slope_on_vector(0, 2)
-        clip(0, 2)
-        clip(0, 3)
-        saved_slice(0, 3)
-        slope_on_vector(0, 3)
-        load_w1(1, 0)
-        cast_w1(1, 0)
-        load_w1(1, 1)
-        cast_w1(1, 1)
-        load_w1(2, 0)
-        quantise_w1(1, 0)
-        quantise_w1(1, 1)
-        multiply(0, 0)
-        cast_w1(2, 0)
-        hidden(1, 0)
-        hidden(1, 1)
-        saved_slice(1, 0)
-        clip(1, 0)
-        load_w1(2, 1)
-        cast_w1(2, 1)
-        quantise_d(0, 0)
-        w2_sc = ring.tile([P, N], U8, name="w2_sc", tag="scales", bufs=CODE_BUFS, align_bytes=64)
+        quantise_w1(FIRST, 1)
+
+        hidden(FIRST, 0)
+        hidden(FIRST, 1)
+        saved_slice(FIRST, 1)
+        clip(FIRST, 0)
+        hidden(FIRST, 2)
+        clip(FIRST, 1)
+        hidden(FIRST, END)
+        saved_slice(FIRST, 2)
+        clip(FIRST, 2)
+        clip(FIRST, END)
+        saved_slice(FIRST, END)
+        first_slopes(1, END)
+
+        for k in range(K_PASSES):
+            load_w1(MIDDLE, k)
+            cast_w1(MIDDLE, k)
+        load_w1(LAST, 0)
+        for k in range(K_PASSES):
+            quantise_w1(MIDDLE, k)
+        multiply(FIRST, 0)
+        cast_w1(LAST, 0)
+        hidden(MIDDLE, 0)
+        hidden(MIDDLE, 1)
+        saved_slice(MIDDLE, 0)
+        clip(MIDDLE, 0)
+        load_w1(LAST, 1)
+        cast_w1(LAST, 1)
+        quantise_d(FIRST, 0)
+        w2_sc = scale_tile("w2_sc")
         nc.vector.memset(w2_sc[:].bitcast(I32), 0)
         for q in range(QUADS):
             nc.sync.dma_start(
                 w2_sc[QUAD * q : QUAD * q + QUAD_ROWS * GROUPS, :].bitcast(I32),
                 w2_scales[:, QUAD_ROWS * q : QUAD_ROWS * (q + 1), :].bitcast(I32),
             )
-        quantise_w1(2, 0)
-        quantise_w1(2, 1)
-        clip(1, 1)
-        saved_slice(1, 1)
-        hidden(1, 2, (0,))
-        turn_there(1, 0, 0)
-        hidden(1, 2, (1,))
-        turn_there(1, 0, 1)
-        multiply(0, 1)
-        clip(1, 2)
-        fetch(1, 0, 0)
-        saved_slice(1, 2)
-        hidden(1, 3, (0,))
-        turn_there(1, 1, 0)
-        fetch(1, 0, 1)
-        hidden(1, 3, (1,))
-        turn_there(1, 1, 1)
-        clip(1, 3)
-        fetch(1, 1, 0)
-        saved_slice(1, 3)
-        hidden(2, 0, (0,))
-        turn_there(1, 2, 0)
-        fetch(1, 1, 1)
-        hidden(2, 0, (1,))
-        turn_there(1, 3, 0)
-        clip(2, 0)
-        fetch(1, 2, 0)
-        saved_slice(2, 0)
-        hidden(2, 1, (0,))
-        turn_there(1, 2, 1)
-        fetch(1, 3, 0)
-        hidden(2, 1, (1,))
-        turn_back(1, 0)
-        turn_there(1, 3, 1)
-        clip(2, 1)
-        fetch(1, 2, 1)
-        saved_slice(2, 1)
-        hidden(2, 2, (0,))
-        turn_there(2, 0, 1)
-        fetch(1, 3, 1)
-        hidden(2, 2, (1,))
-        clip(2, 2)
-        hidden(2, 3, (0,))
-        hidden(2, 3, (1,))
-        turn_there(2, 1, 1)
-        clip(2, 3)
-        fetch(2, 0, 1)
-        saved_slice(2, 2, (0,))
-        saved_slice(2, 3, (0,))
+        for k in range(K_PASSES):
+            quantise_w1(LAST, k)
+        clip(MIDDLE, 1)
+
+        slices = [(a, t) for a in (MIDDLE, LAST) for t in range(PACK)]
+        turns = [(MIDDLE, t, h) for t in (0, 1) for h in BOTH] + [(MIDDLE, t, h) for h in BOTH for t in (2, END)]
+        steps = len(turns) // 2
+        for step in range(steps):
+            saved_slice(*slices[step + 1])
+            hidden(*slices[step + 2], (0,))
+            turn_there(*turns[2 * step])
+            if step > 0:
+                fetch(*turns[2 * step - 1])
+            hidden(*slices[step + 2], (1,))
+            if step == steps - 1:
+                turn_back(MIDDLE, 0)
+            turn_there(*turns[2 * step + 1])
+            if step == 0:
+                multiply(FIRST, 1)
+            clip(*slices[step + 2])
+            fetch(*turns[2 * step])
+
+        saved_slice(LAST, 1)
+        hidden(LAST, 2, (0,))
+        turn_there(LAST, 0, 1)
+        fetch(*turns[-1])
+        hidden(LAST, 2, (1,))
+        clip(LAST, 2)
+        hidden(LAST, END)
+        turn_there(LAST, 1, 1)
+        clip(LAST, END)
+        fetch(LAST, 0, 1)
+
+        saved_slice(LAST, 2, (0,))
+        saved_slice(LAST, END, (0,))
         w2_codes = load_tile([P, GROUPS, N], I32, "w2_codes")
         wgo_t = load_tile([P, S], F32, "wgo_t")
         nc.sync.dma_start(w2_codes[:], w2_words.rearrange("a p e i -> p a (e i)").bitcast(I32))
         nc.sync.dma_start(wgo_t[:], wgo)
-        multiply(1, 0)
-        turn_back(1, 1)
-        gather(2, 2, 1)
-        fetch(2, 1, 1)
-        multiply(1, 1)
-        slope_on_vector(2, 0)
-        quantise_d(1, 0)
-        turn_there(2, 2, 1)
-        multiply(2, 0)
-        quantise_d(0, 1)
-        quantise_d(2, 0)
-        gather(2, 3, 1)
-        fetch(2, 2, 1)
-        scatter((0,), 0, place((0,), 0))
-        scatter((0,), 1, place((0,), 1))
-        quantise_d(1, 1)
-        turn_there(2, 3, 1)
-        fetch(2, 3, 1)
-        turn_back(2, 1)
-        multiply(2, 1)
-        quantise_d(2, 1)
-        scatter((0,), 2, place((0,), 2))
-        scatter((1,), 0, place((1,), 0))
-        scatter((1,), 1, place((1,), 1))
-        scatter((1,), 2, place((1,), 2))
-        scatter((0, 1), 3, place((0, 1), 3))
+        multiply(MIDDLE, 0)
+        turn_back(MIDDLE, 1)
+        gather(LAST, 2, 1)
+        fetch(LAST, 1, 1)
+        multiply(MIDDLE, 1)
+        last_slope()
+        quantise_d(MIDDLE, 0)
+        turn_there(LAST, 2, 1)
+        multiply(LAST, 0)
+        quantise_d(FIRST, 1)
+        quantise_d(LAST, 0)
+        gather(LAST, END, 1)
+        fetch(LAST, 2, 1)
+        for n in range(len(pages) - 1):
+            place((0,), n)
+        quantise_d(MIDDLE, 1)
+        turn_there(LAST, END, 1)
+        fetch(LAST, END, 1)
+        turn_back(LAST, 1)
+        multiply(LAST, 1)
+        quantise_d(LAST, 1)
+        place((0,), len(pages) - 1)
+        for n in range(len(pages)):
+            place((1,), n)
+        for n in range(len(pages), PAGES):
+            place(BOTH, n)

@@ -40,6 +40,7 @@ HEAD_PAGES = 2
 LOAD_BUFS = 6
 WORK_BUFS = 25
 SCALE_BUFS = GROUPS * HALVES + 2
+EARLY = 2
 BANKS = 8
 
 
@@ -152,7 +153,7 @@ def tile_list_timeout_plan_gradients_kernel(
                 s_rows[a, t][:], sT[PASS * a : PASS * (a + 1), :].rearrange("(p t) c -> p t c", t=PACK)[:, t, :]
             )
             if (a, t) == (LAST, 0):
-                slope[a] = own_tile([P, PACK, HALF], F32, "picked_last", "picked_last")
+                gathered[a] = own_tile([P, PACK, HALF], F32, "picked_last", "picked_last")
             if a == FIRST:
                 if t == 0:
                     slope[a] = own_tile([P, PACK, S], F32, "slope_first", "slope")
@@ -163,7 +164,7 @@ def tile_list_timeout_plan_gradients_kernel(
 
         def gather(a, t, h):
             if (a, h) == (LAST, 0):
-                picked[a, t, h] = slope[a][:, t, :]
+                picked[a, t, h] = gathered[a][:, t, :]
             else:
                 if (a, t) not in gathered:
                     gathered[a, t] = work_tile([P, S], F32, "gathered")
@@ -175,12 +176,20 @@ def tile_list_timeout_plan_gradients_kernel(
             x = slope[FIRST][:, first : last + 1, :].rearrange("p t j -> p (t j)")
             nc.vector.scalar_tensor_tensor(x, x, 1.0, x, ALU.subtract, ALU.mult)
 
-        def last_slope():
-            neg_x = slope[LAST][:].rearrange("p t j -> p (t j)")
-            slope[LAST] = own_tile([P, PACK, HALF], F32, "slope_last", "slope")
-            nc.vector.scalar_tensor_tensor(
-                slope[LAST][:].rearrange("p t j -> p (t j)"), neg_x, 1.0, neg_x, ALU.add, ALU.mult
-            )
+        def early_slope(t):
+            if t == 0:
+                slope[LAST] = own_tile([P, PACK, HALF], F32, "slope_last", "slope")
+            neg_x = picked[LAST, t, 0]
+            one_less_x = work_tile([P, HALF], F32, "one_less_x")
+            nc.gpsimd.tensor_scalar(one_less_x[:], neg_x, 1.0, 1.0, ALU.mult, ALU.add)
+            nc.gpsimd.tensor_tensor(slope[LAST][:, t, :], neg_x, one_less_x[:], ALU.mult)
+
+        def late_columns(tile):
+            return tile[:, EARLY:PACK, :].rearrange("p t j -> p (t j)")
+
+        def late_slopes():
+            neg_x = late_columns(gathered[LAST])
+            nc.vector.scalar_tensor_tensor(late_columns(slope[LAST]), neg_x, 1.0, neg_x, ALU.add, ALU.mult)
 
         def hidden(a, t, halves=BOTH):
             for h in halves:
@@ -201,13 +210,13 @@ def tile_list_timeout_plan_gradients_kernel(
             if t == 0:
                 clipped[a] = own_tile([P, PACK, S], F32, "clipped", "clipped_last" if a == LAST else "clipped")
             if (a, t) == (LAST, END):
-                unclipped = own_tile([P, S], F32, "unclipped", "slope")
+                unclipped = late_columns(slope[LAST])
             else:
-                unclipped = work_tile([P, S], F32, "unclipped")
+                unclipped = work_tile([P, S], F32, "unclipped")[:]
             for h in BOTH:
                 nc.scalar.copy(unclipped[:, half(h)], sums[a, t, h][:])
             nc.gpsimd.tensor_scalar(
-                clipped[a][:, t, :], unclipped[:], hi_t[:, a, t : t + 1], lo_t[:, a, t : t + 1], ALU.min, ALU.max
+                clipped[a][:, t, :], unclipped, hi_t[:, a, t : t + 1], lo_t[:, a, t : t + 1], ALU.min, ALU.max
             )
 
         def turn_there(a, t, h):
@@ -354,9 +363,11 @@ def tile_list_timeout_plan_gradients_kernel(
             clip(*slices[step + 2])
             fetch(*turns[2 * step])
 
+        early_slope(0)
         saved_slice(LAST, 1)
         hidden(LAST, 2, (0,))
         turn_there(LAST, 0, 1)
+        early_slope(1)
         fetch(*turns[-1])
         hidden(LAST, 2, (1,))
         clip(LAST, 2)
@@ -376,7 +387,7 @@ def tile_list_timeout_plan_gradients_kernel(
         gather(LAST, 2, 1)
         fetch(LAST, 1, 1)
         multiply(MIDDLE, 1)
-        last_slope()
+        late_slopes()
         quantise_d(MIDDLE, 0)
         turn_there(LAST, 2, 1)
         multiply(LAST, 0)

@@ -35,13 +35,14 @@ QUAD = 32
 QUADS = P // QUAD
 QUAD_ROWS = 4
 TAB_ROW0 = P - QUAD_ROWS * QUADS * K_PASSES
-DIRECT = ((FIRST, 0), (FIRST, 1), (LAST, 0))
+TURNED = ((MIDDLE, 1), (LAST, 1))
 HEAD_PAGES = 2
-LOAD_BUFS = 6
-WORK_BUFS = 25
-SCALE_BUFS = GROUPS * HALVES + 2
-EARLY = 2
+LOAD_BUFS = 5
+WORK_BUFS = 29
+SCALE_BUFS = GROUPS * HALVES + 3
 BANKS = 8
+SLOPE_BYTES = {(0, 0): "s00", (0, 1): "s01", (1, 0): "s00", (2, 0): "s01"}
+CLIPPED_BYTES = {0: "c0", 1: "c0", 2: "c2"}
 
 
 def tile_list_timeout_plan_gradients_kernel(
@@ -73,30 +74,25 @@ def tile_list_timeout_plan_gradients_kernel(
 
         idx = keep.tile([P, S // 16], U16, name="idx")
         nc.sync.dma_start(idx[:], offs)
-        idx2 = keep.tile([P, S // 16], U16, name="idx2")
-        nc.sync.dma_start(idx2[:], offs2)
-
-        tab_sc = keep.tile([P, T], U8, name="tab_sc", align_bytes=64)
+        tab_sc = own_tile([P, T], U8, "tab_sc", "ident")
         nc.vector.memset(tab_sc[0:TAB_ROW0, :].bitcast(I32), 0)
         nc.sync.dma_start(tab_sc[TAB_ROW0:P, :].bitcast(I32), tab_scales.rearrange("a q t -> q a t").bitcast(I32))
+        idx2 = keep.tile([P, S // 16], U16, name="idx2")
         v_sc = keep.tile([P, K_PASSES, S], U8, name="v_sc", align_bytes=64)
         nc.vector.memset(v_sc[:].rearrange("p k j -> p (k j)").bitcast(I32), 0)
         pages = [keep.tile([P, T2], F32, name=f"page{n}") for n in range(HEAD_PAGES)]
         for page in pages:
             nc.vector.memset(page[:].bitcast(I32), 0)
-        ident = keep.tile([P, P], F32, name="ident")
-        make_identity(nc, ident[:])
 
         v_codes = {}
         w1_raw, w1_grouped, w1q = {}, {}, {}
         s_rows = {}
-        gathered = {}
         picked = {}
         slope = {}
-        sums, there, turned = {}, {}, {}
-        back = {}
-        clipped = {}
+        sums, there, turned, back = {}, {}, {}, {}
+        clipped, unclipped = {}, {}
         d_grouped, dq = {}, {}
+        weights, ys = {}, {}
 
         def pick_scales():
             picked_sc = load_tile([P, S], U8, "picked_sc")
@@ -109,13 +105,49 @@ def tile_list_timeout_plan_gradients_kernel(
                 )
 
         def pick_table(k):
-            if k == 0:
-                words = own_tile([P, T], I32, "tab_words", "late_page")
-            else:
-                words = load_tile([P, T], I32, "tab_words")
+            words = own_tile([P, T], I32, "tab_words", "late_page")
             nc.sync.dma_start(words[:], tab_words[k].rearrange("p t i -> p (t i)").bitcast(I32))
             v_codes[k] = work_tile([P, S], U32, "v_codes")
             nc.vector.tensor_copy(v_codes[k][:], words[:].bitcast(U32).indirect(idx[:]))
+
+        def identity():
+            weights["ident"] = own_tile([P, P], F32, "ident", "ident")
+            make_identity(nc, weights["ident"][:])
+
+        def load_table(k):
+            weights["words", k] = load_tile([P, T], I32, "tab_words")
+            nc.sync.dma_start(weights["words", k][:], tab_words[k].rearrange("p t i -> p (t i)").bitcast(I32))
+
+        def pick_half(k, h):
+            if h == 0:
+                v_codes[k] = work_tile([P, S], U32, "v_codes")
+            offsets = idx[:, LIST_COLS * h : LIST_COLS * (h + 1)]
+            nc.vector.tensor_copy(v_codes[k][:, half(h)], weights["words", k][:].bitcast(U32).indirect(offsets))
+
+        def late_page():
+            pages.append(own_tile([P, T2], F32, "late_page", "late_page"))
+            nc.vector.memset(pages[-1][:].bitcast(I32), 0)
+
+        def load_bounds():
+            bounds = ring.tile([P, 2, PACK, PACK], F32, name="bounds", tag="scales", bufs=SCALE_BUFS, align_bytes=64)
+            for side, bound in enumerate((lo, hi)):
+                nc.sync.dma_start(bounds[:, side, 0:GROUPS, :], bound.rearrange("(a p t) -> p a t", p=P, t=PACK))
+            weights["bounds"] = bounds
+
+        def load_w2_scales():
+            weights["scales"] = scale_tile("w2_sc")
+            nc.vector.memset(weights["scales"][:].bitcast(I32), 0)
+            for q in range(QUADS):
+                nc.sync.dma_start(
+                    weights["scales"][QUAD * q : QUAD * q + QUAD_ROWS * GROUPS, :].bitcast(I32),
+                    w2_scales[:, QUAD_ROWS * q : QUAD_ROWS * (q + 1), :].bitcast(I32),
+                )
+
+        def load_last():
+            weights["codes"] = load_tile([P, GROUPS, N], I32, "w2_codes")
+            weights["wgo"] = load_tile([P, S], F32, "wgo_t")
+            nc.sync.dma_start(weights["codes"][:], w2_words.rearrange("a p e i -> p a (e i)").bitcast(I32))
+            nc.sync.dma_start(weights["wgo"][:], wgo)
 
         def load_w1(a, k):
             w1_raw[a, k] = load_tile([P, PACK, PASS], F32, "w1_raw")
@@ -125,71 +157,61 @@ def tile_list_timeout_plan_gradients_kernel(
             )
 
         def cast_w1(a, k):
-            if (a, k) == (LAST, 0):
-                w1_grouped[a, k] = own_tile([P, PASS * PACK], BF16, "w1_grouped", "picked_last")
-            else:
-                w1_grouped[a, k] = work_tile([P, PASS * PACK], BF16, "w1_grouped")
+            w1_grouped[a, k] = work_tile([P, PASS * PACK], BF16, "w1_grouped")
             nc.scalar.activation(
                 w1_grouped[a, k][:].rearrange("p (t m j) -> p m j t", t=PACK, j=PACK),
                 w1_raw[a, k][:].rearrange("p j (m t) -> p m j t", t=PACK),
                 ACT.Copy,
             )
 
-        def quantise(grouped):
+        def quantise(a, k, grouped):
             codes = work_tile([P, PASS], U32, "codes")
             scales = scale_tile("scales")
             nc.vector.quantize_mx(out=codes[:].bitcast(E4M3), scales=scales[:], in_=grouped[:])
             return codes, scales
 
         def quantise_w1(a, k):
-            w1q[a, k] = quantise(w1_grouped[a, k])
+            w1q[a, k] = quantise(a, k, w1_grouped[a, k])
 
         def quantise_d(a, h):
-            dq[a, h] = quantise(d_grouped[a, h])
+            dq[a, h] = quantise(a, h, d_grouped[a, h])
 
-        def saved_slice(a, t, halves=BOTH):
+        def load_saved(a, t):
             s_rows[a, t] = load_tile([P, T], F32, "s_rows")
             nc.sync.dma_start(
                 s_rows[a, t][:], sT[PASS * a : PASS * (a + 1), :].rearrange("(p t) c -> p t c", t=PACK)[:, t, :]
             )
-            if (a, t) == (LAST, 0):
-                gathered[a] = own_tile([P, PACK, HALF], F32, "picked_last", "picked_last")
-            if a == FIRST:
-                if t == 0:
-                    slope[a] = own_tile([P, PACK, S], F32, "slope_first", "slope")
-                nc.vector.tensor_copy(slope[a][:, t, :], s_rows[a, t][:].indirect(idx[:]))
-            else:
-                for h in halves:
-                    gather(a, t, h)
 
         def gather(a, t, h):
-            if (a, h) == (LAST, 0):
-                picked[a, t, h] = gathered[a][:, t, :]
+            if a != FIRST:
+                picked[a, t, h] = work_tile([P, HALF], F32, "picked")[:]
             else:
-                if (a, t) not in gathered:
-                    gathered[a, t] = work_tile([P, S], F32, "gathered")
-                picked[a, t, h] = gathered[a, t][:, half(h)]
+                if (a, h) not in slope:
+                    slope[a, h] = own_tile([P, PACK, HALF], F32, "slope", SLOPE_BYTES[a, h])
+                picked[a, t, h] = slope[a, h][:, t, :]
             offsets = idx[:, LIST_COLS * h : LIST_COLS * (h + 1)]
             nc.vector.tensor_scalar(picked[a, t, h], s_rows[a, t][:].indirect(offsets), -1.0, 0.0, ALU.mult, ALU.add)
 
-        def first_slopes(first, last):
-            x = slope[FIRST][:, first : last + 1, :].rearrange("p t j -> p (t j)")
-            nc.vector.scalar_tensor_tensor(x, x, 1.0, x, ALU.subtract, ALU.mult)
+        def saved(a, t, halves=BOTH):
+            load_saved(a, t)
+            for h in halves:
+                gather(a, t, h)
 
-        def early_slope(t):
-            if t == 0:
-                slope[LAST] = own_tile([P, PACK, HALF], F32, "slope_last", "slope")
-            neg_x = picked[LAST, t, 0]
+        def slope_vector(a, h, first, last):
+            x = slope[a, h][:, first : last + 1, :].rearrange("p t j -> p (t j)")
+            nc.vector.scalar_tensor_tensor(x, x, 1.0, x, ALU.add, ALU.mult)
+
+        def slope_shared(a, t, h):
             one_less_x = work_tile([P, HALF], F32, "one_less_x")
-            nc.gpsimd.tensor_scalar(one_less_x[:], neg_x, 1.0, 1.0, ALU.mult, ALU.add)
-            nc.gpsimd.tensor_tensor(slope[LAST][:, t, :], neg_x, one_less_x[:], ALU.mult)
+            nc.scalar.activation(one_less_x[:], picked[a, t, h], ACT.Copy, bias=1.0)
+            if (a, h) not in slope:
+                slope[a, h] = own_tile([P, PACK, HALF], F32, "slope", SLOPE_BYTES[a, h])
+            nc.gpsimd.tensor_tensor(slope[a, h][:, t, :], picked[a, t, h], one_less_x[:], ALU.mult)
 
-        def late_columns(tile):
-            return tile[:, EARLY:PACK, :].rearrange("p t j -> p (t j)")
-
-        def late_slopes():
-            neg_x = late_columns(gathered[LAST])
-            nc.vector.scalar_tensor_tensor(late_columns(slope[LAST]), neg_x, 1.0, neg_x, ALU.add, ALU.mult)
+        def slope_gpsimd(a, t, h):
+            one_less_x = work_tile([P, HALF], F32, "one_less_x")
+            nc.gpsimd.tensor_scalar(one_less_x[:], picked[a, t, h], 1.0, 1.0, ALU.mult, ALU.add)
+            nc.gpsimd.tensor_tensor(picked[a, t, h], picked[a, t, h], one_less_x[:], ALU.mult)
 
         def hidden(a, t, halves=BOTH):
             for h in halves:
@@ -206,18 +228,20 @@ def tile_list_timeout_plan_gradients_kernel(
                         stop=(k == 0),
                     )
 
-        def clip(a, t):
-            if t == 0:
-                clipped[a] = own_tile([P, PACK, S], F32, "clipped", "clipped_last" if a == LAST else "clipped")
-            if (a, t) == (LAST, END):
-                unclipped = late_columns(slope[LAST])
-            else:
-                unclipped = work_tile([P, S], F32, "unclipped")[:]
-            for h in BOTH:
-                nc.scalar.copy(unclipped[:, half(h)], sums[a, t, h][:])
-            nc.gpsimd.tensor_scalar(
-                clipped[a][:, t, :], unclipped, hi_t[:, a, t : t + 1], lo_t[:, a, t : t + 1], ALU.min, ALU.max
-            )
+        def clip(a, t, halves=BOTH):
+            if (a, halves[0]) not in clipped:
+                if a not in CLIPPED_BYTES:
+                    clipped[a, halves[0]] = own_tile([P, PACK, HALF], F32, "clipped", CLIPPED_BYTES[a, halves[0]])[:]
+                else:
+                    clipped[a] = own_tile([P, PACK, S], F32, "clipped", CLIPPED_BYTES[a])[:]
+                    for h in BOTH:
+                        clipped[a, h] = clipped[a][:, :, half(h)]
+            raw = work_tile([P, HALF * len(halves)], F32, "unclipped")
+            for i, h in enumerate(halves):
+                nc.scalar.copy(raw[:, half(i)], sums[a, t, h][:])
+            dst = clipped[a] if halves == BOTH else clipped[a, halves[0]]
+            lower, upper = (weights["bounds"][:, side, a, t : t + 1] for side in range(2))
+            nc.gpsimd.tensor_scalar(dst[:, t, :], raw[:], upper, lower, ALU.min, ALU.max)
 
         def turn_there(a, t, h):
             squares = work_tile([P, HALF], F32, "squares")
@@ -226,8 +250,8 @@ def tile_list_timeout_plan_gradients_kernel(
             for b in range(BLOCKS):
                 block = slice(P * b, P * (b + 1))
                 dst = there[a, t, h][:, block]
-                nc.tensor.matmul(dst, squares[:, block], ident[:], start=True, stop=False, is_transpose=True)
-                nc.tensor.matmul(dst, picked[a, t, h][:, block], ident[:], start=False, stop=True, is_transpose=True)
+                nc.tensor.matmul(dst, squares[:, block], weights["ident"][:], start=True, stop=False, is_transpose=True)
+                nc.tensor.matmul(dst, picked[a, t, h][:, block], weights["ident"][:], start=False, stop=True, is_transpose=True)
 
         def fetch(a, t, h):
             turned[a, t, h] = work_tile([P, HALF], F32, "turned")
@@ -237,9 +261,9 @@ def tile_list_timeout_plan_gradients_kernel(
             for b in range(BLOCKS):
                 back[a, h, b] = bank([P, PACK, P], "back")
                 for t in range(PACK):
-                    nc.tensor.transpose(back[a, h, b][:, t, :], turned[a, t, h][:, P * b : P * (b + 1)], ident[:])
+                    nc.tensor.transpose(back[a, h, b][:, t, :], turned[a, t, h][:, P * b : P * (b + 1)], weights["ident"][:])
 
-        def interleaved_product(dst, factor, c):
+        def interleaved_product(a, h, dst, factor, c):
             nc.vector.tensor_tensor(
                 dst.rearrange("p (g i t) -> p g t i", i=PAIR, t=PACK),
                 factor.rearrange("p t (g i) -> p g t i", i=PAIR),
@@ -248,15 +272,19 @@ def tile_list_timeout_plan_gradients_kernel(
             )
 
         def multiply(a, h):
-            grouped = d_grouped[a, h] = work_tile([P, HALF * PACK], BF16, "d_grouped")
-            c = clipped[a][:, :, half(h)]
-            if (a, h) in DIRECT:
-                interleaved_product(grouped[:], slope[a][:, :, half(h)], c)
+            if (a, h) == (LAST, 0) and LAST not in CLIPPED_BYTES:
+                grouped = own_tile([P, HALF * PACK], BF16, "d_grouped", CLIPPED_BYTES[LAST, 1])
             else:
+                grouped = work_tile([P, HALF * PACK], BF16, "d_grouped")
+            d_grouped[a, h] = grouped
+            c = clipped[a, h]
+            if (a, h) in TURNED:
                 for b in range(BLOCKS):
                     interleaved_product(
-                        grouped[:, PASS * b : PASS * (b + 1)], back[a, h, b][:], c[:, :, P * b : P * (b + 1)]
+                        a, h, grouped[:, PASS * b : PASS * (b + 1)], back[a, h, b][:], c[:, :, P * b : P * (b + 1)]
                     )
+            else:
+                interleaved_product(a, h, grouped[:], slope[a, h][:], c)
 
         def place(halves, n):
             width = HALF * len(halves)
@@ -267,20 +295,24 @@ def tile_list_timeout_plan_gradients_kernel(
                     codes, scales = dq[a, h]
                     nc.tensor.matmul_mx(
                         out=acc[:],
-                        lhsT=w2_codes[:, a, P * n : P * (n + 1)].bitcast(E4M3),
-                        lhsT_scale=w2_sc[QUAD_ROWS * a : P, P * n : P * (n + 1)],
+                        lhsT=weights["codes"][:, a, P * n : P * (n + 1)].bitcast(E4M3),
+                        lhsT_scale=weights["scales"][QUAD_ROWS * a : P, P * n : P * (n + 1)],
                         rhs=codes[:].bitcast(E4M3),
                         rhs_scale=scales[:],
                         start=(a == 0),
                         stop=(a == LAST),
                     )
                 nc.scalar.activation(y[:, half(i)], acc[:], ACT.Copy, scale=-1.0)
+            ys[halves, n] = y
+
+        def scatter(halves, n):
+            y, width = ys[halves, n], HALF * len(halves)
             page = pages[n % len(pages)]
             first = halves[0]
             nc.vector.tensor_tensor(
                 page[:].indirect(idx2[:, LIST_COLS * first : LIST_COLS * (first + len(halves))]),
                 y[:],
-                wgo_t[:, HALF * first : HALF * first + width],
+                weights["wgo"][:, HALF * first : HALF * first + width],
                 ALU.mult,
             )
             if halves[-1] == HALVES - 1:
@@ -289,122 +321,153 @@ def tile_list_timeout_plan_gradients_kernel(
                     nc.sync.dma_start(out[P * n : P * (n + 1), cols], page[:, cols])
 
         pick_scales()
+        identity()
         pick_table(0)
-        load_w1(FIRST, 0)
-        bounds = keep.tile([P, 2, PACK, PACK], F32, name="bounds")
-        lo_t, hi_t = bounds[:, 0, :, :], bounds[:, 1, :, :]
-        nc.sync.dma_start(lo_t[:, 0:GROUPS, :], lo.rearrange("(a p t) -> p a t", p=P, t=PACK))
-        nc.sync.dma_start(hi_t[:, 0:GROUPS, :], hi.rearrange("(a p t) -> p a t", p=P, t=PACK))
-        pages.append(own_tile([P, T2], F32, "late_page", "late_page"))
-        nc.vector.memset(pages[-1][:].bitcast(I32), 0)
-        saved_slice(FIRST, 0)
-        first_slopes(0, 0)
-        cast_w1(FIRST, 0)
-        load_w1(FIRST, 1)
-        quantise_w1(FIRST, 0)
-        cast_w1(FIRST, 1)
-        pick_table(1)
-        quantise_w1(FIRST, 1)
-
-        hidden(FIRST, 0)
-        hidden(FIRST, 1)
-        saved_slice(FIRST, 1)
-        clip(FIRST, 0)
-        hidden(FIRST, 2)
-        clip(FIRST, 1)
-        hidden(FIRST, END)
-        saved_slice(FIRST, 2)
-        clip(FIRST, 2)
-        clip(FIRST, END)
-        saved_slice(FIRST, END)
-        first_slopes(1, END)
-
-        for k in range(K_PASSES):
-            load_w1(MIDDLE, k)
-            cast_w1(MIDDLE, k)
-        load_w1(LAST, 0)
-        for k in range(K_PASSES):
-            quantise_w1(MIDDLE, k)
-        multiply(FIRST, 0)
-        cast_w1(LAST, 0)
-        hidden(MIDDLE, 0)
-        hidden(MIDDLE, 1)
-        saved_slice(MIDDLE, 0)
-        clip(MIDDLE, 0)
-        load_w1(LAST, 1)
-        cast_w1(LAST, 1)
-        quantise_d(FIRST, 0)
-        w2_sc = scale_tile("w2_sc")
-        nc.vector.memset(w2_sc[:].bitcast(I32), 0)
-        for q in range(QUADS):
-            nc.sync.dma_start(
-                w2_sc[QUAD * q : QUAD * q + QUAD_ROWS * GROUPS, :].bitcast(I32),
-                w2_scales[:, QUAD_ROWS * q : QUAD_ROWS * (q + 1), :].bitcast(I32),
-            )
-        for k in range(K_PASSES):
-            quantise_w1(LAST, k)
-        clip(MIDDLE, 1)
-
-        slices = [(a, t) for a in (MIDDLE, LAST) for t in range(PACK)]
-        turns = [(MIDDLE, t, h) for t in (0, 1) for h in BOTH] + [(MIDDLE, t, h) for h in BOTH for t in (2, END)]
-        steps = len(turns) // 2
-        for step in range(steps):
-            saved_slice(*slices[step + 1])
-            hidden(*slices[step + 2], (0,))
-            turn_there(*turns[2 * step])
-            if step > 0:
-                fetch(*turns[2 * step - 1])
-            hidden(*slices[step + 2], (1,))
-            if step == steps - 1:
-                turn_back(MIDDLE, 0)
-            turn_there(*turns[2 * step + 1])
-            if step == 0:
-                multiply(FIRST, 1)
-            clip(*slices[step + 2])
-            fetch(*turns[2 * step])
-
-        early_slope(0)
-        saved_slice(LAST, 1)
-        hidden(LAST, 2, (0,))
-        turn_there(LAST, 0, 1)
-        early_slope(1)
-        fetch(*turns[-1])
-        hidden(LAST, 2, (1,))
-        clip(LAST, 2)
-        hidden(LAST, END)
-        turn_there(LAST, 1, 1)
-        clip(LAST, END)
-        fetch(LAST, 0, 1)
-
-        saved_slice(LAST, 2, (0,))
-        saved_slice(LAST, END, (0,))
-        w2_codes = load_tile([P, GROUPS, N], I32, "w2_codes")
-        wgo_t = load_tile([P, S], F32, "wgo_t")
-        nc.sync.dma_start(w2_codes[:], w2_words.rearrange("a p e i -> p a (e i)").bitcast(I32))
-        nc.sync.dma_start(wgo_t[:], wgo)
-        multiply(MIDDLE, 0)
-        turn_back(MIDDLE, 1)
-        gather(LAST, 2, 1)
-        fetch(LAST, 1, 1)
-        multiply(MIDDLE, 1)
-        late_slopes()
-        quantise_d(MIDDLE, 0)
-        turn_there(LAST, 2, 1)
-        multiply(LAST, 0)
-        quantise_d(FIRST, 1)
-        quantise_d(LAST, 0)
-        gather(LAST, END, 1)
-        fetch(LAST, 2, 1)
-        for n in range(len(pages) - 1):
-            place((0,), n)
-        quantise_d(MIDDLE, 1)
-        turn_there(LAST, END, 1)
-        fetch(LAST, END, 1)
-        turn_back(LAST, 1)
-        multiply(LAST, 1)
-        quantise_d(LAST, 1)
-        place((0,), len(pages) - 1)
-        for n in range(len(pages)):
-            place((1,), n)
-        for n in range(len(pages), PAGES):
-            place(BOTH, n)
+        load_saved(0, 0)
+        gather(0, 0, 0)
+        gather(0, 0, 1)
+        late_page()
+        load_w1(0, 0)
+        cast_w1(0, 0)
+        load_w1(0, 1)
+        slope_vector(0, 0, 0, 0)
+        slope_vector(0, 1, 0, 0)
+        quantise_w1(0, 0)
+        cast_w1(0, 1)
+        load_table(1)
+        nc.sync.dma_start(idx2[:], offs2)
+        pick_half(1, 0)
+        quantise_w1(0, 1)
+        pick_half(1, 1)
+        load_saved(0, 1)
+        load_saved(0, 2)
+        load_bounds()
+        hidden(0, 0, (0,))
+        hidden(0, 1, (0,))
+        hidden(0, 2, (0,))
+        hidden(0, 3, (0,))
+        gather(0, 1, 0)
+        clip(0, 0, (0,))
+        clip(0, 1, (0,))
+        hidden(0, 0, (1,))
+        hidden(0, 1, (1,))
+        gather(0, 1, 1)
+        clip(0, 2, (0,))
+        clip(0, 3, (0,))
+        hidden(0, 2, (1,))
+        hidden(0, 3, (1,))
+        gather(0, 2, 0)
+        clip(0, 0, (1,))
+        clip(0, 1, (1,))
+        gather(0, 2, 1)
+        clip(0, 2, (1,))
+        clip(0, 3, (1,))
+        load_saved(0, 3)
+        gather(0, 3, 0)
+        gather(0, 3, 1)
+        slope_vector(0, 0, 1, 3)
+        slope_vector(0, 1, 1, 3)
+        load_w1(1, 0)
+        cast_w1(1, 0)
+        load_w1(1, 1)
+        cast_w1(1, 1)
+        quantise_w1(1, 0)
+        multiply(0, 0)
+        quantise_w1(1, 1)
+        hidden(1, 0)
+        hidden(1, 1)
+        load_w2_scales()
+        load_w1(2, 0)
+        cast_w1(2, 0)
+        multiply(0, 1)
+        quantise_d(0, 0)
+        load_w1(2, 1)
+        cast_w1(2, 1)
+        quantise_w1(2, 0)
+        quantise_d(0, 1)
+        quantise_w1(2, 1)
+        clip(1, 0)
+        hidden(1, 2)
+        clip(1, 1)
+        hidden(1, 3)
+        load_saved(1, 0)
+        gather(1, 0, 0)
+        gather(1, 0, 1)
+        slope_shared(1, 0, 0)
+        clip(1, 2)
+        hidden(2, 0)
+        turn_there(1, 0, 1)
+        load_saved(1, 1)
+        gather(1, 1, 0)
+        gather(1, 1, 1)
+        slope_shared(1, 1, 0)
+        clip(1, 3)
+        hidden(2, 1)
+        turn_there(1, 1, 1)
+        load_saved(1, 2)
+        gather(1, 2, 0)
+        gather(1, 2, 1)
+        slope_shared(1, 2, 0)
+        fetch(1, 0, 1)
+        clip(2, 0)
+        hidden(2, 2)
+        turn_there(1, 2, 1)
+        load_saved(1, 3)
+        gather(1, 3, 0)
+        gather(1, 3, 1)
+        slope_shared(1, 3, 0)
+        fetch(1, 1, 1)
+        clip(2, 1)
+        hidden(2, 3)
+        turn_there(1, 3, 1)
+        load_saved(2, 0)
+        gather(2, 0, 0)
+        gather(2, 0, 1)
+        slope_shared(2, 0, 0)
+        fetch(1, 2, 1)
+        clip(2, 2)
+        turn_there(2, 0, 1)
+        load_saved(2, 1)
+        gather(2, 1, 0)
+        gather(2, 1, 1)
+        slope_shared(2, 1, 0)
+        fetch(1, 3, 1)
+        turn_back(1, 1)
+        clip(2, 3)
+        turn_there(2, 1, 1)
+        load_saved(2, 2)
+        gather(2, 2, 0)
+        gather(2, 2, 1)
+        slope_shared(2, 2, 0)
+        fetch(2, 0, 1)
+        turn_there(2, 2, 1)
+        load_saved(2, 3)
+        gather(2, 3, 0)
+        gather(2, 3, 1)
+        load_last()
+        multiply(1, 1)
+        slope_shared(2, 3, 0)
+        fetch(2, 1, 1)
+        turn_there(2, 3, 1)
+        fetch(2, 2, 1)
+        fetch(2, 3, 1)
+        turn_back(2, 1)
+        multiply(1, 0)
+        quantise_d(1, 1)
+        multiply(2, 0)
+        quantise_d(1, 0)
+        quantise_d(2, 0)
+        place((0,), 0)
+        multiply(2, 1)
+        quantise_d(2, 1)
+        place((0,), 1)
+        scatter((0,), 0)
+        place((1,), 0)
+        scatter((0,), 1)
+        place((1,), 1)
+        scatter((1,), 0)
+        scatter((1,), 1)
+        place(BOTH, 2)
+        scatter(BOTH, 2)
+        place(BOTH, 3)
+        scatter(BOTH, 3)

@@ -39,10 +39,10 @@ TURNED = ((MIDDLE, 1), (LAST, 1))
 HEAD_PAGES = 2
 LOAD_BUFS = 5
 WORK_BUFS = 29
-SCALE_BUFS = GROUPS * HALVES + 3
+SCALE_BUFS = GROUPS * HALVES + 2
 BANKS = 8
 SLOPE_BYTES = {(0, 0): "s00", (0, 1): "s01", (1, 0): "s00", (2, 0): "s01"}
-CLIPPED_BYTES = {0: "c0", 1: "c0", 2: "c2"}
+CLIPPED_BYTES = {0: "c0", 1: "c1", 2: "c0"}
 
 
 def tile_list_timeout_plan_gradients_kernel(
@@ -129,7 +129,7 @@ def tile_list_timeout_plan_gradients_kernel(
             nc.vector.memset(pages[-1][:].bitcast(I32), 0)
 
         def load_bounds():
-            bounds = ring.tile([P, 2, PACK, PACK], F32, name="bounds", tag="scales", bufs=SCALE_BUFS, align_bytes=64)
+            bounds = keep.tile([P, 2, PACK, PACK], F32, name="bounds")
             for side, bound in enumerate((lo, hi)):
                 nc.sync.dma_start(bounds[:, side, 0:GROUPS, :], bound.rearrange("(a p t) -> p a t", p=P, t=PACK))
             weights["bounds"] = bounds
@@ -157,7 +157,10 @@ def tile_list_timeout_plan_gradients_kernel(
             )
 
         def cast_w1(a, k):
-            w1_grouped[a, k] = work_tile([P, PASS * PACK], BF16, "w1_grouped")
+            if (a, k) == (LAST, K_PASSES - 1):
+                w1_grouped[a, k] = own_tile([P, PASS * PACK], BF16, "w1_grouped", CLIPPED_BYTES[MIDDLE])
+            else:
+                w1_grouped[a, k] = work_tile([P, PASS * PACK], BF16, "w1_grouped")
             nc.scalar.activation(
                 w1_grouped[a, k][:].rearrange("p (t m j) -> p m j t", t=PACK, j=PACK),
                 w1_raw[a, k][:].rearrange("p j (m t) -> p m j t", t=PACK),
@@ -182,36 +185,37 @@ def tile_list_timeout_plan_gradients_kernel(
                 s_rows[a, t][:], sT[PASS * a : PASS * (a + 1), :].rearrange("(p t) c -> p t c", t=PACK)[:, t, :]
             )
 
+        def gather_first(t):
+            if t == 0:
+                slope[FIRST] = own_tile([P, PACK, S], F32, "slope_first", "slope")
+                for h in BOTH:
+                    slope[FIRST, h] = slope[FIRST][:, :, half(h)]
+            nc.vector.tensor_copy(slope[FIRST][:, t, :], s_rows[FIRST, t][:].indirect(idx[:]))
+
+        def first_slopes(first, last):
+            x = slope[FIRST][:, first : last + 1, :].rearrange("p t j -> p (t j)")
+            nc.vector.scalar_tensor_tensor(x, x, 1.0, x, ALU.subtract, ALU.mult)
+
         def gather(a, t, h):
-            if a != FIRST:
-                picked[a, t, h] = work_tile([P, HALF], F32, "picked")[:]
-            else:
-                if (a, h) not in slope:
-                    slope[a, h] = own_tile([P, PACK, HALF], F32, "slope", SLOPE_BYTES[a, h])
-                picked[a, t, h] = slope[a, h][:, t, :]
+            picked[a, t, h] = work_tile([P, HALF], F32, "picked")[:]
             offsets = idx[:, LIST_COLS * h : LIST_COLS * (h + 1)]
             nc.vector.tensor_scalar(picked[a, t, h], s_rows[a, t][:].indirect(offsets), -1.0, 0.0, ALU.mult, ALU.add)
 
-        def saved(a, t, halves=BOTH):
-            load_saved(a, t)
-            for h in halves:
-                gather(a, t, h)
+        def later_slope(a, t, h):
+            if (a, h) not in slope:
+                both = own_tile([P, GROUPS - 1, PACK, HALF], F32, "slope_later", "slope")
+                for group in (MIDDLE, LAST):
+                    slope[group, h] = both[:, group - MIDDLE, :, :]
+            return slope[a, h][:, t, :]
 
-        def slope_vector(a, h, first, last):
-            x = slope[a, h][:, first : last + 1, :].rearrange("p t j -> p (t j)")
-            nc.vector.scalar_tensor_tensor(x, x, 1.0, x, ALU.add, ALU.mult)
+        def slope_vector(a, t, h):
+            x = picked[a, t, h]
+            nc.vector.scalar_tensor_tensor(later_slope(a, t, h), x, 1.0, x, ALU.add, ALU.mult)
 
         def slope_shared(a, t, h):
             one_less_x = work_tile([P, HALF], F32, "one_less_x")
             nc.scalar.activation(one_less_x[:], picked[a, t, h], ACT.Copy, bias=1.0)
-            if (a, h) not in slope:
-                slope[a, h] = own_tile([P, PACK, HALF], F32, "slope", SLOPE_BYTES[a, h])
-            nc.gpsimd.tensor_tensor(slope[a, h][:, t, :], picked[a, t, h], one_less_x[:], ALU.mult)
-
-        def slope_gpsimd(a, t, h):
-            one_less_x = work_tile([P, HALF], F32, "one_less_x")
-            nc.gpsimd.tensor_scalar(one_less_x[:], picked[a, t, h], 1.0, 1.0, ALU.mult, ALU.add)
-            nc.gpsimd.tensor_tensor(picked[a, t, h], picked[a, t, h], one_less_x[:], ALU.mult)
+            nc.gpsimd.tensor_tensor(later_slope(a, t, h), picked[a, t, h], one_less_x[:], ALU.mult)
 
         def hidden(a, t, halves=BOTH):
             for h in halves:
@@ -284,7 +288,7 @@ def tile_list_timeout_plan_gradients_kernel(
                         a, h, grouped[:, PASS * b : PASS * (b + 1)], back[a, h, b][:], c[:, :, P * b : P * (b + 1)]
                     )
             else:
-                interleaved_product(a, h, grouped[:], slope[a, h][:], c)
+                interleaved_product(a, h, grouped[:], slope[a, h], c)
 
         def place(halves, n):
             width = HALF * len(halves)
@@ -320,53 +324,47 @@ def tile_list_timeout_plan_gradients_kernel(
                     cols = slice(side * T2 // 2, (side + 1) * T2 // 2)
                     nc.sync.dma_start(out[P * n : P * (n + 1), cols], page[:, cols])
 
+        load_bounds()
+        nc.sync.dma_start(idx2[:], offs2)
         pick_scales()
         identity()
         pick_table(0)
         load_saved(0, 0)
-        gather(0, 0, 0)
-        gather(0, 0, 1)
+        gather_first(0)
         late_page()
         load_w1(0, 0)
         cast_w1(0, 0)
         load_w1(0, 1)
-        slope_vector(0, 0, 0, 0)
-        slope_vector(0, 1, 0, 0)
+        first_slopes(0, 0)
         quantise_w1(0, 0)
         cast_w1(0, 1)
         load_table(1)
-        nc.sync.dma_start(idx2[:], offs2)
         pick_half(1, 0)
         quantise_w1(0, 1)
         pick_half(1, 1)
         load_saved(0, 1)
         load_saved(0, 2)
-        load_bounds()
         hidden(0, 0, (0,))
         hidden(0, 1, (0,))
         hidden(0, 2, (0,))
         hidden(0, 3, (0,))
-        gather(0, 1, 0)
+        gather_first(1)
         clip(0, 0, (0,))
         clip(0, 1, (0,))
         hidden(0, 0, (1,))
         hidden(0, 1, (1,))
-        gather(0, 1, 1)
         clip(0, 2, (0,))
         clip(0, 3, (0,))
         hidden(0, 2, (1,))
         hidden(0, 3, (1,))
-        gather(0, 2, 0)
+        gather_first(2)
         clip(0, 0, (1,))
         clip(0, 1, (1,))
-        gather(0, 2, 1)
         clip(0, 2, (1,))
         clip(0, 3, (1,))
         load_saved(0, 3)
-        gather(0, 3, 0)
-        gather(0, 3, 1)
-        slope_vector(0, 0, 1, 3)
-        slope_vector(0, 1, 1, 3)
+        gather_first(3)
+        first_slopes(1, 3)
         load_w1(1, 0)
         cast_w1(1, 0)
         load_w1(1, 1)

@@ -196,10 +196,20 @@ def tile_list_timeout_plan_gradients_kernel(
             x = slope[FIRST][:, first : last + 1, :].rearrange("p t j -> p (t j)")
             nc.vector.scalar_tensor_tensor(x, x, 1.0, x, ALU.subtract, ALU.mult)
 
-        def gather(a, t, h):
-            picked[a, t, h] = work_tile([P, HALF], F32, "picked")[:]
-            offsets = idx[:, LIST_COLS * h : LIST_COLS * (h + 1)]
-            nc.vector.tensor_scalar(picked[a, t, h], s_rows[a, t][:].indirect(offsets), -1.0, 0.0, ALU.mult, ALU.add)
+        def first_shared(t, h):
+            x = slope[FIRST, h][:, t, :]
+            x_less_one = work_tile([P, HALF], F32, "x_less_one")
+            nc.scalar.activation(x_less_one[:], x, ACT.Copy, bias=-1.0)
+            nc.gpsimd.tensor_tensor(x, x, x_less_one[:], ALU.mult)
+
+        def gather(a, t):
+            picked[a, t] = work_tile([P, S], F32, "picked")
+            if (a, t) == (LAST, END):
+                for h in BOTH:
+                    offsets = idx[:, LIST_COLS * h : LIST_COLS * (h + 1)]
+                    nc.vector.tensor_copy(picked[a, t][:, half(h)], s_rows[a, t][:].indirect(offsets))
+            else:
+                nc.vector.tensor_copy(picked[a, t][:], s_rows[a, t][:].indirect(idx[:]))
 
         def later_slope(a, t, h):
             if (a, h) not in slope:
@@ -209,13 +219,14 @@ def tile_list_timeout_plan_gradients_kernel(
             return slope[a, h][:, t, :]
 
         def slope_vector(a, t, h):
-            x = picked[a, t, h]
-            nc.vector.scalar_tensor_tensor(later_slope(a, t, h), x, 1.0, x, ALU.add, ALU.mult)
+            x = picked[a, t][:, half(h)]
+            nc.vector.scalar_tensor_tensor(later_slope(a, t, h), x, 1.0, x, ALU.subtract, ALU.mult)
 
         def slope_shared(a, t, h):
-            one_less_x = work_tile([P, HALF], F32, "one_less_x")
-            nc.scalar.activation(one_less_x[:], picked[a, t, h], ACT.Copy, bias=1.0)
-            nc.gpsimd.tensor_tensor(later_slope(a, t, h), picked[a, t, h], one_less_x[:], ALU.mult)
+            x = picked[a, t][:, half(h)]
+            x_less_one = work_tile([P, HALF], F32, "x_less_one")
+            nc.scalar.activation(x_less_one[:], x, ACT.Copy, bias=-1.0)
+            nc.gpsimd.tensor_tensor(later_slope(a, t, h), x, x_less_one[:], ALU.mult)
 
         def hidden(a, t, halves=BOTH):
             for h in halves:
@@ -248,24 +259,30 @@ def tile_list_timeout_plan_gradients_kernel(
             nc.gpsimd.tensor_scalar(dst[:, t, :], raw[:], upper, lower, ALU.min, ALU.max)
 
         def turn_there(a, t, h):
-            squares = work_tile([P, HALF], F32, "squares")
-            nc.scalar.activation(squares[:], picked[a, t, h], ACT.Square)
             there[a, t, h] = bank([P, HALF], "there")
             for b in range(BLOCKS):
                 block = slice(P * b, P * (b + 1))
-                dst = there[a, t, h][:, block]
-                nc.tensor.matmul(dst, squares[:, block], weights["ident"][:], start=True, stop=False, is_transpose=True)
-                nc.tensor.matmul(dst, picked[a, t, h][:, block], weights["ident"][:], start=False, stop=True, is_transpose=True)
+                nc.tensor.transpose(there[a, t, h][:, block], picked[a, t][:, half(h)][:, block], weights["ident"][:])
 
         def fetch(a, t, h):
-            turned[a, t, h] = work_tile([P, HALF], F32, "turned")
-            nc.scalar.copy(turned[a, t, h][:], there[a, t, h][:])
+            turned[a, t, h] = work_tile([P, 2, HALF], F32, "turned")
+            nc.scalar.activation(turned[a, t, h][:, 0, :], there[a, t, h][:], ACT.Square)
+            nc.scalar.activation(turned[a, t, h][:, 1, :], there[a, t, h][:], ACT.Copy, scale=-1.0)
 
-        def turn_back(a, h):
+        def turn_back(a, h, first, last):
             for b in range(BLOCKS):
-                back[a, h, b] = bank([P, PACK, P], "back")
-                for t in range(PACK):
-                    nc.tensor.transpose(back[a, h, b][:, t, :], turned[a, t, h][:, P * b : P * (b + 1)], weights["ident"][:])
+                if first == 0:
+                    back[a, h, b] = bank([P, PACK, P], "back")
+                for t in range(first, last + 1):
+                    for term in range(2):
+                        nc.tensor.matmul(
+                            back[a, h, b][:, t, :],
+                            turned[a, t, h][:, term, P * b : P * (b + 1)],
+                            weights["ident"][:],
+                            start=(term == 0),
+                            stop=(term == 1),
+                            is_transpose=True,
+                        )
 
         def interleaved_product(a, h, dst, factor, c):
             nc.vector.tensor_tensor(
@@ -388,68 +405,61 @@ def tile_list_timeout_plan_gradients_kernel(
         hidden(1, 2)
         clip(1, 1)
         hidden(1, 3)
-        load_saved(1, 0)
-        gather(1, 0, 0)
-        gather(1, 0, 1)
-        slope_shared(1, 0, 0)
         clip(1, 2)
         hidden(2, 0)
-        turn_there(1, 0, 1)
-        load_saved(1, 1)
-        gather(1, 1, 0)
-        gather(1, 1, 1)
-        slope_shared(1, 1, 0)
         clip(1, 3)
         hidden(2, 1)
-        turn_there(1, 1, 1)
-        load_saved(1, 2)
-        gather(1, 2, 0)
-        gather(1, 2, 1)
-        slope_shared(1, 2, 0)
-        fetch(1, 0, 1)
+        load_saved(1, 0)
+        gather(1, 0)
+        slope_shared(1, 0, 0)
+        turn_there(1, 0, 1)
         clip(2, 0)
         hidden(2, 2)
-        turn_there(1, 2, 1)
-        load_saved(1, 3)
-        gather(1, 3, 0)
-        gather(1, 3, 1)
-        slope_shared(1, 3, 0)
-        fetch(1, 1, 1)
+        load_saved(1, 1)
+        gather(1, 1)
+        slope_shared(1, 1, 0)
+        turn_there(1, 1, 1)
         clip(2, 1)
         hidden(2, 3)
+        load_saved(1, 2)
+        gather(1, 2)
+        slope_shared(1, 2, 0)
+        fetch(1, 0, 1)
+        turn_there(1, 2, 1)
+        clip(2, 2)
+        load_saved(1, 3)
+        gather(1, 3)
+        slope_shared(1, 3, 0)
+        fetch(1, 1, 1)
         turn_there(1, 3, 1)
+        clip(2, 3)
         load_saved(2, 0)
-        gather(2, 0, 0)
-        gather(2, 0, 1)
+        gather(2, 0)
         slope_shared(2, 0, 0)
         fetch(1, 2, 1)
-        clip(2, 2)
         turn_there(2, 0, 1)
         load_saved(2, 1)
-        gather(2, 1, 0)
-        gather(2, 1, 1)
+        gather(2, 1)
         slope_shared(2, 1, 0)
         fetch(1, 3, 1)
-        turn_back(1, 1)
-        clip(2, 3)
         turn_there(2, 1, 1)
+        turn_back(1, 1, 0, 3)
         load_saved(2, 2)
-        gather(2, 2, 0)
-        gather(2, 2, 1)
+        gather(2, 2)
         slope_shared(2, 2, 0)
         fetch(2, 0, 1)
         turn_there(2, 2, 1)
         load_saved(2, 3)
-        gather(2, 3, 0)
-        gather(2, 3, 1)
+        gather(2, 3)
         load_last()
         multiply(1, 1)
         slope_shared(2, 3, 0)
         fetch(2, 1, 1)
         turn_there(2, 3, 1)
         fetch(2, 2, 1)
+        turn_back(2, 1, 0, 2)
         fetch(2, 3, 1)
-        turn_back(2, 1)
+        turn_back(2, 1, 3, 3)
         multiply(1, 0)
         quantise_d(1, 1)
         multiply(2, 0)

@@ -35,14 +35,15 @@ QUAD = 32
 QUADS = P // QUAD
 QUAD_ROWS = 4
 TAB_ROW0 = P - QUAD_ROWS * QUADS * K_PASSES
-TURNED = ((MIDDLE, 1), (LAST, 1))
+TURNED = ((MIDDLE, 0), (LAST, 0))
 HEAD_PAGES = 2
 LOAD_BUFS = 5
-WORK_BUFS = 29
-SCALE_BUFS = GROUPS * HALVES + 2
+WORK_BUFS = 25
+SCALE_BUFS = GROUPS * HALVES + 1
 BANKS = 8
 SLOPE_BYTES = {(0, 0): "s00", (0, 1): "s01", (1, 0): "s00", (2, 0): "s01"}
 CLIPPED_BYTES = {0: "c0", 1: "c1", 2: "c0"}
+GATE = (LAST, 0)
 
 
 def tile_list_timeout_plan_gradients_kernel(
@@ -91,8 +92,8 @@ def tile_list_timeout_plan_gradients_kernel(
         slope = {}
         sums, there, turned, back = {}, {}, {}, {}
         clipped, unclipped = {}, {}
-        d_grouped, dq = {}, {}
-        weights, ys = {}, {}
+        d_grouped, dq, d_plain = {}, {}, {}
+        weights, ys, accs = {}, {}, {}
 
         def pick_scales():
             picked_sc = load_tile([P, S], U8, "picked_sc")
@@ -135,10 +136,10 @@ def tile_list_timeout_plan_gradients_kernel(
             weights["bounds"] = bounds
 
         def load_w2_scales():
-            weights["scales"] = scale_tile("w2_sc")
+            weights["scales"] = own_tile([P, N], U8, "w2_sc", "w2_sc")
             nc.vector.memset(weights["scales"][:].bitcast(I32), 0)
             for q in range(QUADS):
-                nc.sync.dma_start(
+                nc.gpsimd.dma_start(
                     weights["scales"][QUAD * q : QUAD * q + QUAD_ROWS * GROUPS, :].bitcast(I32),
                     w2_scales[:, QUAD_ROWS * q : QUAD_ROWS * (q + 1), :].bitcast(I32),
                 )
@@ -159,6 +160,8 @@ def tile_list_timeout_plan_gradients_kernel(
         def cast_w1(a, k):
             if (a, k) == (LAST, K_PASSES - 1):
                 w1_grouped[a, k] = own_tile([P, PASS * PACK], BF16, "w1_grouped", CLIPPED_BYTES[MIDDLE])
+            elif (a, k) == (FIRST, 0):
+                w1_grouped[a, k] = own_tile([P, PASS * PACK], BF16, "w1_grouped", "extra_page")
             else:
                 w1_grouped[a, k] = work_tile([P, PASS * PACK], BF16, "w1_grouped")
             nc.scalar.activation(
@@ -167,14 +170,17 @@ def tile_list_timeout_plan_gradients_kernel(
                 ACT.Copy,
             )
 
-        def quantise(a, k, grouped):
+        def quantise(a, k, pieces):
             codes = work_tile([P, PASS], U32, "codes")
             scales = scale_tile("scales")
-            nc.vector.quantize_mx(out=codes[:].bitcast(E4M3), scales=scales[:], in_=grouped[:])
+            width = PASS // len(pieces)
+            for i, grouped in enumerate(pieces):
+                cols = slice(width * i, width * (i + 1))
+                nc.vector.quantize_mx(out=codes[:, cols].bitcast(E4M3), scales=scales[:, cols], in_=grouped[:])
             return codes, scales
 
         def quantise_w1(a, k):
-            w1q[a, k] = quantise(a, k, w1_grouped[a, k])
+            w1q[a, k] = quantise(a, k, [w1_grouped[a, k]])
 
         def quantise_d(a, h):
             dq[a, h] = quantise(a, h, d_grouped[a, h])
@@ -202,14 +208,16 @@ def tile_list_timeout_plan_gradients_kernel(
             nc.scalar.activation(x_less_one[:], x, ACT.Copy, bias=-1.0)
             nc.gpsimd.tensor_tensor(x, x, x_less_one[:], ALU.mult)
 
-        def gather(a, t):
-            picked[a, t] = work_tile([P, S], F32, "picked")
-            if (a, t) == (LAST, END):
-                for h in BOTH:
-                    offsets = idx[:, LIST_COLS * h : LIST_COLS * (h + 1)]
-                    nc.vector.tensor_copy(picked[a, t][:, half(h)], s_rows[a, t][:].indirect(offsets))
-            else:
+        def gather(a, t, h=None):
+            if h is None:
+                picked[a, t] = work_tile([P, S], F32, "picked")
                 nc.vector.tensor_copy(picked[a, t][:], s_rows[a, t][:].indirect(idx[:]))
+                for h in BOTH:
+                    picked[a, t, h] = picked[a, t][:, half(h)]
+            else:
+                picked[a, t, h] = work_tile([P, HALF], F32, "picked")[:]
+                offsets = idx[:, LIST_COLS * h : LIST_COLS * (h + 1)]
+                nc.vector.tensor_copy(picked[a, t, h], s_rows[a, t][:].indirect(offsets))
 
         def later_slope(a, t, h):
             if (a, h) not in slope:
@@ -219,14 +227,21 @@ def tile_list_timeout_plan_gradients_kernel(
             return slope[a, h][:, t, :]
 
         def slope_vector(a, t, h):
-            x = picked[a, t][:, half(h)]
+            x = picked[a, t, h]
             nc.vector.scalar_tensor_tensor(later_slope(a, t, h), x, 1.0, x, ALU.subtract, ALU.mult)
 
         def slope_shared(a, t, h):
-            x = picked[a, t][:, half(h)]
-            x_less_one = work_tile([P, HALF], F32, "x_less_one")
-            nc.scalar.activation(x_less_one[:], x, ACT.Copy, bias=-1.0)
-            nc.gpsimd.tensor_tensor(later_slope(a, t, h), x, x_less_one[:], ALU.mult)
+            x = picked[a, t, h]
+            if (a, t) == (LAST, 2):
+                weights["late"] = own_tile([P, 4, HALF], F32, "late", "d_plain")
+                pairs = weights["late"][:, 2:4, :].rearrange("p r j -> p (r j)")
+                d_plain[LAST, 1] = pairs.bitcast(BF16).rearrange("p (t j) -> p t j", t=PACK)
+            if a == LAST and t >= 2:
+                x_less_one = weights["late"][:, t - 2, :]
+            else:
+                x_less_one = later_slope(a, t, h)
+            nc.scalar.activation(x_less_one, x, ACT.Copy, bias=-1.0)
+            nc.gpsimd.tensor_tensor(later_slope(a, t, h), x, x_less_one, ALU.mult)
 
         def hidden(a, t, halves=BOTH):
             for h in halves:
@@ -262,7 +277,7 @@ def tile_list_timeout_plan_gradients_kernel(
             there[a, t, h] = bank([P, HALF], "there")
             for b in range(BLOCKS):
                 block = slice(P * b, P * (b + 1))
-                nc.tensor.transpose(there[a, t, h][:, block], picked[a, t][:, half(h)][:, block], weights["ident"][:])
+                nc.tensor.transpose(there[a, t, h][:, block], picked[a, t, h][:, block], weights["ident"][:])
 
         def fetch(a, t, h):
             turned[a, t, h] = work_tile([P, 2, HALF], F32, "turned")
@@ -292,20 +307,57 @@ def tile_list_timeout_plan_gradients_kernel(
                 ALU.mult,
             )
 
-        def multiply(a, h):
-            if (a, h) == (LAST, 0) and LAST not in CLIPPED_BYTES:
-                grouped = own_tile([P, HALF * PACK], BF16, "d_grouped", CLIPPED_BYTES[LAST, 1])
+        def multiply(a, h, first=0, last=BLOCKS - 1):
+            width = PASS * (last + 1 - first)
+            if (a, h) == GATE:
+                grouped = own_tile([P, width], BF16, "d_grouped", "d_plain")
             else:
-                grouped = work_tile([P, HALF * PACK], BF16, "d_grouped")
-            d_grouped[a, h] = grouped
+                grouped = work_tile([P, width], BF16, "d_grouped")
+            d_grouped.setdefault((a, h), []).append(grouped)
             c = clipped[a, h]
             if (a, h) in TURNED:
-                for b in range(BLOCKS):
-                    interleaved_product(
-                        a, h, grouped[:, PASS * b : PASS * (b + 1)], back[a, h, b][:], c[:, :, P * b : P * (b + 1)]
-                    )
+                for b in range(first, last + 1):
+                    cols = slice(PASS * (b - first), PASS * (b - first + 1))
+                    interleaved_product(a, h, grouped[:, cols], back[a, h, b][:], c[:, :, P * b : P * (b + 1)])
             else:
                 interleaved_product(a, h, grouped[:], slope[a, h], c)
+
+        def shared_product(a, t):
+            if (a, 1) not in d_plain:
+                d_plain[a, 1] = work_tile([P, PACK, HALF], BF16, "d_plain")[:]
+            nc.gpsimd.tensor_tensor(d_plain[a, 1][:, t, :], slope[a, 1][:, t, :], clipped[a, 1][:, t, :], ALU.mult)
+
+        def interleave(a):
+            d_grouped[a, 1] = [work_tile([P, HALF * PACK], BF16, "d_grouped")]
+            nc.scalar.copy(
+                d_grouped[a, 1][0][:].rearrange("p (g i t) -> p g t i", i=PACK, t=PACK),
+                d_plain[a, 1].rearrange("p t (g i) -> p g t i", i=PACK),
+            )
+
+        def first_half_pass(n, a):
+            if a == 0:
+                accs[n] = bank([P, HALF], "y_sum")
+            codes, scales = dq[a, 0]
+            nc.tensor.matmul_mx(
+                out=accs[n][:],
+                lhsT=weights["codes"][:, a, P * n : P * (n + 1)].bitcast(E4M3),
+                lhsT_scale=weights["scales"][QUAD_ROWS * a : P, P * n : P * (n + 1)],
+                rhs=codes[:].bitcast(E4M3),
+                rhs_scale=scales[:],
+                start=(a == 0),
+                stop=(a == LAST),
+            )
+
+        def weigh(n):
+            ys[0, n] = work_tile([P, HALF], F32, "y")
+            nc.vector.scalar_tensor_tensor(ys[0, n][:], accs[n][:], -1.0, weights["wgo"][:, half(0)], ALU.mult, ALU.mult)
+
+        def put(n):
+            nc.vector.tensor_copy(pages[n][:].indirect(idx2[:, 0:LIST_COLS]), ys[0, n][:])
+
+        def extra_page():
+            pages.append(own_tile([P, T2], F32, "extra_page", "extra_page"))
+            nc.vector.memset(pages[-1][:].bitcast(I32), 0)
 
         def place(halves, n):
             width = HALF * len(halves)
@@ -343,6 +395,7 @@ def tile_list_timeout_plan_gradients_kernel(
 
         load_bounds()
         nc.sync.dma_start(idx2[:], offs2)
+        load_w2_scales()
         pick_scales()
         identity()
         pick_table(0)
@@ -354,6 +407,7 @@ def tile_list_timeout_plan_gradients_kernel(
         load_w1(0, 1)
         first_slopes(0, 0)
         quantise_w1(0, 0)
+        extra_page()
         cast_w1(0, 1)
         load_table(1)
         pick_half(1, 0)
@@ -391,7 +445,6 @@ def tile_list_timeout_plan_gradients_kernel(
         quantise_w1(1, 1)
         hidden(1, 0)
         hidden(1, 1)
-        load_w2_scales()
         load_w1(2, 0)
         cast_w1(2, 0)
         multiply(0, 1)
@@ -399,7 +452,6 @@ def tile_list_timeout_plan_gradients_kernel(
         load_w1(2, 1)
         cast_w1(2, 1)
         quantise_w1(2, 0)
-        quantise_d(0, 1)
         quantise_w1(2, 1)
         clip(1, 0)
         hidden(1, 2)
@@ -411,71 +463,104 @@ def tile_list_timeout_plan_gradients_kernel(
         hidden(2, 1)
         load_saved(1, 0)
         gather(1, 0)
-        slope_shared(1, 0, 0)
-        turn_there(1, 0, 1)
+        turn_there(1, 0, 0)
         clip(2, 0)
         hidden(2, 2)
+        slope_shared(1, 0, 1)
         load_saved(1, 1)
         gather(1, 1)
-        slope_shared(1, 1, 0)
-        turn_there(1, 1, 1)
+        turn_there(1, 1, 0)
+        fetch(1, 0, 0)
         clip(2, 1)
-        hidden(2, 3)
+        turn_back(1, 0, 0, 0)
+        slope_shared(1, 1, 1)
         load_saved(1, 2)
         gather(1, 2)
-        slope_shared(1, 2, 0)
-        fetch(1, 0, 1)
-        turn_there(1, 2, 1)
+        turn_there(1, 2, 0)
+        fetch(1, 1, 0)
+        turn_back(1, 0, 1, 1)
         clip(2, 2)
+        hidden(2, 3)
+        slope_shared(1, 2, 1)
         load_saved(1, 3)
         gather(1, 3)
-        slope_shared(1, 3, 0)
-        fetch(1, 1, 1)
-        turn_there(1, 3, 1)
+        turn_there(1, 3, 0)
+        fetch(1, 2, 0)
+        turn_back(1, 0, 2, 2)
         clip(2, 3)
+        slope_shared(1, 3, 1)
         load_saved(2, 0)
         gather(2, 0)
-        slope_shared(2, 0, 0)
-        fetch(1, 2, 1)
-        turn_there(2, 0, 1)
+        turn_there(2, 0, 0)
+        fetch(1, 3, 0)
+        turn_back(1, 0, 3, 3)
+        slope_shared(2, 0, 1)
+        shared_product(1, 0)
         load_saved(2, 1)
         gather(2, 1)
-        slope_shared(2, 1, 0)
-        fetch(1, 3, 1)
-        turn_there(2, 1, 1)
-        turn_back(1, 1, 0, 3)
+        multiply(1, 0, 0, 1)
+        turn_there(2, 1, 0)
+        fetch(2, 0, 0)
+        turn_back(2, 0, 0, 0)
+        slope_shared(2, 1, 1)
+        shared_product(1, 1)
         load_saved(2, 2)
-        gather(2, 2)
-        slope_shared(2, 2, 0)
-        fetch(2, 0, 1)
-        turn_there(2, 2, 1)
+        gather(2, 2, 0)
+        turn_there(2, 2, 0)
+        fetch(2, 1, 0)
+        turn_back(2, 0, 1, 1)
+        shared_product(1, 2)
         load_saved(2, 3)
-        gather(2, 3)
+        gather(2, 3, 0)
         load_last()
-        multiply(1, 1)
-        slope_shared(2, 3, 0)
-        fetch(2, 1, 1)
-        turn_there(2, 3, 1)
-        fetch(2, 2, 1)
-        turn_back(2, 1, 0, 2)
-        fetch(2, 3, 1)
-        turn_back(2, 1, 3, 3)
-        multiply(1, 0)
-        quantise_d(1, 1)
+        fetch(2, 2, 0)
+        turn_there(2, 3, 0)
+        turn_back(2, 0, 2, 2)
+        shared_product(1, 3)
+        gather(2, 2, 1)
+        fetch(2, 3, 0)
+        turn_back(2, 0, 3, 3)
+        gather(2, 3, 1)
+        multiply(1, 0, 2, 3)
+        first_half_pass(0, 0)
+        first_half_pass(1, 0)
+        first_half_pass(2, 0)
+        first_half_pass(3, 0)
         multiply(2, 0)
         quantise_d(1, 0)
+        first_half_pass(0, 1)
+        first_half_pass(1, 1)
         quantise_d(2, 0)
-        place((0,), 0)
-        multiply(2, 1)
+        first_half_pass(0, 2)
+        first_half_pass(1, 2)
+        first_half_pass(2, 1)
+        first_half_pass(3, 1)
+        first_half_pass(2, 2)
+        first_half_pass(3, 2)
+        quantise_d(0, 1)
+        slope_shared(2, 2, 1)
+        slope_shared(2, 3, 1)
+        shared_product(2, 0)
+        shared_product(2, 1)
+        shared_product(2, 2)
+        shared_product(2, 3)
+        weigh(0)
+        weigh(1)
+        interleave(1)
+        put(0)
+        weigh(2)
+        put(1)
+        put(2)
+        interleave(2)
+        quantise_d(1, 1)
         quantise_d(2, 1)
-        place((0,), 1)
-        scatter((0,), 0)
+        weigh(3)
+        put(3)
         place((1,), 0)
-        scatter((0,), 1)
-        place((1,), 1)
         scatter((1,), 0)
+        place((1,), 1)
         scatter((1,), 1)
-        place(BOTH, 2)
-        scatter(BOTH, 2)
-        place(BOTH, 3)
-        scatter(BOTH, 3)
+        place((1,), 2)
+        scatter((1,), 2)
+        place((1,), 3)
+        scatter((1,), 3)

@@ -38,11 +38,12 @@ TAB_ROW0 = P - QUAD_ROWS * QUADS * K_PASSES
 TURNED = ((MIDDLE, 0), (LAST, 0))
 HEAD_PAGES = 2
 LOAD_BUFS = 5
-WORK_BUFS = 25
+WORK_BUFS = 28
 SCALE_BUFS = GROUPS * HALVES + 1
 BANKS = 8
-SLOPE_BYTES = {(0, 0): "s00", (0, 1): "s01", (1, 0): "s00", (2, 0): "s01"}
+SLOPE_BYTES = {(0, 0): "s00", (0, 1): "s01", (1, 1): "s11", (2, 0): "s00", (1, 0): "s10", (2, 1): "s21"}
 CLIPPED_BYTES = {0: "c0", 1: "c1", 2: "c0"}
+PASS_ORDER = ((FIRST, MIDDLE, LAST), (FIRST, LAST, MIDDLE), (LAST, MIDDLE, FIRST))
 GATE = (LAST, 0)
 
 
@@ -160,8 +161,6 @@ def tile_list_timeout_plan_gradients_kernel(
         def cast_w1(a, k):
             if (a, k) == (LAST, K_PASSES - 1):
                 w1_grouped[a, k] = own_tile([P, PASS * PACK], BF16, "w1_grouped", CLIPPED_BYTES[MIDDLE])
-            elif (a, k) == (FIRST, 0):
-                w1_grouped[a, k] = own_tile([P, PASS * PACK], BF16, "w1_grouped", "extra_page")
             else:
                 w1_grouped[a, k] = work_tile([P, PASS * PACK], BF16, "w1_grouped")
             nc.scalar.activation(
@@ -232,14 +231,7 @@ def tile_list_timeout_plan_gradients_kernel(
 
         def slope_shared(a, t, h):
             x = picked[a, t, h]
-            if (a, t) == (LAST, 2):
-                weights["late"] = own_tile([P, 4, HALF], F32, "late", "d_plain")
-                pairs = weights["late"][:, 2:4, :].rearrange("p r j -> p (r j)")
-                d_plain[LAST, 1] = pairs.bitcast(BF16).rearrange("p (t j) -> p t j", t=PACK)
-            if a == LAST and t >= 2:
-                x_less_one = weights["late"][:, t - 2, :]
-            else:
-                x_less_one = later_slope(a, t, h)
+            x_less_one = later_slope(a, t, h)
             nc.scalar.activation(x_less_one, x, ACT.Copy, bias=-1.0)
             nc.gpsimd.tensor_tensor(later_slope(a, t, h), x, x_less_one, ALU.mult)
 
@@ -322,7 +314,34 @@ def tile_list_timeout_plan_gradients_kernel(
             else:
                 interleaved_product(a, h, grouped[:], slope[a, h], c)
 
+        def early_tile():
+            tile = own_tile([P, PACK + 1, S], F32, "early", CLIPPED_BYTES[MIDDLE])
+            clipped[MIDDLE] = tile[:, 0:PACK, :]
+            for h in BOTH:
+                clipped[MIDDLE, h] = clipped[MIDDLE][:, :, half(h)]
+            d_plain[FIRST, 1] = tile[:, PACK, :].bitcast(BF16).rearrange("p (t j) -> p t j", t=PACK)
+
+        def turn_slope(t):
+            both = bank([P, HALF], "slope_back")
+            for b in range(BLOCKS):
+                for term in range(2):
+                    nc.tensor.matmul(
+                        both[:, P * b : P * (b + 1)],
+                        turned[LAST, t, 1][:, term, P * b : P * (b + 1)],
+                        weights["ident"][:],
+                        start=(term == 0),
+                        stop=(term == 1),
+                        is_transpose=True,
+                    )
+            nc.scalar.copy(later_slope(LAST, t, 1), both[:])
+
+        def empty(a, t, h):
+            unclipped[a, t, h] = work_tile([P, HALF], F32, "unclipped")
+            nc.scalar.copy(unclipped[a, t, h][:], sums[a, t, h][:])
+
         def shared_product(a, t):
+            if (a, t) == (LAST, 0):
+                d_plain[a, 1] = own_tile([P, PACK, HALF], BF16, "d_plain", "d_plain")[:]
             if (a, 1) not in d_plain:
                 d_plain[a, 1] = work_tile([P, PACK, HALF], BF16, "d_plain")[:]
             nc.gpsimd.tensor_tensor(d_plain[a, 1][:, t, :], slope[a, 1][:, t, :], clipped[a, 1][:, t, :], ALU.mult)
@@ -335,7 +354,8 @@ def tile_list_timeout_plan_gradients_kernel(
             )
 
         def first_half_pass(n, a):
-            if a == 0:
+            groups = PASS_ORDER[min(n, 2)]
+            if a == groups[0]:
                 accs[n] = bank([P, HALF], "y_sum")
             codes, scales = dq[a, 0]
             nc.tensor.matmul_mx(
@@ -344,8 +364,8 @@ def tile_list_timeout_plan_gradients_kernel(
                 lhsT_scale=weights["scales"][QUAD_ROWS * a : P, P * n : P * (n + 1)],
                 rhs=codes[:].bitcast(E4M3),
                 rhs_scale=scales[:],
-                start=(a == 0),
-                stop=(a == LAST),
+                start=(a == groups[0]),
+                stop=(a == groups[-1]),
             )
 
         def weigh(n):
@@ -407,7 +427,6 @@ def tile_list_timeout_plan_gradients_kernel(
         load_w1(0, 1)
         first_slopes(0, 0)
         quantise_w1(0, 0)
-        extra_page()
         cast_w1(0, 1)
         load_table(1)
         pick_half(1, 0)
@@ -521,46 +540,45 @@ def tile_list_timeout_plan_gradients_kernel(
         fetch(2, 3, 0)
         turn_back(2, 0, 3, 3)
         gather(2, 3, 1)
+        turn_there(2, 2, 1)
+        turn_there(2, 3, 1)
         multiply(1, 0, 2, 3)
+        fetch(2, 2, 1)
         first_half_pass(0, 0)
         first_half_pass(1, 0)
-        first_half_pass(2, 0)
-        first_half_pass(3, 0)
+        turn_slope(2)
+        fetch(2, 3, 1)
         multiply(2, 0)
         quantise_d(1, 0)
         first_half_pass(0, 1)
-        first_half_pass(1, 1)
         quantise_d(2, 0)
         first_half_pass(0, 2)
         first_half_pass(1, 2)
-        first_half_pass(2, 1)
-        first_half_pass(3, 1)
+        first_half_pass(1, 1)
+        turn_slope(3)
         first_half_pass(2, 2)
-        first_half_pass(3, 2)
+        first_half_pass(2, 1)
+        first_half_pass(2, 0)
         quantise_d(0, 1)
-        slope_shared(2, 2, 1)
-        slope_shared(2, 3, 1)
         shared_product(2, 0)
         shared_product(2, 1)
         shared_product(2, 2)
         shared_product(2, 3)
         weigh(0)
         weigh(1)
-        interleave(1)
         put(0)
-        weigh(2)
+        interleave(1)
         put(1)
-        put(2)
         interleave(2)
         quantise_d(1, 1)
         quantise_d(2, 1)
-        weigh(3)
-        put(3)
+        weigh(2)
+        put(2)
         place((1,), 0)
         scatter((1,), 0)
         place((1,), 1)
         scatter((1,), 1)
         place((1,), 2)
         scatter((1,), 2)
-        place((1,), 3)
-        scatter((1,), 3)
+        place(BOTH, 3)
+        scatter(BOTH, 3)

@@ -111,6 +111,8 @@ def tile_list_timeout_plan_gradients_kernel(
             nc.sync.dma_start(words[:], tab_words[k].rearrange("p t i -> p (t i)").bitcast(I32))
             v_codes[k] = work_tile([P, S], U32, "v_codes")
             nc.vector.tensor_copy(v_codes[k][:], words[:].bitcast(U32).indirect(idx[:]))
+            for h in BOTH:
+                v_codes[k, h] = v_codes[k][:, half(h)]
 
         def identity():
             weights["ident"] = own_tile([P, P], F32, "ident", "ident")
@@ -121,10 +123,9 @@ def tile_list_timeout_plan_gradients_kernel(
             nc.sync.dma_start(weights["words", k][:], tab_words[k].rearrange("p t i -> p (t i)").bitcast(I32))
 
         def pick_half(k, h):
-            if h == 0:
-                v_codes[k] = work_tile([P, S], U32, "v_codes")
+            v_codes[k, h] = work_tile([P, HALF], U32, "v_codes")[:]
             offsets = idx[:, LIST_COLS * h : LIST_COLS * (h + 1)]
-            nc.vector.tensor_copy(v_codes[k][:, half(h)], weights["words", k][:].bitcast(U32).indirect(offsets))
+            nc.vector.tensor_copy(v_codes[k, h], weights["words", k][:].bitcast(U32).indirect(offsets))
 
         def late_page():
             pages.append(own_tile([P, T2], F32, "late_page", "late_page"))
@@ -244,7 +245,7 @@ def tile_list_timeout_plan_gradients_kernel(
                         out=sums[a, t, h][:],
                         lhsT=codes[:, P * t : P * (t + 1)].bitcast(E4M3),
                         lhsT_scale=scales[:, P * t : P * (t + 1)],
-                        rhs=v_codes[k][:, half(h)].bitcast(E5M2),
+                        rhs=v_codes[k, h].bitcast(E5M2),
                         rhs_scale=v_sc[:, k, half(h)],
                         start=(k == K_PASSES - 1),
                         stop=(k == 0),
@@ -276,20 +277,26 @@ def tile_list_timeout_plan_gradients_kernel(
             nc.scalar.activation(turned[a, t, h][:, 0, :], there[a, t, h][:], ACT.Square)
             nc.scalar.activation(turned[a, t, h][:, 1, :], there[a, t, h][:], ACT.Copy, scale=-1.0)
 
-        def turn_back(a, h, first, last):
-            for b in range(BLOCKS):
-                if first == 0:
+        def add_turned(a, h, b, t):
+            for term in (1, 0):
+                nc.tensor.matmul(
+                    back[a, h, b][:, t, :],
+                    turned[a, t, h][:, term, P * b : P * (b + 1)],
+                    weights["ident"][:],
+                    start=(term == 1),
+                    stop=(term == 0),
+                    is_transpose=True,
+                )
+
+        def turn_back(a, h, t, _):
+            for b in range(BLOCKS - 1):
+                if t == 0:
                     back[a, h, b] = bank([P, PACK, P], "back")
-                for t in range(first, last + 1):
-                    for term in range(2):
-                        nc.tensor.matmul(
-                            back[a, h, b][:, t, :],
-                            turned[a, t, h][:, term, P * b : P * (b + 1)],
-                            weights["ident"][:],
-                            start=(term == 0),
-                            stop=(term == 1),
-                            is_transpose=True,
-                        )
+                add_turned(a, h, b, t)
+            if t == END:
+                back[a, h, BLOCKS - 1] = bank([P, PACK, P], "back")
+                for late in reversed(range(PACK)):
+                    add_turned(a, h, BLOCKS - 1, late)
 
         def interleaved_product(a, h, dst, factor, c):
             nc.vector.tensor_tensor(
@@ -544,19 +551,19 @@ def tile_list_timeout_plan_gradients_kernel(
         turn_there(2, 3, 1)
         multiply(1, 0, 2, 3)
         fetch(2, 2, 1)
+        fetch(2, 3, 1)
         first_half_pass(0, 0)
         first_half_pass(1, 0)
-        turn_slope(2)
-        fetch(2, 3, 1)
         multiply(2, 0)
         quantise_d(1, 0)
         first_half_pass(0, 1)
         quantise_d(2, 0)
         first_half_pass(0, 2)
         first_half_pass(1, 2)
-        first_half_pass(1, 1)
-        turn_slope(3)
         first_half_pass(2, 2)
+        first_half_pass(1, 1)
+        turn_slope(2)
+        turn_slope(3)
         first_half_pass(2, 1)
         first_half_pass(2, 0)
         quantise_d(0, 1)

@@ -38,7 +38,7 @@ TAB_ROW0 = P - QUAD_ROWS * QUADS * K_PASSES
 TURNED = ((MIDDLE, 0), (LAST, 0))
 HEAD_PAGES = 2
 LOAD_BUFS = 5
-WORK_BUFS = 28
+WORK_BUFS = 27
 SCALE_BUFS = GROUPS * HALVES + 1
 BANKS = 8
 SLOPE_BYTES = {(0, 0): "s00", (0, 1): "s01", (1, 1): "s11", (2, 0): "s00", (1, 0): "s10", (2, 1): "s21"}
@@ -273,7 +273,10 @@ def tile_list_timeout_plan_gradients_kernel(
                 nc.tensor.transpose(there[a, t, h][:, block], picked[a, t, h][:, block], weights["ident"][:])
 
         def fetch(a, t, h):
-            turned[a, t, h] = work_tile([P, 2, HALF], F32, "turned")
+            if (a, t, h) == (LAST, END, 1):
+                turned[a, t, h] = own_tile([P, 2, HALF], F32, "turned", "last_turned")
+            else:
+                turned[a, t, h] = work_tile([P, 2, HALF], F32, "turned")
             nc.scalar.activation(turned[a, t, h][:, 0, :], there[a, t, h][:], ACT.Square)
             nc.scalar.activation(turned[a, t, h][:, 1, :], there[a, t, h][:], ACT.Copy, scale=-1.0)
 
@@ -354,10 +357,13 @@ def tile_list_timeout_plan_gradients_kernel(
             nc.gpsimd.tensor_tensor(d_plain[a, 1][:, t, :], slope[a, 1][:, t, :], clipped[a, 1][:, t, :], ALU.mult)
 
         def interleave(a):
-            d_grouped[a, 1] = [work_tile([P, HALF * PACK], BF16, "d_grouped")]
+            if a == MIDDLE:
+                d_grouped[a, 1] = [own_tile([P, HALF * PACK], BF16, "d_grouped", "last_turned")]
+            else:
+                d_grouped[a, 1] = [work_tile([P, HALF * PACK], BF16, "d_grouped")]
             nc.scalar.copy(
-                d_grouped[a, 1][0][:].rearrange("p (g i t) -> p g t i", i=PACK, t=PACK),
-                d_plain[a, 1].rearrange("p t (g i) -> p g t i", i=PACK),
+                d_grouped[a, 1][0][:].rearrange("p (j t) -> p j t", t=PACK),
+                d_plain[a, 1].rearrange("p t j -> p j t"),
             )
 
         def first_half_pass(n, a):

@@ -35,16 +35,15 @@ QUAD = 32
 QUADS = P // QUAD
 QUAD_ROWS = 4
 TAB_ROW0 = P - QUAD_ROWS * QUADS * K_PASSES
-TURNED = ((MIDDLE, 0), (LAST, 0))
 HEAD_PAGES = 2
 LOAD_BUFS = 5
 WORK_BUFS = 27
 SCALE_BUFS = GROUPS * HALVES + 1
 BANKS = 8
-SLOPE_BYTES = {(0, 0): "s00", (0, 1): "s01", (1, 1): "s11", (2, 0): "s00", (1, 0): "s10", (2, 1): "s21"}
-CLIPPED_BYTES = {0: "c0", 1: "c1", 2: "c0"}
-PASS_ORDER = ((FIRST, MIDDLE, LAST), (FIRST, LAST, MIDDLE), (LAST, MIDDLE, FIRST))
-GATE = (LAST, 0)
+CLIPPED_BYTES = {FIRST: "c_outer", MIDDLE: "c_middle", LAST: "c_outer"}
+IN_ORDER = (FIRST, MIDDLE, LAST)
+LAST_SECOND = (FIRST, LAST, MIDDLE)
+LAST_FIRST = (LAST, MIDDLE, FIRST)
 
 
 def tile_list_timeout_plan_gradients_kernel(
@@ -62,8 +61,8 @@ def tile_list_timeout_plan_gradients_kernel(
         def load_tile(shape, dtype, name):
             return ring.tile(shape, dtype, name=name, tag="loads", bufs=LOAD_BUFS, align_bytes=64)
 
-        def scale_tile(name):
-            return ring.tile([P, PASS], U8, name=name, tag="scales", bufs=SCALE_BUFS, align_bytes=64)
+        def scale_tile():
+            return ring.tile([P, PASS], U8, name="scales", tag="scales", bufs=SCALE_BUFS, align_bytes=64)
 
         def own_tile(shape, dtype, name, tag):
             return keep.tile(shape, dtype, name=name, tag=tag, align_bytes=64)
@@ -73,6 +72,9 @@ def tile_list_timeout_plan_gradients_kernel(
 
         def half(h):
             return slice(HALF * h, HALF * (h + 1))
+
+        def offsets(tile, halves):
+            return tile[:, LIST_COLS * halves[0] : LIST_COLS * (halves[-1] + 1)]
 
         idx = keep.tile([P, S // 16], U16, name="idx")
         nc.sync.dma_start(idx[:], offs)
@@ -85,72 +87,46 @@ def tile_list_timeout_plan_gradients_kernel(
         pages = [keep.tile([P, T2], F32, name=f"page{n}") for n in range(HEAD_PAGES)]
         for page in pages:
             nc.vector.memset(page[:].bitcast(I32), 0)
+        bounds = keep.tile([P, 2, PACK, PACK], F32, name="bounds")
+        for side, bound in enumerate((lo, hi)):
+            nc.sync.dma_start(bounds[:, side, 0:GROUPS, :], bound.rearrange("(a p t) -> p a t", p=P, t=PACK))
+        nc.sync.dma_start(idx2[:], offs2)
+        w2_sc = own_tile([P, N], U8, "w2_sc", "w2_sc")
+        nc.vector.memset(w2_sc[:].bitcast(I32), 0)
+        for q in range(QUADS):
+            nc.gpsimd.dma_start(
+                w2_sc[QUAD * q : QUAD * q + QUAD_ROWS * GROUPS, :].bitcast(I32),
+                w2_scales[:, QUAD_ROWS * q : QUAD_ROWS * (q + 1), :].bitcast(I32),
+            )
 
-        v_codes = {}
+        picked_sc = load_tile([P, S], U8, "picked_sc")
+        nc.vector.tensor_copy(picked_sc[:], tab_sc[:].indirect(idx[:]))
+        for q in range(QUADS):
+            row = TAB_ROW0 + QUAD_ROWS * K_PASSES * q
+            nc.scalar.dma_start(
+                v_sc[QUAD * q : QUAD * q + QUAD_ROWS, :, :].bitcast(I32),
+                picked_sc[row : row + QUAD_ROWS * K_PASSES, :].bitcast(I32),
+            )
+        ident = own_tile([P, P], F32, "ident", "ident")
+        make_identity(nc, ident[:])
+
+        words, v_codes = {}, {}
         w1_raw, w1_grouped, w1q = {}, {}, {}
-        s_rows = {}
-        picked = {}
-        slope = {}
+        s_rows, picked = {}, {}
+        slope, clipped = {}, {}
         sums, there, turned, back = {}, {}, {}, {}
-        clipped, unclipped = {}, {}
-        d_grouped, dq, d_plain = {}, {}, {}
-        weights, ys, accs = {}, {}, {}
+        d_plain, d_grouped, dq = {}, {}, {}
+        w2, accs, ys = {}, {}, {}
 
-        def pick_scales():
-            picked_sc = load_tile([P, S], U8, "picked_sc")
-            nc.vector.tensor_copy(picked_sc[:], tab_sc[:].indirect(idx[:]))
-            for q in range(QUADS):
-                first = TAB_ROW0 + QUAD_ROWS * K_PASSES * q
-                nc.scalar.dma_start(
-                    v_sc[QUAD * q : QUAD * q + QUAD_ROWS, :, :].bitcast(I32),
-                    picked_sc[first : first + QUAD_ROWS * K_PASSES, :].bitcast(I32),
-                )
+        def load_table(k, tile):
+            words[k] = tile
+            nc.sync.dma_start(tile[:], tab_words[k].rearrange("p t i -> p (t i)").bitcast(I32))
 
-        def pick_table(k):
-            words = own_tile([P, T], I32, "tab_words", "late_page")
-            nc.sync.dma_start(words[:], tab_words[k].rearrange("p t i -> p (t i)").bitcast(I32))
-            v_codes[k] = work_tile([P, S], U32, "v_codes")
-            nc.vector.tensor_copy(v_codes[k][:], words[:].bitcast(U32).indirect(idx[:]))
-            for h in BOTH:
-                v_codes[k, h] = v_codes[k][:, half(h)]
-
-        def identity():
-            weights["ident"] = own_tile([P, P], F32, "ident", "ident")
-            make_identity(nc, weights["ident"][:])
-
-        def load_table(k):
-            weights["words", k] = load_tile([P, T], I32, "tab_words")
-            nc.sync.dma_start(weights["words", k][:], tab_words[k].rearrange("p t i -> p (t i)").bitcast(I32))
-
-        def pick_half(k, h):
-            v_codes[k, h] = work_tile([P, HALF], U32, "v_codes")[:]
-            offsets = idx[:, LIST_COLS * h : LIST_COLS * (h + 1)]
-            nc.vector.tensor_copy(v_codes[k, h], weights["words", k][:].bitcast(U32).indirect(offsets))
-
-        def late_page():
-            pages.append(own_tile([P, T2], F32, "late_page", "late_page"))
-            nc.vector.memset(pages[-1][:].bitcast(I32), 0)
-
-        def load_bounds():
-            bounds = keep.tile([P, 2, PACK, PACK], F32, name="bounds")
-            for side, bound in enumerate((lo, hi)):
-                nc.sync.dma_start(bounds[:, side, 0:GROUPS, :], bound.rearrange("(a p t) -> p a t", p=P, t=PACK))
-            weights["bounds"] = bounds
-
-        def load_w2_scales():
-            weights["scales"] = own_tile([P, N], U8, "w2_sc", "w2_sc")
-            nc.vector.memset(weights["scales"][:].bitcast(I32), 0)
-            for q in range(QUADS):
-                nc.gpsimd.dma_start(
-                    weights["scales"][QUAD * q : QUAD * q + QUAD_ROWS * GROUPS, :].bitcast(I32),
-                    w2_scales[:, QUAD_ROWS * q : QUAD_ROWS * (q + 1), :].bitcast(I32),
-                )
-
-        def load_last():
-            weights["codes"] = load_tile([P, GROUPS, N], I32, "w2_codes")
-            weights["wgo"] = load_tile([P, S], F32, "wgo_t")
-            nc.sync.dma_start(weights["codes"][:], w2_words.rearrange("a p e i -> p a (e i)").bitcast(I32))
-            nc.sync.dma_start(weights["wgo"][:], wgo)
+        def pick_table(k, halves):
+            codes = work_tile([P, HALF * len(halves)], U32, "v_codes")
+            nc.vector.tensor_copy(codes[:], words[k][:].bitcast(U32).indirect(offsets(idx, halves)))
+            for i, h in enumerate(halves):
+                v_codes[k, h] = codes[:, half(i)]
 
         def load_w1(a, k):
             w1_raw[a, k] = load_tile([P, PACK, PASS], F32, "w1_raw")
@@ -170,71 +146,17 @@ def tile_list_timeout_plan_gradients_kernel(
                 ACT.Copy,
             )
 
-        def quantise(a, k, pieces):
-            codes = work_tile([P, PASS], U32, "codes")
-            scales = scale_tile("scales")
-            width = PASS // len(pieces)
-            for i, grouped in enumerate(pieces):
-                cols = slice(width * i, width * (i + 1))
-                nc.vector.quantize_mx(out=codes[:, cols].bitcast(E4M3), scales=scales[:, cols], in_=grouped[:])
-            return codes, scales
+        def new_operand():
+            return work_tile([P, PASS], U32, "codes"), scale_tile()
+
+        def quantise_piece(operand, values, i, pieces):
+            codes, scales = operand
+            cols = slice(PASS * i // pieces, PASS * (i + 1) // pieces)
+            nc.vector.quantize_mx(out=codes[:, cols].bitcast(E4M3), scales=scales[:, cols], in_=values)
 
         def quantise_w1(a, k):
-            w1q[a, k] = quantise(a, k, [w1_grouped[a, k]])
-
-        def quantise_d(a, h):
-            dq[a, h] = quantise(a, h, d_grouped[a, h])
-
-        def load_saved(a, t):
-            s_rows[a, t] = load_tile([P, T], F32, "s_rows")
-            nc.sync.dma_start(
-                s_rows[a, t][:], sT[PASS * a : PASS * (a + 1), :].rearrange("(p t) c -> p t c", t=PACK)[:, t, :]
-            )
-
-        def gather_first(t):
-            if t == 0:
-                slope[FIRST] = own_tile([P, PACK, S], F32, "slope_first", "slope")
-                for h in BOTH:
-                    slope[FIRST, h] = slope[FIRST][:, :, half(h)]
-            nc.vector.tensor_copy(slope[FIRST][:, t, :], s_rows[FIRST, t][:].indirect(idx[:]))
-
-        def first_slopes(first, last):
-            x = slope[FIRST][:, first : last + 1, :].rearrange("p t j -> p (t j)")
-            nc.vector.scalar_tensor_tensor(x, x, 1.0, x, ALU.subtract, ALU.mult)
-
-        def first_shared(t, h):
-            x = slope[FIRST, h][:, t, :]
-            x_less_one = work_tile([P, HALF], F32, "x_less_one")
-            nc.scalar.activation(x_less_one[:], x, ACT.Copy, bias=-1.0)
-            nc.gpsimd.tensor_tensor(x, x, x_less_one[:], ALU.mult)
-
-        def gather(a, t, h=None):
-            if h is None:
-                picked[a, t] = work_tile([P, S], F32, "picked")
-                nc.vector.tensor_copy(picked[a, t][:], s_rows[a, t][:].indirect(idx[:]))
-                for h in BOTH:
-                    picked[a, t, h] = picked[a, t][:, half(h)]
-            else:
-                picked[a, t, h] = work_tile([P, HALF], F32, "picked")[:]
-                offsets = idx[:, LIST_COLS * h : LIST_COLS * (h + 1)]
-                nc.vector.tensor_copy(picked[a, t, h], s_rows[a, t][:].indirect(offsets))
-
-        def later_slope(a, t, h):
-            if (a, h) not in slope:
-                both = own_tile([P, GROUPS - 1, PACK, HALF], F32, "slope_later", "slope")
-                for group in (MIDDLE, LAST):
-                    slope[group, h] = both[:, group - MIDDLE, :, :]
-            return slope[a, h][:, t, :]
-
-        def slope_vector(a, t, h):
-            x = picked[a, t, h]
-            nc.vector.scalar_tensor_tensor(later_slope(a, t, h), x, 1.0, x, ALU.subtract, ALU.mult)
-
-        def slope_shared(a, t, h):
-            x = picked[a, t, h]
-            x_less_one = later_slope(a, t, h)
-            nc.scalar.activation(x_less_one, x, ACT.Copy, bias=-1.0)
-            nc.gpsimd.tensor_tensor(later_slope(a, t, h), x, x_less_one, ALU.mult)
+            w1q[a, k] = new_operand()
+            quantise_piece(w1q[a, k], w1_grouped[a, k][:], 0, 1)
 
         def hidden(a, t, halves=BOTH):
             for h in halves:
@@ -252,27 +174,58 @@ def tile_list_timeout_plan_gradients_kernel(
                     )
 
         def clip(a, t, halves=BOTH):
-            if (a, halves[0]) not in clipped:
-                if a not in CLIPPED_BYTES:
-                    clipped[a, halves[0]] = own_tile([P, PACK, HALF], F32, "clipped", CLIPPED_BYTES[a, halves[0]])[:]
-                else:
-                    clipped[a] = own_tile([P, PACK, S], F32, "clipped", CLIPPED_BYTES[a])[:]
-                    for h in BOTH:
-                        clipped[a, h] = clipped[a][:, :, half(h)]
+            if a not in clipped:
+                clipped[a] = own_tile([P, PACK, S], F32, "clipped", CLIPPED_BYTES[a])
+                for h in BOTH:
+                    clipped[a, h] = clipped[a][:, :, half(h)]
             raw = work_tile([P, HALF * len(halves)], F32, "unclipped")
             for i, h in enumerate(halves):
                 nc.scalar.copy(raw[:, half(i)], sums[a, t, h][:])
-            dst = clipped[a] if halves == BOTH else clipped[a, halves[0]]
-            lower, upper = (weights["bounds"][:, side, a, t : t + 1] for side in range(2))
-            nc.gpsimd.tensor_scalar(dst[:, t, :], raw[:], upper, lower, ALU.min, ALU.max)
+            cols = slice(HALF * halves[0], HALF * (halves[-1] + 1))
+            lower, upper = (bounds[:, side, a, t : t + 1] for side in range(2))
+            nc.gpsimd.tensor_scalar(clipped[a][:, t, cols], raw[:], upper, lower, ALU.min, ALU.max)
 
-        def turn_there(a, t, h):
+        def load_saved(a, t):
+            s_rows[a, t] = load_tile([P, T], F32, "s_rows")
+            nc.sync.dma_start(
+                s_rows[a, t][:], sT[PASS * a : PASS * (a + 1), :].rearrange("(p t) c -> p t c", t=PACK)[:, t, :]
+            )
+
+        def gather_first(t, halves=BOTH):
+            if t == 0:
+                slope[FIRST] = own_tile([P, PACK, S], F32, "slope_first", "slope")
+                for h in BOTH:
+                    slope[FIRST, h] = slope[FIRST][:, :, half(h)]
+            cols = slice(HALF * halves[0], HALF * (halves[-1] + 1))
+            nc.vector.tensor_copy(slope[FIRST][:, t, cols], s_rows[FIRST, t][:].indirect(offsets(idx, halves)))
+
+        def slope_in_place(x):
+            nc.vector.scalar_tensor_tensor(x, x, 1.0, x, ALU.subtract, ALU.mult)
+
+        def gather(a, t, halves=BOTH):
+            x = work_tile([P, HALF * len(halves)], F32, "picked")
+            nc.vector.tensor_copy(x[:], s_rows[a, t][:].indirect(offsets(idx, halves)))
+            for i, h in enumerate(halves):
+                picked[a, t, h] = x[:, half(i)]
+
+        def second_slope(a, t):
+            if (a, 1) not in slope:
+                both = own_tile([P, GROUPS - 1, PACK, HALF], F32, "slope_later", "slope")
+                for group in (MIDDLE, LAST):
+                    slope[group, 1] = both[:, group - MIDDLE, :, :]
+            return slope[a, 1][:, t, :]
+
+        def shared_slope(a, t):
+            nc.scalar.activation(second_slope(a, t), picked[a, t, 1], ACT.Copy, bias=-1.0)
+            nc.gpsimd.tensor_tensor(second_slope(a, t), picked[a, t, 1], second_slope(a, t), ALU.mult)
+
+        def turn_there(a, t, h=0):
             there[a, t, h] = bank([P, HALF], "there")
             for b in range(BLOCKS):
                 block = slice(P * b, P * (b + 1))
-                nc.tensor.transpose(there[a, t, h][:, block], picked[a, t, h][:, block], weights["ident"][:])
+                nc.tensor.transpose(there[a, t, h][:, block], picked[a, t, h][:, block], ident[:])
 
-        def fetch(a, t, h):
+        def fetch(a, t, h=0):
             if (a, t, h) == (LAST, END, 1):
                 turned[a, t, h] = own_tile([P, 2, HALF], F32, "turned", "last_turned")
             else:
@@ -280,28 +233,35 @@ def tile_list_timeout_plan_gradients_kernel(
             nc.scalar.activation(turned[a, t, h][:, 0, :], there[a, t, h][:], ACT.Square)
             nc.scalar.activation(turned[a, t, h][:, 1, :], there[a, t, h][:], ACT.Copy, scale=-1.0)
 
-        def add_turned(a, h, b, t):
-            for term in (1, 0):
+        def add_turned(dst, terms, b, order):
+            for term in order:
                 nc.tensor.matmul(
-                    back[a, h, b][:, t, :],
-                    turned[a, t, h][:, term, P * b : P * (b + 1)],
-                    weights["ident"][:],
-                    start=(term == 1),
-                    stop=(term == 0),
+                    dst,
+                    terms[:, term, P * b : P * (b + 1)],
+                    ident[:],
+                    start=(term == order[0]),
+                    stop=(term == order[-1]),
                     is_transpose=True,
                 )
 
-        def turn_back(a, h, t, _):
+        def turn_back(a, t):
             for b in range(BLOCKS - 1):
                 if t == 0:
-                    back[a, h, b] = bank([P, PACK, P], "back")
-                add_turned(a, h, b, t)
+                    back[a, b] = bank([P, PACK, P], "back")
+                add_turned(back[a, b][:, t, :], turned[a, t, 0], b, (1, 0))
             if t == END:
-                back[a, h, BLOCKS - 1] = bank([P, PACK, P], "back")
+                b = BLOCKS - 1
+                back[a, b] = bank([P, PACK, P], "back")
                 for late in reversed(range(PACK)):
-                    add_turned(a, h, BLOCKS - 1, late)
+                    add_turned(back[a, b][:, late, :], turned[a, late, 0], b, (1, 0))
 
-        def interleaved_product(a, h, dst, factor, c):
+        def turned_slope(t):
+            total = bank([P, HALF], "slope_back")
+            for b in range(BLOCKS):
+                add_turned(total[:, P * b : P * (b + 1)], turned[LAST, t, 1], b, (0, 1))
+            nc.scalar.copy(second_slope(LAST, t), total[:])
+
+        def interleaved_product(dst, factor, c):
             nc.vector.tensor_tensor(
                 dst.rearrange("p (g i t) -> p g t i", i=PAIR, t=PACK),
                 factor.rearrange("p t (g i) -> p g t i", i=PAIR),
@@ -309,289 +269,222 @@ def tile_list_timeout_plan_gradients_kernel(
                 ALU.mult,
             )
 
-        def multiply(a, h, first=0, last=BLOCKS - 1):
-            width = PASS * (last + 1 - first)
-            if (a, h) == GATE:
-                grouped = own_tile([P, width], BF16, "d_grouped", "d_plain")
+        def multiply_first(h):
+            d_grouped[FIRST, h] = [work_tile([P, HALF * PACK], BF16, "d_grouped")]
+            interleaved_product(d_grouped[FIRST, h][0][:], slope[FIRST, h], clipped[FIRST, h])
+
+        def multiply_turned(a, blocks):
+            if a == LAST:
+                grouped = own_tile([P, PASS * len(blocks)], BF16, "d_grouped", "d_plain")
             else:
-                grouped = work_tile([P, width], BF16, "d_grouped")
-            d_grouped.setdefault((a, h), []).append(grouped)
-            c = clipped[a, h]
-            if (a, h) in TURNED:
-                for b in range(first, last + 1):
-                    cols = slice(PASS * (b - first), PASS * (b - first + 1))
-                    interleaved_product(a, h, grouped[:, cols], back[a, h, b][:], c[:, :, P * b : P * (b + 1)])
-            else:
-                interleaved_product(a, h, grouped[:], slope[a, h], c)
-
-        def early_tile():
-            tile = own_tile([P, PACK + 1, S], F32, "early", CLIPPED_BYTES[MIDDLE])
-            clipped[MIDDLE] = tile[:, 0:PACK, :]
-            for h in BOTH:
-                clipped[MIDDLE, h] = clipped[MIDDLE][:, :, half(h)]
-            d_plain[FIRST, 1] = tile[:, PACK, :].bitcast(BF16).rearrange("p (t j) -> p t j", t=PACK)
-
-        def turn_slope(t):
-            both = bank([P, HALF], "slope_back")
-            for b in range(BLOCKS):
-                for term in range(2):
-                    nc.tensor.matmul(
-                        both[:, P * b : P * (b + 1)],
-                        turned[LAST, t, 1][:, term, P * b : P * (b + 1)],
-                        weights["ident"][:],
-                        start=(term == 0),
-                        stop=(term == 1),
-                        is_transpose=True,
-                    )
-            nc.scalar.copy(later_slope(LAST, t, 1), both[:])
-
-        def empty(a, t, h):
-            unclipped[a, t, h] = work_tile([P, HALF], F32, "unclipped")
-            nc.scalar.copy(unclipped[a, t, h][:], sums[a, t, h][:])
+                grouped = work_tile([P, PASS * len(blocks)], BF16, "d_grouped")
+            d_grouped.setdefault((a, 0), []).append(grouped)
+            for i, b in enumerate(blocks):
+                c = clipped[a, 0][:, :, P * b : P * (b + 1)]
+                interleaved_product(grouped[:, PASS * i : PASS * (i + 1)], back[a, b][:], c)
 
         def shared_product(a, t):
-            if (a, t) == (LAST, 0):
-                d_plain[a, 1] = own_tile([P, PACK, HALF], BF16, "d_plain", "d_plain")[:]
-            if (a, 1) not in d_plain:
-                d_plain[a, 1] = work_tile([P, PACK, HALF], BF16, "d_plain")[:]
-            nc.gpsimd.tensor_tensor(d_plain[a, 1][:, t, :], slope[a, 1][:, t, :], clipped[a, 1][:, t, :], ALU.mult)
+            if t == 0 and a == LAST:
+                d_plain[a] = own_tile([P, PACK, HALF], BF16, "d_plain", "d_plain")
+            elif t == 0:
+                d_plain[a] = work_tile([P, PACK, HALF], BF16, "d_plain")
+            nc.gpsimd.tensor_tensor(d_plain[a][:, t, :], slope[a, 1][:, t, :], clipped[a, 1][:, t, :], ALU.mult)
 
         def interleave(a):
             if a == MIDDLE:
-                d_grouped[a, 1] = [own_tile([P, HALF * PACK], BF16, "d_grouped", "last_turned")]
+                grouped = own_tile([P, HALF * PACK], BF16, "d_grouped", "last_turned")
             else:
-                d_grouped[a, 1] = [work_tile([P, HALF * PACK], BF16, "d_grouped")]
-            nc.scalar.copy(
-                d_grouped[a, 1][0][:].rearrange("p (j t) -> p j t", t=PACK),
-                d_plain[a, 1].rearrange("p t j -> p j t"),
-            )
+                grouped = work_tile([P, HALF * PACK], BF16, "d_grouped")
+            d_grouped[a, 1] = [grouped]
+            nc.scalar.copy(grouped[:].rearrange("p (j t) -> p j t", t=PACK), d_plain[a][:].rearrange("p t j -> p j t"))
 
-        def first_half_pass(n, a):
-            groups = PASS_ORDER[min(n, 2)]
-            if a == groups[0]:
-                accs[n] = bank([P, HALF], "y_sum")
-            codes, scales = dq[a, 0]
+        def quantise_d(a, h):
+            dq[a, h] = new_operand()
+            for i, grouped in enumerate(d_grouped[a, h]):
+                quantise_piece(dq[a, h], grouped[:], i, len(d_grouped[a, h]))
+
+        def second_pass(acc, n, h, a, order):
+            codes, scales = dq[a, h]
             nc.tensor.matmul_mx(
-                out=accs[n][:],
-                lhsT=weights["codes"][:, a, P * n : P * (n + 1)].bitcast(E4M3),
-                lhsT_scale=weights["scales"][QUAD_ROWS * a : P, P * n : P * (n + 1)],
+                out=acc[:],
+                lhsT=w2["codes"][:, a, P * n : P * (n + 1)].bitcast(E4M3),
+                lhsT_scale=w2_sc[QUAD_ROWS * a : P, P * n : P * (n + 1)],
                 rhs=codes[:].bitcast(E4M3),
                 rhs_scale=scales[:],
-                start=(a == groups[0]),
-                stop=(a == groups[-1]),
+                start=(a == order[0]),
+                stop=(a == order[-1]),
             )
+
+        def early_pass(n, a):
+            order = (IN_ORDER, LAST_SECOND, LAST_FIRST)[n]
+            if a == order[0]:
+                accs[n] = bank([P, HALF], "y_sum")
+            second_pass(accs[n], n, 0, a, order)
 
         def weigh(n):
-            ys[0, n] = work_tile([P, HALF], F32, "y")
-            nc.vector.scalar_tensor_tensor(ys[0, n][:], accs[n][:], -1.0, weights["wgo"][:, half(0)], ALU.mult, ALU.mult)
+            ys[n] = work_tile([P, HALF], F32, "y")
+            nc.vector.scalar_tensor_tensor(ys[n][:], accs[n][:], -1.0, w2["wgo"][:, half(0)], ALU.mult, ALU.mult)
 
         def put(n):
-            nc.vector.tensor_copy(pages[n][:].indirect(idx2[:, 0:LIST_COLS]), ys[0, n][:])
+            nc.vector.tensor_copy(pages[n][:].indirect(offsets(idx2, (0,))), ys[n][:])
 
-        def extra_page():
-            pages.append(own_tile([P, T2], F32, "extra_page", "extra_page"))
-            nc.vector.memset(pages[-1][:].bitcast(I32), 0)
-
-        def place(halves, n):
-            width = HALF * len(halves)
-            y = work_tile([P, width], F32, "y")
+        def finish_page(n, halves):
+            y = work_tile([P, HALF * len(halves)], F32, "y")
+            order = IN_ORDER if n == 0 else LAST_FIRST
             for i, h in enumerate(halves):
                 acc = bank([P, HALF], "y_sum")
-                for a in range(GROUPS):
-                    codes, scales = dq[a, h]
-                    nc.tensor.matmul_mx(
-                        out=acc[:],
-                        lhsT=weights["codes"][:, a, P * n : P * (n + 1)].bitcast(E4M3),
-                        lhsT_scale=weights["scales"][QUAD_ROWS * a : P, P * n : P * (n + 1)],
-                        rhs=codes[:].bitcast(E4M3),
-                        rhs_scale=scales[:],
-                        start=(a == 0),
-                        stop=(a == LAST),
-                    )
+                for a in order:
+                    second_pass(acc, n, h, a, order)
                 nc.scalar.activation(y[:, half(i)], acc[:], ACT.Copy, scale=-1.0)
-            ys[halves, n] = y
-
-        def scatter(halves, n):
-            y, width = ys[halves, n], HALF * len(halves)
             page = pages[n % len(pages)]
-            first = halves[0]
-            nc.vector.tensor_tensor(
-                page[:].indirect(idx2[:, LIST_COLS * first : LIST_COLS * (first + len(halves))]),
-                y[:],
-                weights["wgo"][:, HALF * first : HALF * first + width],
-                ALU.mult,
-            )
-            if halves[-1] == HALVES - 1:
-                for side in range(2):
-                    cols = slice(side * T2 // 2, (side + 1) * T2 // 2)
-                    nc.sync.dma_start(out[P * n : P * (n + 1), cols], page[:, cols])
+            cols = slice(HALF * halves[0], HALF * (halves[-1] + 1))
+            nc.vector.tensor_tensor(page[:].indirect(offsets(idx2, halves)), y[:], w2["wgo"][:, cols], ALU.mult)
+            for side in range(2):
+                cols = slice(side * T2 // 2, (side + 1) * T2 // 2)
+                nc.sync.dma_start(out[P * n : P * (n + 1), cols], page[:, cols])
 
-        load_bounds()
-        nc.sync.dma_start(idx2[:], offs2)
-        load_w2_scales()
-        pick_scales()
-        identity()
-        pick_table(0)
-        load_saved(0, 0)
+        load_table(0, own_tile([P, T], I32, "tab_words", "late_page"))
+        pick_table(0, BOTH)
+        load_saved(FIRST, 0)
         gather_first(0)
-        late_page()
-        load_w1(0, 0)
-        cast_w1(0, 0)
-        load_w1(0, 1)
-        first_slopes(0, 0)
-        quantise_w1(0, 0)
-        cast_w1(0, 1)
-        load_table(1)
-        pick_half(1, 0)
-        quantise_w1(0, 1)
-        pick_half(1, 1)
-        load_saved(0, 1)
-        load_saved(0, 2)
-        hidden(0, 0, (0,))
-        hidden(0, 1, (0,))
-        hidden(0, 2, (0,))
-        hidden(0, 3, (0,))
+        pages.append(own_tile([P, T2], F32, "late_page", "late_page"))
+        nc.vector.memset(pages[-1][:].bitcast(I32), 0)
+        load_w1(FIRST, 0)
+        cast_w1(FIRST, 0)
+        load_w1(FIRST, 1)
+        slope_in_place(slope[FIRST][:, 0, :])
+        quantise_w1(FIRST, 0)
+        cast_w1(FIRST, 1)
+        load_table(1, load_tile([P, T], I32, "tab_words"))
+        pick_table(1, (0,))
+        quantise_w1(FIRST, 1)
+        pick_table(1, (1,))
+        load_saved(FIRST, 1)
+        load_saved(FIRST, 2)
+        for t in range(PACK):
+            hidden(FIRST, t, (0,))
         gather_first(1)
-        clip(0, 0, (0,))
-        clip(0, 1, (0,))
-        hidden(0, 0, (1,))
-        hidden(0, 1, (1,))
-        clip(0, 2, (0,))
-        clip(0, 3, (0,))
-        hidden(0, 2, (1,))
-        hidden(0, 3, (1,))
+        for pair in ((0, 1), (2, 3)):
+            for t in pair:
+                clip(FIRST, t, (0,))
+            for t in pair:
+                hidden(FIRST, t, (1,))
         gather_first(2)
-        clip(0, 0, (1,))
-        clip(0, 1, (1,))
-        clip(0, 2, (1,))
-        clip(0, 3, (1,))
-        load_saved(0, 3)
-        gather_first(3)
-        first_slopes(1, 3)
-        load_w1(1, 0)
-        cast_w1(1, 0)
-        load_w1(1, 1)
-        cast_w1(1, 1)
-        quantise_w1(1, 0)
-        multiply(0, 0)
-        quantise_w1(1, 1)
-        hidden(1, 0)
-        hidden(1, 1)
-        load_w1(2, 0)
-        cast_w1(2, 0)
-        multiply(0, 1)
-        quantise_d(0, 0)
-        load_w1(2, 1)
-        cast_w1(2, 1)
-        quantise_w1(2, 0)
-        quantise_w1(2, 1)
-        clip(1, 0)
-        hidden(1, 2)
-        clip(1, 1)
-        hidden(1, 3)
-        clip(1, 2)
-        hidden(2, 0)
-        clip(1, 3)
-        hidden(2, 1)
-        load_saved(1, 0)
-        gather(1, 0)
-        turn_there(1, 0, 0)
-        clip(2, 0)
-        hidden(2, 2)
-        slope_shared(1, 0, 1)
-        load_saved(1, 1)
-        gather(1, 1)
-        turn_there(1, 1, 0)
-        fetch(1, 0, 0)
-        clip(2, 1)
-        turn_back(1, 0, 0, 0)
-        slope_shared(1, 1, 1)
-        load_saved(1, 2)
-        gather(1, 2)
-        turn_there(1, 2, 0)
-        fetch(1, 1, 0)
-        turn_back(1, 0, 1, 1)
-        clip(2, 2)
-        hidden(2, 3)
-        slope_shared(1, 2, 1)
-        load_saved(1, 3)
-        gather(1, 3)
-        turn_there(1, 3, 0)
-        fetch(1, 2, 0)
-        turn_back(1, 0, 2, 2)
-        clip(2, 3)
-        slope_shared(1, 3, 1)
-        load_saved(2, 0)
-        gather(2, 0)
-        turn_there(2, 0, 0)
-        fetch(1, 3, 0)
-        turn_back(1, 0, 3, 3)
-        slope_shared(2, 0, 1)
-        shared_product(1, 0)
-        load_saved(2, 1)
-        gather(2, 1)
-        multiply(1, 0, 0, 1)
-        turn_there(2, 1, 0)
-        fetch(2, 0, 0)
-        turn_back(2, 0, 0, 0)
-        slope_shared(2, 1, 1)
-        shared_product(1, 1)
-        load_saved(2, 2)
-        gather(2, 2, 0)
-        turn_there(2, 2, 0)
-        fetch(2, 1, 0)
-        turn_back(2, 0, 1, 1)
-        shared_product(1, 2)
-        load_saved(2, 3)
-        gather(2, 3, 0)
-        load_last()
-        fetch(2, 2, 0)
-        turn_there(2, 3, 0)
-        turn_back(2, 0, 2, 2)
-        shared_product(1, 3)
-        gather(2, 2, 1)
-        fetch(2, 3, 0)
-        turn_back(2, 0, 3, 3)
-        gather(2, 3, 1)
-        turn_there(2, 2, 1)
-        turn_there(2, 3, 1)
-        multiply(1, 0, 2, 3)
-        fetch(2, 2, 1)
-        fetch(2, 3, 1)
-        first_half_pass(0, 0)
-        first_half_pass(1, 0)
-        multiply(2, 0)
-        quantise_d(1, 0)
-        first_half_pass(0, 1)
-        quantise_d(2, 0)
-        first_half_pass(0, 2)
-        first_half_pass(1, 2)
-        first_half_pass(2, 2)
-        first_half_pass(1, 1)
-        turn_slope(2)
-        turn_slope(3)
-        first_half_pass(2, 1)
-        first_half_pass(2, 0)
-        quantise_d(0, 1)
-        shared_product(2, 0)
-        shared_product(2, 1)
-        shared_product(2, 2)
-        shared_product(2, 3)
+        for t in range(PACK):
+            clip(FIRST, t, (1,))
+        load_saved(FIRST, END)
+        for h in BOTH:
+            gather_first(END, (h,))
+        for h in BOTH:
+            slope_in_place(slope[FIRST, h][:, 1:PACK, :])
+
+        for k in range(K_PASSES):
+            load_w1(MIDDLE, k)
+            cast_w1(MIDDLE, k)
+        quantise_w1(MIDDLE, 0)
+        multiply_first(0)
+        quantise_w1(MIDDLE, 1)
+        hidden(MIDDLE, 0)
+        hidden(MIDDLE, 1)
+        load_w1(LAST, 0)
+        cast_w1(LAST, 0)
+        multiply_first(1)
+        quantise_d(FIRST, 0)
+        load_w1(LAST, 1)
+        cast_w1(LAST, 1)
+        quantise_w1(LAST, 0)
+        quantise_w1(LAST, 1)
+        later = [(a, t) for a in (MIDDLE, LAST) for t in range(PACK)]
+        for i in range(PACK):
+            clip(*later[i])
+            hidden(*later[i + 2])
+
+        for t in range(PACK):
+            load_saved(MIDDLE, t)
+            gather(MIDDLE, t)
+            turn_there(MIDDLE, t)
+            if t > 0:
+                fetch(MIDDLE, t - 1)
+            if t > 1:
+                turn_back(MIDDLE, t - 1)
+            clip(LAST, t)
+            if t == 1:
+                turn_back(MIDDLE, 0)
+            if t in (0, 2):
+                hidden(LAST, 2 + t // 2)
+            shared_slope(MIDDLE, t)
+        load_saved(LAST, 0)
+        gather(LAST, 0)
+        turn_there(LAST, 0)
+        fetch(MIDDLE, END)
+        turn_back(MIDDLE, END)
+        shared_slope(LAST, 0)
+        shared_product(MIDDLE, 0)
+        load_saved(LAST, 1)
+        gather(LAST, 1)
+        turn_there(LAST, 1)
+        fetch(LAST, 0)
+        shared_slope(LAST, 1)
+        shared_product(MIDDLE, 1)
+
+        load_saved(LAST, 2)
+        gather(LAST, 2, (0,))
+        multiply_turned(MIDDLE, (0, 1))
+        fetch(LAST, 1)
+        turn_there(LAST, 2)
+        turn_back(LAST, 0)
+        turn_back(LAST, 1)
+        shared_product(MIDDLE, 2)
+        load_saved(LAST, END)
+        gather(LAST, END, (0,))
+        w2["codes"] = load_tile([P, GROUPS, N], I32, "w2_codes")
+        w2["wgo"] = load_tile([P, S], F32, "wgo_t")
+        nc.sync.dma_start(w2["codes"][:], w2_words.rearrange("a p e i -> p a (e i)").bitcast(I32))
+        nc.sync.dma_start(w2["wgo"][:], wgo)
+        fetch(LAST, 2)
+        turn_there(LAST, END)
+        turn_back(LAST, 2)
+        shared_product(MIDDLE, END)
+        gather(LAST, 2, (1,))
+        fetch(LAST, END)
+        turn_back(LAST, END)
+        gather(LAST, END, (1,))
+        turn_there(LAST, 2, 1)
+        turn_there(LAST, END, 1)
+        multiply_turned(MIDDLE, (2, 3))
+        fetch(LAST, 2, 1)
+        fetch(LAST, END, 1)
+
+        early_pass(0, FIRST)
+        early_pass(1, FIRST)
+        multiply_turned(LAST, range(BLOCKS))
+        quantise_d(MIDDLE, 0)
+        early_pass(0, MIDDLE)
+        quantise_d(LAST, 0)
+        for n in range(len(pages)):
+            early_pass(n, LAST)
+        early_pass(1, MIDDLE)
+        turned_slope(2)
+        turned_slope(END)
+        early_pass(2, MIDDLE)
+        early_pass(2, FIRST)
+        quantise_d(FIRST, 1)
+
+        for t in range(PACK):
+            shared_product(LAST, t)
         weigh(0)
         weigh(1)
         put(0)
-        interleave(1)
+        interleave(MIDDLE)
         put(1)
-        interleave(2)
-        quantise_d(1, 1)
-        quantise_d(2, 1)
+        interleave(LAST)
+        quantise_d(MIDDLE, 1)
+        dq[LAST, 1] = new_operand()
+        last_values = d_grouped[LAST, 1][0][:].rearrange("p (i c) -> p i c", i=2)
+        quantise_piece(dq[LAST, 1], last_values[:, 0, :], 0, 2)
         weigh(2)
+        quantise_piece(dq[LAST, 1], last_values[:, 1, :], 1, 2)
         put(2)
-        place((1,), 0)
-        scatter((1,), 0)
-        place((1,), 1)
-        scatter((1,), 1)
-        place((1,), 2)
-        scatter((1,), 2)
-        place(BOTH, 3)
-        scatter(BOTH, 3)
+        for n in range(len(pages)):
+            finish_page(n, (1,))
+        finish_page(PAGES - 1, BOTH)

from contextlib import ExitStack

import concourse.mybir as mybir
from concourse.masks import make_identity

K, H, N, T, S, T2 = 1024, 1536, 512, 2048, 1024, 2048
FLOPS = 2 * K * H * S + 2 * H * N * S

F32 = mybir.dt.float32
BF16 = mybir.dt.bfloat16
I32 = mybir.dt.int32
U32 = mybir.dt.uint32
U16 = mybir.dt.uint16
U8 = mybir.dt.uint8
E4M3 = mybir.dt.float8_e4m3fn_x4
E5M2 = mybir.dt.float8_e5m2_x4
ALU = mybir.AluOpType
ACT = mybir.ActivationFunctionType

P = 128
PACK = 4
PASS = P * PACK
HALF = 512
HALVES = S // HALF
BOTH = tuple(range(HALVES))
K_PASSES = K // PASS
GROUPS = H // PASS
FIRST, MIDDLE, LAST = range(GROUPS)
END = PACK - 1
LIST_COLS = HALF // 16
PAGES = N // P
BLOCKS = HALF // P
PAIR = 2
QUAD = 32
QUADS = P // QUAD
QUAD_ROWS = 4
TAB_ROW0 = P - QUAD_ROWS * QUADS * K_PASSES
HEAD_PAGES = 2
LOAD_BUFS = 5
WORK_BUFS = 27
SCALE_BUFS = GROUPS * HALVES + 1
BANKS = 8
CLIPPED_BYTES = {FIRST: "c_outer", MIDDLE: "c_middle", LAST: "c_outer"}
IN_ORDER = (FIRST, MIDDLE, LAST)
LAST_SECOND = (FIRST, LAST, MIDDLE)
LAST_FIRST = (LAST, MIDDLE, FIRST)


def tile_list_timeout_plan_gradients_kernel(
    tc, tab_words, tab_scales, w1, lo, hi, sT, w2_words, w2_scales, wgo, offs, offs2, out
):
    nc = tc.nc
    with ExitStack() as ctx:
        keep = ctx.enter_context(tc.tile_pool(name="keep", bufs=1))
        ring = ctx.enter_context(tc.tile_pool(name="ring", bufs=2))
        psum = ctx.enter_context(tc.psum_pool(name="psum", bufs=BANKS))

        def work_tile(shape, dtype, name):
            return ring.tile(shape, dtype, name=name, tag="work", bufs=WORK_BUFS, align_bytes=64)

        def load_tile(shape, dtype, name):
            return ring.tile(shape, dtype, name=name, tag="loads", bufs=LOAD_BUFS, align_bytes=64)

        def scale_tile():
            return ring.tile([P, PASS], U8, name="scales", tag="scales", bufs=SCALE_BUFS, align_bytes=64)

        def own_tile(shape, dtype, name, tag):
            return keep.tile(shape, dtype, name=name, tag=tag, align_bytes=64)

        def bank(shape, name):
            return psum.tile(shape, F32, name=name, tag="bank")

        def half(h):
            return slice(HALF * h, HALF * (h + 1))

        def offsets(tile, halves):
            return tile[:, LIST_COLS * halves[0] : LIST_COLS * (halves[-1] + 1)]

        idx = keep.tile([P, S // 16], U16, name="idx")
        nc.sync.dma_start(idx[:], offs)
        tab_sc = own_tile([P, T], U8, "tab_sc", "ident")
        nc.vector.memset(tab_sc[0:TAB_ROW0, :].bitcast(I32), 0)
        nc.sync.dma_start(tab_sc[TAB_ROW0:P, :].bitcast(I32), tab_scales.rearrange("a q t -> q a t").bitcast(I32))
        idx2 = keep.tile([P, S // 16], U16, name="idx2")
        v_sc = keep.tile([P, K_PASSES, S], U8, name="v_sc", align_bytes=64)
        nc.vector.memset(v_sc[:].rearrange("p k j -> p (k j)").bitcast(I32), 0)
        pages = [keep.tile([P, T2], F32, name=f"page{n}") for n in range(HEAD_PAGES)]
        for page in pages:
            nc.vector.memset(page[:].bitcast(I32), 0)
        bounds = keep.tile([P, 2, PACK, PACK], F32, name="bounds")
        for side, bound in enumerate((lo, hi)):
            nc.sync.dma_start(bounds[:, side, 0:GROUPS, :], bound.rearrange("(a p t) -> p a t", p=P, t=PACK))
        nc.sync.dma_start(idx2[:], offs2)
        w2_sc = own_tile([P, N], U8, "w2_sc", "w2_sc")
        nc.vector.memset(w2_sc[:].bitcast(I32), 0)
        for q in range(QUADS):
            nc.gpsimd.dma_start(
                w2_sc[QUAD * q : QUAD * q + QUAD_ROWS * GROUPS, :].bitcast(I32),
                w2_scales[:, QUAD_ROWS * q : QUAD_ROWS * (q + 1), :].bitcast(I32),
            )

        picked_sc = load_tile([P, S], U8, "picked_sc")
        nc.vector.tensor_copy(picked_sc[:], tab_sc[:].indirect(idx[:]))
        for q in range(QUADS):
            row = TAB_ROW0 + QUAD_ROWS * K_PASSES * q
            nc.scalar.dma_start(
                v_sc[QUAD * q : QUAD * q + QUAD_ROWS, :, :].bitcast(I32),
                picked_sc[row : row + QUAD_ROWS * K_PASSES, :].bitcast(I32),
            )
        ident = own_tile([P, P], F32, "ident", "ident")
        make_identity(nc, ident[:])

        words, v_codes = {}, {}
        w1_raw, w1_grouped, w1q = {}, {}, {}
        s_rows, picked = {}, {}
        slope, clipped = {}, {}
        sums, there, turned, back = {}, {}, {}, {}
        d_plain, d_grouped, dq = {}, {}, {}
        w2, accs, ys = {}, {}, {}

        def load_table(k, tile):
            words[k] = tile
            nc.sync.dma_start(tile[:], tab_words[k].rearrange("p t i -> p (t i)").bitcast(I32))

        def pick_table(k, halves):
            codes = work_tile([P, HALF * len(halves)], U32, "v_codes")
            nc.vector.tensor_copy(codes[:], words[k][:].bitcast(U32).indirect(offsets(idx, halves)))
            for i, h in enumerate(halves):
                v_codes[k, h] = codes[:, half(i)]

        def load_w1(a, k):
            w1_raw[a, k] = load_tile([P, PACK, PASS], F32, "w1_raw")
            nc.sync.dma_start(
                w1_raw[a, k][:],
                w1[PASS * k : PASS * (k + 1), PASS * a : PASS * (a + 1)].rearrange("(p j) c -> p j c", j=PACK),
            )

        def cast_w1(a, k):
            if (a, k) == (LAST, K_PASSES - 1):
                w1_grouped[a, k] = own_tile([P, PASS * PACK], BF16, "w1_grouped", CLIPPED_BYTES[MIDDLE])
            else:
                w1_grouped[a, k] = work_tile([P, PASS * PACK], BF16, "w1_grouped")
            nc.scalar.activation(
                w1_grouped[a, k][:].rearrange("p (t m j) -> p m j t", t=PACK, j=PACK),
                w1_raw[a, k][:].rearrange("p j (m t) -> p m j t", t=PACK),
                ACT.Copy,
            )

        def new_operand():
            return work_tile([P, PASS], U32, "codes"), scale_tile()

        def quantise_piece(operand, values, i, pieces):
            codes, scales = operand
            cols = slice(PASS * i // pieces, PASS * (i + 1) // pieces)
            nc.vector.quantize_mx(out=codes[:, cols].bitcast(E4M3), scales=scales[:, cols], in_=values)

        def quantise_w1(a, k):
            w1q[a, k] = new_operand()
            quantise_piece(w1q[a, k], w1_grouped[a, k][:], 0, 1)

        def hidden(a, t, halves=BOTH):
            for h in halves:
                sums[a, t, h] = bank([P, HALF], "h")
                for k in reversed(range(K_PASSES)):
                    codes, scales = w1q[a, k]
                    nc.tensor.matmul_mx(
                        out=sums[a, t, h][:],
                        lhsT=codes[:, P * t : P * (t + 1)].bitcast(E4M3),
                        lhsT_scale=scales[:, P * t : P * (t + 1)],
                        rhs=v_codes[k, h].bitcast(E5M2),
                        rhs_scale=v_sc[:, k, half(h)],
                        start=(k == K_PASSES - 1),
                        stop=(k == 0),
                    )

        def clip(a, t, halves=BOTH):
            if a not in clipped:
                clipped[a] = own_tile([P, PACK, S], F32, "clipped", CLIPPED_BYTES[a])
                for h in BOTH:
                    clipped[a, h] = clipped[a][:, :, half(h)]
            raw = work_tile([P, HALF * len(halves)], F32, "unclipped")
            for i, h in enumerate(halves):
                nc.scalar.copy(raw[:, half(i)], sums[a, t, h][:])
            cols = slice(HALF * halves[0], HALF * (halves[-1] + 1))
            lower, upper = (bounds[:, side, a, t : t + 1] for side in range(2))
            nc.gpsimd.tensor_scalar(clipped[a][:, t, cols], raw[:], upper, lower, ALU.min, ALU.max)

        def load_saved(a, t):
            s_rows[a, t] = load_tile([P, T], F32, "s_rows")
            nc.sync.dma_start(
                s_rows[a, t][:], sT[PASS * a : PASS * (a + 1), :].rearrange("(p t) c -> p t c", t=PACK)[:, t, :]
            )

        def gather_first(t, halves=BOTH):
            if t == 0:
                slope[FIRST] = own_tile([P, PACK, S], F32, "slope_first", "slope")
                for h in BOTH:
                    slope[FIRST, h] = slope[FIRST][:, :, half(h)]
            cols = slice(HALF * halves[0], HALF * (halves[-1] + 1))
            nc.vector.tensor_copy(slope[FIRST][:, t, cols], s_rows[FIRST, t][:].indirect(offsets(idx, halves)))

        def slope_in_place(x):
            nc.vector.scalar_tensor_tensor(x, x, 1.0, x, ALU.subtract, ALU.mult)

        def gather(a, t, halves=BOTH):
            x = work_tile([P, HALF * len(halves)], F32, "picked")
            nc.vector.tensor_copy(x[:], s_rows[a, t][:].indirect(offsets(idx, halves)))
            for i, h in enumerate(halves):
                picked[a, t, h] = x[:, half(i)]

        def second_slope(a, t):
            if (a, 1) not in slope:
                both = own_tile([P, GROUPS - 1, PACK, HALF], F32, "slope_later", "slope")
                for group in (MIDDLE, LAST):
                    slope[group, 1] = both[:, group - MIDDLE, :, :]
            return slope[a, 1][:, t, :]

        def shared_slope(a, t):
            nc.scalar.activation(second_slope(a, t), picked[a, t, 1], ACT.Copy, bias=-1.0)
            nc.gpsimd.tensor_tensor(second_slope(a, t), picked[a, t, 1], second_slope(a, t), ALU.mult)

        def turn_there(a, t, h=0):
            there[a, t, h] = bank([P, HALF], "there")
            for b in range(BLOCKS):
                block = slice(P * b, P * (b + 1))
                nc.tensor.transpose(there[a, t, h][:, block], picked[a, t, h][:, block], ident[:])

        def fetch(a, t, h=0):
            if (a, t, h) == (LAST, END, 1):
                turned[a, t, h] = own_tile([P, 2, HALF], F32, "turned", "last_turned")
            else:
                turned[a, t, h] = work_tile([P, 2, HALF], F32, "turned")
            nc.scalar.activation(turned[a, t, h][:, 0, :], there[a, t, h][:], ACT.Square)
            nc.scalar.activation(turned[a, t, h][:, 1, :], there[a, t, h][:], ACT.Copy, scale=-1.0)

        def add_turned(dst, terms, b, order):
            for term in order:
                nc.tensor.matmul(
                    dst,
                    terms[:, term, P * b : P * (b + 1)],
                    ident[:],
                    start=(term == order[0]),
                    stop=(term == order[-1]),
                    is_transpose=True,
                )

        def turn_back(a, t):
            for b in range(BLOCKS - 1):
                if t == 0:
                    back[a, b] = bank([P, PACK, P], "back")
                add_turned(back[a, b][:, t, :], turned[a, t, 0], b, (1, 0))
            if t == END:
                b = BLOCKS - 1
                back[a, b] = bank([P, PACK, P], "back")
                for late in reversed(range(PACK)):
                    add_turned(back[a, b][:, late, :], turned[a, late, 0], b, (1, 0))

        def turned_slope(t):
            total = bank([P, HALF], "slope_back")
            for b in range(BLOCKS):
                add_turned(total[:, P * b : P * (b + 1)], turned[LAST, t, 1], b, (0, 1))
            nc.scalar.copy(second_slope(LAST, t), total[:])

        def interleaved_product(dst, factor, c):
            nc.vector.tensor_tensor(
                dst.rearrange("p (g i t) -> p g t i", i=PAIR, t=PACK),
                factor.rearrange("p t (g i) -> p g t i", i=PAIR),
                c.rearrange("p t (g i) -> p g t i", i=PAIR),
                ALU.mult,
            )

        def multiply_first(h):
            d_grouped[FIRST, h] = [work_tile([P, HALF * PACK], BF16, "d_grouped")]
            interleaved_product(d_grouped[FIRST, h][0][:], slope[FIRST, h], clipped[FIRST, h])

        def multiply_turned(a, blocks):
            if a == LAST:
                grouped = own_tile([P, PASS * len(blocks)], BF16, "d_grouped", "d_plain")
            else:
                grouped = work_tile([P, PASS * len(blocks)], BF16, "d_grouped")
            d_grouped.setdefault((a, 0), []).append(grouped)
            for i, b in enumerate(blocks):
                c = clipped[a, 0][:, :, P * b : P * (b + 1)]
                interleaved_product(grouped[:, PASS * i : PASS * (i + 1)], back[a, b][:], c)

        def shared_product(a, t):
            if t == 0 and a == LAST:
                d_plain[a] = own_tile([P, PACK, HALF], BF16, "d_plain", "d_plain")
            elif t == 0:
                d_plain[a] = work_tile([P, PACK, HALF], BF16, "d_plain")
            nc.gpsimd.tensor_tensor(d_plain[a][:, t, :], slope[a, 1][:, t, :], clipped[a, 1][:, t, :], ALU.mult)

        def interleave(a):
            if a == MIDDLE:
                grouped = own_tile([P, HALF * PACK], BF16, "d_grouped", "last_turned")
            else:
                grouped = work_tile([P, HALF * PACK], BF16, "d_grouped")
            d_grouped[a, 1] = [grouped]
            nc.scalar.copy(grouped[:].rearrange("p (j t) -> p j t", t=PACK), d_plain[a][:].rearrange("p t j -> p j t"))

        def quantise_d(a, h):
            dq[a, h] = new_operand()
            for i, grouped in enumerate(d_grouped[a, h]):
                quantise_piece(dq[a, h], grouped[:], i, len(d_grouped[a, h]))

        def second_pass(acc, n, h, a, order):
            codes, scales = dq[a, h]
            nc.tensor.matmul_mx(
                out=acc[:],
                lhsT=w2["codes"][:, a, P * n : P * (n + 1)].bitcast(E4M3),
                lhsT_scale=w2_sc[QUAD_ROWS * a : P, P * n : P * (n + 1)],
                rhs=codes[:].bitcast(E4M3),
                rhs_scale=scales[:],
                start=(a == order[0]),
                stop=(a == order[-1]),
            )

        def early_pass(n, a):
            order = (IN_ORDER, LAST_SECOND, LAST_FIRST)[n]
            if a == order[0]:
                accs[n] = bank([P, HALF], "y_sum")
            second_pass(accs[n], n, 0, a, order)

        def weigh(n):
            ys[n] = work_tile([P, HALF], F32, "y")
            nc.vector.scalar_tensor_tensor(ys[n][:], accs[n][:], -1.0, w2["wgo"][:, half(0)], ALU.mult, ALU.mult)

        def put(n):
            nc.vector.tensor_copy(pages[n][:].indirect(offsets(idx2, (0,))), ys[n][:])

        def finish_page(n, halves):
            y = work_tile([P, HALF * len(halves)], F32, "y")
            order = IN_ORDER if n == 0 else LAST_FIRST
            for i, h in enumerate(halves):
                acc = bank([P, HALF], "y_sum")
                for a in order:
                    second_pass(acc, n, h, a, order)
                nc.scalar.activation(y[:, half(i)], acc[:], ACT.Copy, scale=-1.0)
            page = pages[n % len(pages)]
            cols = slice(HALF * halves[0], HALF * (halves[-1] + 1))
            nc.vector.tensor_tensor(page[:].indirect(offsets(idx2, halves)), y[:], w2["wgo"][:, cols], ALU.mult)
            for side in range(2):
                cols = slice(side * T2 // 2, (side + 1) * T2 // 2)
                nc.sync.dma_start(out[P * n : P * (n + 1), cols], page[:, cols])

        load_table(0, own_tile([P, T], I32, "tab_words", "late_page"))
        pick_table(0, BOTH)
        load_saved(FIRST, 0)
        gather_first(0)
        pages.append(own_tile([P, T2], F32, "late_page", "late_page"))
        nc.vector.memset(pages[-1][:].bitcast(I32), 0)
        load_w1(FIRST, 0)
        cast_w1(FIRST, 0)
        load_w1(FIRST, 1)
        slope_in_place(slope[FIRST][:, 0, :])
        quantise_w1(FIRST, 0)
        cast_w1(FIRST, 1)
        load_table(1, load_tile([P, T], I32, "tab_words"))
        pick_table(1, (0,))
        quantise_w1(FIRST, 1)
        pick_table(1, (1,))
        load_saved(FIRST, 1)
        load_saved(FIRST, 2)
        for t in range(PACK):
            hidden(FIRST, t, (0,))
        gather_first(1)
        for pair in ((0, 1), (2, 3)):
            for t in pair:
                clip(FIRST, t, (0,))
            for t in pair:
                hidden(FIRST, t, (1,))
        gather_first(2)
        for t in range(PACK):
            clip(FIRST, t, (1,))
        load_saved(FIRST, END)
        for h in BOTH:
            gather_first(END, (h,))
        for h in BOTH:
            slope_in_place(slope[FIRST, h][:, 1:PACK, :])

        for k in range(K_PASSES):
            load_w1(MIDDLE, k)
            cast_w1(MIDDLE, k)
        quantise_w1(MIDDLE, 0)
        multiply_first(0)
        quantise_w1(MIDDLE, 1)
        hidden(MIDDLE, 0)
        hidden(MIDDLE, 1)
        load_w1(LAST, 0)
        cast_w1(LAST, 0)
        multiply_first(1)
        quantise_d(FIRST, 0)
        load_w1(LAST, 1)
        cast_w1(LAST, 1)
        quantise_w1(LAST, 0)
        quantise_w1(LAST, 1)
        later = [(a, t) for a in (MIDDLE, LAST) for t in range(PACK)]
        for i in range(PACK):
            clip(*later[i])
            hidden(*later[i + 2])

        for t in range(PACK):
            load_saved(MIDDLE, t)
            gather(MIDDLE, t)
            turn_there(MIDDLE, t)
            if t > 0:
                fetch(MIDDLE, t - 1)
            if t > 1:
                turn_back(MIDDLE, t - 1)
            clip(LAST, t)
            if t == 1:
                turn_back(MIDDLE, 0)
            if t in (0, 2):
                hidden(LAST, 2 + t // 2)
            shared_slope(MIDDLE, t)
        load_saved(LAST, 0)
        gather(LAST, 0)
        turn_there(LAST, 0)
        fetch(MIDDLE, END)
        turn_back(MIDDLE, END)
        shared_slope(LAST, 0)
        shared_product(MIDDLE, 0)
        load_saved(LAST, 1)
        gather(LAST, 1)
        turn_there(LAST, 1)
        fetch(LAST, 0)
        shared_slope(LAST, 1)
        shared_product(MIDDLE, 1)

        load_saved(LAST, 2)
        gather(LAST, 2, (0,))
        multiply_turned(MIDDLE, (0, 1))
        fetch(LAST, 1)
        turn_there(LAST, 2)
        turn_back(LAST, 0)
        turn_back(LAST, 1)
        shared_product(MIDDLE, 2)
        load_saved(LAST, END)
        gather(LAST, END, (0,))
        w2["codes"] = load_tile([P, GROUPS, N], I32, "w2_codes")
        w2["wgo"] = load_tile([P, S], F32, "wgo_t")
        nc.sync.dma_start(w2["codes"][:], w2_words.rearrange("a p e i -> p a (e i)").bitcast(I32))
        nc.sync.dma_start(w2["wgo"][:], wgo)
        fetch(LAST, 2)
        turn_there(LAST, END)
        turn_back(LAST, 2)
        shared_product(MIDDLE, END)
        gather(LAST, 2, (1,))
        fetch(LAST, END)
        turn_back(LAST, END)
        gather(LAST, END, (1,))
        turn_there(LAST, 2, 1)
        turn_there(LAST, END, 1)
        multiply_turned(MIDDLE, (2, 3))
        fetch(LAST, 2, 1)
        fetch(LAST, END, 1)

        early_pass(0, FIRST)
        early_pass(1, FIRST)
        multiply_turned(LAST, range(BLOCKS))
        quantise_d(MIDDLE, 0)
        early_pass(0, MIDDLE)
        quantise_d(LAST, 0)
        for n in range(len(pages)):
            early_pass(n, LAST)
        early_pass(1, MIDDLE)
        turned_slope(2)
        turned_slope(END)
        early_pass(2, MIDDLE)
        early_pass(2, FIRST)
        quantise_d(FIRST, 1)

        for t in range(PACK):
            shared_product(LAST, t)
        weigh(0)
        weigh(1)
        put(0)
        interleave(MIDDLE)
        put(1)
        interleave(LAST)
        quantise_d(MIDDLE, 1)
        dq[LAST, 1] = new_operand()
        last_values = d_grouped[LAST, 1][0][:].rearrange("p (i c) -> p i c", i=2)
        quantise_piece(dq[LAST, 1], last_values[:, 0, :], 0, 2)
        weigh(2)
        quantise_piece(dq[LAST, 1], last_values[:, 1, :], 1, 2)
        put(2)
        for n in range(len(pages)):
            finish_page(n, (1,))
        finish_page(PAGES - 1, BOTH)
